import numpy as np, ml_dtypes
CORES = [16,17,18,19,150,151]
N = 6
BF = ml_dtypes.bfloat16
def gentries(a):
    return np.ascontiguousarray(a.reshape(8, 16, -1).transpose(0, 2, 1)).reshape(8, -1)
def gtable(e):
    e = np.asarray(e); return np.ascontiguousarray(e.reshape(8, -1, 16).transpose(0, 2, 1)).reshape(128, -1).astype(np.int32)
V, G, CAP, D, P, RO = 768, 192, 64, 6, 1536, 6
W = V + (N - 1) * G
def paths(rng, n):
    s = (N, 8, 16, V)
    q = np.where(rng.random(s) < 0.6, np.arange(N).reshape(N, 1, 1, 1), rng.integers(0, N, s))
    u = np.where(rng.random(s) < 0.6, (np.arange(V) + rng.integers(-8, 9, s)) % V, rng.integers(0, V, s))
    a = q * V + u + 1; a[:, :, 0] = (np.arange(N * V) + 1).reshape(N, 1, V)
    return np.where(np.arange(16).reshape(16, 1) < n, a, 0)
def parts(rng):
    s = (N, 8, D, V)
    n = np.where(rng.random((N, 8, 1, V)) < rng.choice(np.array([0.1, 0.3, 0.6]), (N, 8, 1, 1)), 0, rng.integers(1, 17, (N, 8, 1, V)))
    return {"path": paths(rng, n), "toll": rng.integers(0, 256, (N, 128, W)),
            "nb": np.where(rng.random(s) < 0.5, (np.arange(V) + rng.integers(-8, 9, s)) % V, rng.integers(0, W, s)),
            "pr": rng.integers(0, 16, s) % rng.choice(np.array([2, 4, 16]), (N, 8, 1, 1)),
            "dn": np.where(rng.random(s) < 0.75, 15, rng.integers(0, RO + 1, s)),
            "org": rng.random((N, 8, V)) < rng.choice(np.array([0.01, 0.05]), (N, 8, 1)),
            "shown": np.ascontiguousarray(np.argsort(rng.random((N, 8, N - 1, V)), axis=-1)[..., :G]),
            "at": rng.integers(0, W, (N, 8, P))}
def pack(d):
    return {"path0": np.ascontiguousarray(d["path"].reshape(N, 128, V)).astype(np.int32), "toll": d["toll"].astype(np.float32).astype(BF),
            "nb": np.stack([gtable(a.reshape(8, -1)) for a in d["nb"]]), "lk": (16 * d["dn"] + d["pr"]).reshape(N, 8, D * V).astype(np.int32),
            "org": d["org"].astype(np.int32), "shown": np.stack([gtable(a.reshape(8, -1)) for a in d["shown"]]), "at0": np.stack([gtable(a) for a in d["at"]])}
def setup_inputs(rng):
    return pack(parts(rng))
def late(rng, d, p, q, g):
    odd = 2 * rng.permutation(V // 2) + 1; even = 2 * rng.permutation(V // 2); u = V // 16
    x, y1, y3, f0, f1 = odd[:u], odd[u:2 * u], odd[2 * u:3 * u], odd[3 * u:3 * u + 16], odd[3 * u + 16:3 * u + 32]
    z0, z2 = even[:u], even[u:2 * u]
    quiet = np.concatenate([even[2 * u:3 * u], odd[3 * u + 32:4 * u + 32]]); rd = np.concatenate([even[3 * u:], odd[4 * u + 32:]])
    for k in (y1, y3, f1, z2, quiet): p[:, k] = 0
    p[8:, f0] = 0; p[1:, f0[:8]] = 0
    o = d["org"][q, g]; o[:] = False; o[f0] = True; o[f1] = True
    nb = d["nb"][q, g]; dn = d["dn"][q, g]
    for k, f, m in ((x, f0, (2, 15)), (y1, f0, (3, 15)), (y3, f1, (4, 15)), (z0, f0[:8], (15, 15)), (z2, f1, (3, 15)), (quiet, f0, (0, 0))):
        nb[:, k] = rng.choice(f, len(k)); dn[:, k] = rng.choice(np.array(m), len(k))
    nb[:, rd] = np.where(rng.random((D, len(rd))) < 0.75, rng.integers(V, W, (D, len(rd))), nb[:, rd])
    for e in range(N - 1):
        sc = (q + e + g // 2) % 4; m = CAP - 1 + (q + e) % 3; n = rng.integers(0, 4, 5)
        if sc == 0: n[0] = rng.integers(8, 20); n[1] = rng.integers(3, 7); n[2] = 0; n[3] = rng.integers(0, 2)
        if sc == 1: n[2] = m - n[1]
        if sc == 2: n[3] = m
        if sc == 3: n[1:3] = 0; n[4] = m
        a = np.concatenate([rng.choice(k, int(i)) for k, i in zip((z0, x, y1, z2, y3), n)])
        if sc > 0: a = rng.permutation(a)
        a = np.concatenate([rng.choice(quiet, G - len(a)), a])
        if sc > 0 and rng.random() < 0.5: a = rng.permutation(a)
        d["shown"][q, g, e] = a
def setup_inputs_room(rng):
    d = parts(rng); path = paths(rng, rng.integers(1, 17, (N, 8, 1, V))); odd = 2 * np.arange(V // 2) + 1; h = V // 4
    for q in range(N):
        for g in range(0, 8, 2):
            o = rng.permutation(odd); a, b = o[:h], o[h:]
            path[q, g][:, b] = 0
            for e in range(N - 1):
                n = int(rng.choice(np.array([0, 1, CAP - 1, CAP, CAP + 1, G])))
                if q < 2 and e == 0: n = ((CAP, CAP + 1, G, CAP - 1), (1, 0, CAP, CAP + 1))[q][g // 2]
                d["shown"][q, g, e] = rng.permutation(np.concatenate([rng.permutation(a)[:n], rng.permutation(b)[:G - n]]))
        for g in range(1, 8, 2): late(rng, d, path[q, g], q, g)
    d["path"] = path
    return pack(d)
def setup_inputs_ties(rng):
    d = parts(rng); s = (N, 8, D, V)
    path = paths(rng, rng.choice(np.array([1, 14, 15, 16]), (N, 8, 1, V)))
    d["pr"] = rng.choice(np.array([0, 7, 14]), (N, 8, 1, 1)) + rng.integers(0, 2, s) * rng.integers(0, 2, (N, 8, 1, 1))
    d["dn"] = rng.choice(np.array([0, 1, 2, RO - 1, RO, 15, 15, 15]), s)
    v = np.arange(1, V, 4); c = v + 2; j = np.arange(16).reshape(16, 1); z = len(v); x = np.arange(z); m = N * V // 2
    wt = np.array([1, 37, 101, 13, 89, 53, 127, 7, 71, 113, 29, 97, 61, 19, 109, 43])
    for q in range(N):
        for g in (1, 3, 5, 7):
            lo, hi = {1: (2, 15), 3: (2, 16), 5: (3, 15), 7: (8, 15)}[g]
            n = rng.integers(lo, hi, z); kd = rng.integers(0, 6, z); rim = 128 if g == 7 else 0
            if g == 3: n = np.where(kd == 5, 15, np.where(kd == 4, np.minimum(n, 14), n))
            a = 2 * rng.integers(rim, m - rim, (16, z)) + 1; a[0] = q * V + c + 1; a = np.where(j < n, a, 0)
            h = np.flatnonzero((kd == 4) & (x % 2 == 0))
            if g == 3: a[n[h] - 1, h] = N * V
            b = np.concatenate([a[:1], a[:15]])
            if g == 1:
                b = np.take_along_axis(a, np.clip(n - j, 0, 15), 0); b = np.where((j >= 1) & (j <= n), b, 0)
            elif g == 5:
                i = rng.integers(2, n); k = rng.integers(i + 1, n + 1)
                b[i, x] = a[k - 1, x]; b[k, x] = a[i - 1, x]
            elif g == 3:
                k = np.where(kd == 5, 15, rng.integers(1, n + 1))
                by = np.where(kd == 1, V * rng.integers(1, N, z), np.where(kd == 2, 2, np.where(kd == 3, 2 ** rng.integers(1, 13, z), 2 * rng.integers(1, m, z))))
                b[k, x] = np.where(kd == 4, b[k, x], (b[k, x] - 1 + by) % (N * V) + 1)
                b[n[h], h] = 0
                h = np.flatnonzero((kd == 4) & (x % 2 == 1)); b[n[h] + 1, h] = N * V
                h = np.flatnonzero(kd == 5)[::3]; b[15, h] = 0
            else:
                kd = kd % 3; o = np.argsort(np.where((j >= 2) & (j <= n), rng.random((16, z)), 2.0), axis=0)[:4]
                by = np.where(kd == 0, np.array([[2], [2], [-2], [-2]]), 0); w2 = 2 ** rng.integers(1, 7, (2, z))
                by[0] = np.where(kd == 1, w2[0], np.where(kd == 2, 2 * wt[o[1]], by[0]))
                by[1] = np.where(kd == 1, -w2[1], np.where(kd == 2, -2 * wt[o[0]], by[1]))
                b[o, x] = b[o, x] + by
            b[0] = q * V + v + 1
            path[q, g][:, c] = a; path[q, g][:, v] = b
            d["nb"][q, g][:, v] = c; d["dn"][q, g][:, v] = 15; d["org"][q, g, v] = False
            for e in range(N - 1): d["shown"][q, g, e] = rng.permutation(v)[:G]
    d["path"] = path
    return pack(d)
def setup_inputs_loops(rng):
    d = parts(rng); nb = d["nb"]; snd = d["shown"]
    for g in range(8): nb[N - 1, g, :, V - 1] = 2 * rng.permutation(V // 2 - 1)[:D] + 1
    d["dn"][N - 1, :, :, V - 1] = 15; d["org"][N - 1, :, V - 1] = False
    n = np.where(rng.random((N, 8, 1, V)) < 0.8, 15, rng.integers(1, 16, (N, 8, 1, V))); path = paths(rng, n)
    for q in range(N):
        for g in range(8):
            for i in range(D):
                v = np.flatnonzero((nb[q, g, i] < V) & (rng.random(V) < 0.3)); u = nb[q, g, i][v]
                who = np.where(rng.random(len(v)) < 0.7, q, (q + 1) % N)
                path[q, g][(rng.random(len(v)) * n[q, g, 0, u]).astype(np.int64), u] = who * V + v + 1
                for e in range(N - 1):
                    b = (q + e + 1) % N; k = nb[b, g, i] - V - e * G
                    v = np.flatnonzero((k >= 0) & (k < G) & (rng.random(V) < 0.5)); u = snd[q, g, e][k[v]]
                    path[q, g][(rng.random(len(v)) * n[q, g, 0, u]).astype(np.int64), u] = b * V + v + 1
    for g in range(8):
        u = nb[N - 1, g, :, V - 1]; path[N - 1, g][(rng.random(D) * n[N - 1, g, 0, u]).astype(np.int64), u] = N * V
    d["path"] = path
    return pack(d)
def setup_inputs_ends(rng):
    d = parts(rng); nb = d["nb"]
    d["shown"][:, ::2] = rng.choice(np.array([0, V - 1, V // 2, 3]), (N, 4, N - 1, G)); d["at"][:, ::2] = rng.choice(np.array([0, V - 1, V, W - 1]), (N, 4, P))
    nb[:, 0] = nb[:, 0, :1]; nb[:, 2] = rng.integers(V, W, (N, D, V)); nb[:, 4] = rng.integers(0, V, (N, D, V))
    nb[:, 6] = rng.choice(np.array([0, V - 1, V, W - 1]), (N, D, V))
    d["path"][:, 3] = 0; d["org"][:, 3] = False
    d["path"][:, 1] = 0; d["org"][:, 1] = False; d["org"][0, 1, V - 1] = True
    d["org"][:, 5] = True; d["dn"][:, 7] = 0; d["toll"][:, :, ::3] = 255
    return pack(d)
def setup_inputs_spread(rng):
    d = parts(rng); s = (N, 8, D, V)
    n = np.minimum(np.exp2(4.2 * rng.random((N, 8, 1, V))).astype(np.int64) - 1, 16)
    a = np.minimum(np.exp2(13 * rng.random((N, 8, 16, V))).astype(np.int64), N * V)
    d["path"] = np.where(np.arange(16).reshape(16, 1) < n, a, 0)
    d["nb"] = rng.integers(0, W, s); d["pr"] = rng.integers(0, 16, s); d["dn"] = rng.integers(0, 16, s)
    d["org"] = rng.random((N, 8, V)) < np.exp2(-8 * rng.random((N, 8, 1))); d["shown"] = rng.integers(0, V, (N, 8, N - 1, G))
    d["toll"] = np.minimum((np.exp2(8 * rng.random((N, 1, W))) * rng.random((N, 128, W))).astype(np.int64), 255)
    d["at"] = np.minimum((W * rng.random((N, 8, P)) ** 3).astype(np.int64), W - 1)
    return pack(d)
def check_inputs(d):
    bad = []
    for k, hi in (("path0", N * V), ("nb", W - 1), ("lk", 255), ("org", 1), ("shown", V - 1), ("at0", W - 1)):
        if np.min(d[k]) < 0 or np.max(d[k]) > hi: bad.append("range of " + k)
    t = d["toll"].astype(np.float32)
    if not np.all((t >= 0) & (t <= 255) & (t == np.floor(t))): bad.append("toll: whole numbers from 0 to 255")
    p = d["path0"].reshape(-1, 16, V)
    if np.any((p[:, :15] == 0) & (p[:, 1:] != 0)): bad.append("filled rows of path0 come first")
    return bad
def reference(path0, toll, nb, lk, org, shown, at0):
    A = np.zeros((N, 8, 16, W), np.int32); A[..., :V] = path0.reshape(N, 8, 16, V)
    nbl = np.stack([gentries(a) for a in nb]).astype(np.int64).reshape(N, 8, D, V)
    sl = np.stack([gentries(a) for a in shown]).astype(np.int64).reshape(N, 8, N - 1, G)
    pos = [gentries(a).astype(np.int64) for a in at0]
    pr = (lk & 15).reshape(N, 8, D, V); dn = (lk >> 4).reshape(N, 8, D, V)
    fee = toll.astype(np.float32).astype(np.int32).reshape(N, 8, 16, W); S = np.zeros((N, 8, 16, P), np.int32)
    me = np.arange(V, dtype=np.int64); rest = np.broadcast_to(np.arange(V, W, dtype=np.int64), (8, W - V))
    for t in range(RO):
        for r in range(N):
            name = (r * V + me + 1).astype(np.int32)
            c = np.take_along_axis(A[r], nbl[r].reshape(8, 1, D * V), 2).reshape(8, 16, D, V)
            length = np.add.reduce((c > 0).astype(np.int32), axis=1)
            ok = (t < dn[r]) & (c[:, 0] > 0) & (c[:, 15] == 0) & ~np.any(c == name, axis=1)
            w = np.argmax(np.where(ok, 32 * pr[r] + 16 - length, -1), axis=1)
            some = np.any(ok, axis=1) & (org[r] == 0)
            best = np.take_along_axis(c, w[:, None, None, :], 2)[:, :, 0]
            new = np.zeros((8, 16, V), np.int32)
            new[:, 0] = np.where(some | (org[r] == 1), name, 0); new[:, 1:] = np.where(some[:, None], best[:, :15], 0)
            nh = np.where(some, np.take_along_axis(nbl[r], w[:, None], 1)[:, 0], me)
            A[r, :, :, (t & 1):V:2] = new[:, :, (t & 1)::2]
            pos[r] = np.take_along_axis(np.concatenate([nh, rest], axis=1), pos[r], 1)
            S[r] = (S[r] + np.take_along_axis(fee[r], pos[r][:, None], 2)) & 255
        for q in range(N):
            for d in range(1, N):
                b = (q + d) % N; lo = V + (d - 1) * G
                cur = np.take_along_axis(A[q], sl[q, :, d - 1][:, None], 2); old = A[b, :, :, lo:lo + G].copy()
                ch = np.any(cur != old, axis=1).astype(np.int64); before = np.add.accumulate(ch, axis=1) - ch
                A[b, :, :, lo:lo + G] = np.where(((ch == 1) & (before < CAP))[:, None], cur, old)
    return {"ypath": A[..., :V].reshape(N, 128, V).astype(np.float32), "ysum": S.reshape(N, 128, P).astype(np.float32).astype(BF)}

@@ -1,0 +1,618 @@
+import math
+import numpy as np
+from concourse.bass import DstId, RemoteDMATransfer
+from concourse.mybir import AluOpType as A, ActivationFunctionType as F
+
+NV, NG, RO, NR = 768, 192, 6, 6
+GH = 960
+TW = GH + 16 + NV + GH
+WIN = 16 + NV + GH
+CS = 0.0095
+CB = -CS * 2316
+C0 = math.exp(CB) * 1.001
+MAGIC = 12582912.0
+B23 = 8388608.0
+CHUNKS = ((0, 6), (6, 10), (10, 14), (14, 16))
+
+f32, bf, i32, u16, f16 = "float32", "bfloat16", "int32", "uint16", "float16"
+SB = {
+    "tab": (7 * TW, bf), "pin": (NV, i32), "pf": (NV, f32), "pe": (NV, f32),
+    "nbi": (288, i32), "nbh": (288, f16), "l1h": (320, f16), "l1t": (320, f16), "l2": (288, u16),
+    "lki": (352, i32), "lkb": (352, bf), "lkt": (352, bf), "lb": (288, bf), "li": (288, i32), "lj": (288, i32),
+    "a0": (288, bf), "dn": (6 * 288, bf), "orgv": (48, f32), "orgn": (48, bf), "bc": (144, bf),
+    "shi": (60, i32), "sh16": (60, u16), "shf": (60, f32), "ati": (96, i32), "at16": (96, u16),
+    "ki": (4, i32), "kf": (4, f32), "cols": (4, f32),
+    "fp": (144, f32), "fq": (160, f32), "fr": (160, f32), "iox": (144, f32), "fo": (128, f32),
+    "pm": (288, f16), "qm": (320, f16), "rm": (320, bf), "ib": (128, bf),
+    "beq": (144, bf), "bsg": (144, bf), "bx": (144, f32), "shm": (128, bf), "obn": (128, bf), "upm": (128, bf),
+    "nti": (NV, f32), "nte": (NV, f32), "ntc": (NV, bf), "nt": (4608, bf),
+    "nni": (NV, f32), "nne": (NV, f32), "mt": (NV, bf),
+    "v16": (48, f32), "oldp": (60, f32), "r6": (144, f32), "r12": (60, f32),
+    "eq": (4608, bf), "sg": (4608, bf), "sc": (288, f32), "si": (24, i32), "sj": (24, i32), "src": (24, u16),
+    "hi": (48, i32), "hj": (48, i32), "nh": (288, u16), "best": (384, bf), "neq": (GH, bf),
+    "ch": (60, bf), "ci": (60, bf), "m1": (60, f32), "m2": (60, f32), "sl": (60, u16),
+    "hh": (WIN, f32), "xx": (3 * WIN, f32), "sm": (2 * NV, f32), "smi": (NV, i32), "smj": (NV, i32),
+    "ee": (96, f32), "ei": (48, i32), "ej": (48, i32), "pl": (48, u16),
+    "tg": (GH, bf), "tgi": (GH, i32), "tgj": (GH, i32), "gt": (WIN, bf), "ys": (1536, bf),
+    "lo": (384, f32), "d1": (NV, f32), "d2": (NV, f32), "yp": (NV, f32),
+}
+PS = ["pfa", "pfb", "pnb", "pcn", "ppf", "pee", "ps1", "ps2"]
+SCRATCH = {k: ("sbuf", [128, v[0]], v[1]) for k, v in SB.items()}
+for _n in PS:
+    SCRATCH[_n] = ("psum", [128, 512], "float32")
+NDMA = 24
+SEMAPHORES = ["eV", "eS", "eP", "eG", "sent"] + ["arr%d" % t for t in range(RO - 1)] + ["dm%d" % k for k in range(NDMA)]
+
+
+def share(eng, ds):
+    out, at = {}, 0
+    for k, d in enumerate(ds):
+        left = len(ds) - k
+        n = 1 << int(math.log2((len(eng) - at + left - 1) // left))
+        while at + n + (left - 1) > len(eng):
+            n //= 2
+        out[d] = eng[at:at + n]
+        at += n
+    return out
+
+
+def calls_of(T, topo, src):
+    r = T.rank_of(src)
+    dst = {d: T.cores[(r + d) % NR] for d in range(1, NR)}
+    near = [d for d in dst if dst[d] in topo.cores_of(src)]
+    far = [d for d in dst if d not in near]
+    off = topo.engines(src, dst[far[0]])
+    on = [e for e in topo.engines(src, dst[near[0]]) if e not in off]
+    second = share(on, near[:2])
+    second.update(share(off, far[2:] + near[2:]))
+    return [share(off, far[:2]), second]
+
+
+def rank_program(g, core, T, topo):
+    r = T.rank_of(core)
+    if r is None:
+        return
+    Q = {"V": g.vector, "S": g.scalar, "P": g.tensor, "G": g, "Y": g.sync}
+    ops = []
+    wr = {k: np.full(v[0], -1) for k, v in SB.items()}
+    rd = {k: [] for k in SB}
+    bank = {k: {} for k in PS}
+    ndma = [0]
+
+    def R(n, a=0, b=None, s=1):
+        return (n, a, SB[n][0] if b is None else b, s)
+
+    def I(win, off):
+        return ("*", win, off)
+
+    def ap(x):
+        if not isinstance(x, tuple):
+            return x
+        if x[0] == "*":
+            return ap(x[1]).indirect(ap(x[2]))
+        return T[x[0]][:, x[1]:x[2]] if x[3] == 1 else T[x[0]][:, x[1]:x[2]:x[3]]
+
+    def add(e, fn, reads, writes, key=None, inc=1):
+        me = len(ops)
+        deps = set()
+        flat = []
+        for x in reads:
+            if isinstance(x, tuple):
+                flat += [x[1], x[2]] if x[0] == "*" else [x]
+        for x in flat + list(writes):
+            if x[0] in bank:
+                deps.update(k for q, k in bank[x[0]].items() if q != e)
+            else:
+                deps.update(int(k) for k in np.unique(wr[x[0]][x[1]:x[2]:x[3]]) if k >= 0)
+        for x in writes:
+            if x[0] not in bank:
+                m = np.zeros(SB[x[0]][0], bool)
+                m[x[1]:x[2]:x[3]] = True
+                deps.update(k for k, y in rd[x[0]] if m[y[1]:y[2]:y[3]].any())
+        for x in flat + list(writes):
+            if x[0] in bank:
+                bank[x[0]][e] = me
+        for x in flat:
+            if x[0] not in bank:
+                rd[x[0]].append((me, x))
+        for x in writes:
+            if x[0] not in bank:
+                wr[x[0]][x[1]:x[2]:x[3]] = me
+        ops.append({"e": e, "fn": fn, "deps": deps, "key": key, "inc": inc, "sig": False})
+
+    def ts(out, in0, s1, s2, o0, o1=None):
+        if o1 is None:
+            add("V", lambda: g.vector.tensor_scalar(ap(out), ap(in0), ap(s1), None, o0), [in0, s1], [out])
+        else:
+            add("V", lambda: g.vector.tensor_scalar(ap(out), ap(in0), ap(s1), ap(s2), o0, o1), [in0, s1, s2], [out])
+
+    def tt(out, in0, in1, op):
+        add("V", lambda: g.vector.tensor_tensor(ap(out), ap(in0), ap(in1), op), [in0, in1], [out])
+
+    def cp(out, in_):
+        add("V", lambda: g.vector.tensor_copy(ap(out), ap(in_)), [in_], [out])
+
+    def ms(out, c):
+        add("V", lambda: g.vector.memset(ap(out), c), [], [out])
+
+    def scan(out, d0, d1, init, o0, o1):
+        add("V", lambda: g.vector.tensor_tensor_scan(ap(out), ap(d0), ap(d1), init, o0, o1), [d0, d1], [out])
+
+    def vt(out, in_):
+        add("V", lambda: g.vector.transpose(ap(out), ap(in_)), [in_], [out])
+
+    def act(out, in_, fn=F.Copy, bias=0.0, scale=1.0):
+        add("S", lambda: g.scalar.activation(ap(out), ap(in_), fn, bias=bias, scale=scale), [in_], [out])
+
+    def mm(out, lhs, rhs, start, stop):
+        add("P", lambda: g.tensor.matmul(ap(out), ap(lhs), ap(rhs), start, stop), [lhs, rhs], [out])
+
+    def iota(out, pat, base, cm=0):
+        if SB[out[0]][1] == i32:
+            add("G", lambda: g.iota(ap(out), pat, base, cm), [], [out])
+        else:
+            add("G", lambda: g.iota(ap(out), pat, base, cm, allow_small_or_imprecise_dtypes=True), [], [out])
+
+    def sel(x, pat, op, fill, base):
+        add("G", lambda: g.affine_select(ap(x), ap(x), pat, op, fill, base, 1), [x], [x])
+
+    def dma(e, out, in_, accum=False):
+        key = "dm%d" % ndma[0]
+        ndma[0] += 1
+        reads = [in_] if isinstance(in_, tuple) else []
+        writes = [out] if isinstance(out, tuple) else []
+        if accum:
+            add(e, lambda: g.dma_start(ap(out), ap(in_), accum_op=A.add), reads + writes, writes, key, 16)
+        else:
+            add(e, lambda: Q[e].dma_start(ap(out), ap(in_)), reads, writes, key, 16)
+
+    def old(t, a=0, b=GH):
+        return R("tab", t * TW + a, t * TW + b)
+
+    def own(t, p):
+        return R("tab", t * TW + GH + 16 + p, t * TW + GH + 16 + NV, 2)
+
+    def ghost(t, a=0, b=GH):
+        return R("tab", t * TW + GH + 16 + NV + a, t * TW + GH + 16 + NV + b)
+
+    def H(n, p, w, u=None):
+        return R(n, w * p, w * p + (w if u is None else u))
+
+    K, KG, KL = R("kf", 0, 1), R("kf", 1, 2), R("kf", 2, 3)
+    O0 = GH + 16
+
+    def pads(a, b, mark):
+        if mark:
+            ts(R("tab", a * TW + GH + 2, (b - 1) * TW + GH + 3, TW), R("iox", 0, b - a), 0.0, R("cols", 0, 1), A.mult, A.add)
+        else:
+            for t in range(a, b):
+                ms(R("tab", t * TW + GH, t * TW + GH + 16), 0.0)
+
+    def list1(p, b):
+        for i in range(6):
+            for h in range(2):
+                x = 144 * p + 16 - 8 * h
+                mm(R(b, i, 144, 6), R("pm", x, x + 128), R("nbh", 48 * i + h, 48 * i + 48, 2), h == 0, h == 1)
+
+    def list2(p):
+        for b in range(9):
+            for c in range(2):
+                q = 160 * (b % 2) + 32 - 16 * c
+                x = 160 * p + 32 * (b // 2) + 16 * c
+                mm(R("ps2", 144 * p + b, 144 * p + 144, 9), R("qm", q, q + 128), R("l1t", x, x + 16), c == 0, c == 1)
+
+    def list3(p):
+        outs = [(R("ps1", 144 * p + e, 144 * p + 144, 9), 32 * e, 16) for e in range(9)]
+        outs += [(R("ps1", 288 + 24 * p, 304 + 24 * p), 288, 16), (R("ps1", 304 + 24 * p, 312 + 24 * p), 328, 8)]
+        for o, x, n in outs:
+            for c in range(2):
+                q = 160 * p + 32 - 16 * c
+                mm(o, R("rm", q, q + 128), R("lkt", x + 16 * c, x + 16 * c + n), c == 0, c == 1)
+
+    def prefs(p):
+        cp(H("li", p, 144), H("ps1", p, 144))
+        ts(H("lj", p, 144), H("li", p, 144), 15, None, A.bitwise_and)
+        ts(H("a0", p, 144), H("lj", p, 144), -16.0, -524288.0, A.add, A.mult)
+
+    def down(t, a=0, b=288):
+        act(R("dn", 288 * t + a, 288 * t + b), R("lb", a, b), F.Relu, B23 * 16 * (t + 1), -B23)
+
+    def statics(t, p, fb, first):
+        mm(R(fb, 0, 144), R("ib"), R("bc"), first, False)
+        for i in range(6):
+            x = 144 * p + 24 * i
+            mm(R(fb, i, 144, 6), R("ib"), R("a0", x, x + 24), False, False)
+            mm(R(fb, i, 144, 6), R("ib"), R("dn", 288 * t + x, 288 * t + x + 24), False, False)
+            mm(R(fb, i, 144, 6), R("ib"), H("orgn", p, 24), False, False)
+        mm(R(fb, 0, 144), R("qm", 32, 160), H("l1h", p, 160, 144), False, False)
+        mm(R(fb, 0, 144), R("qm", 176, 304), H("l1h", p, 160, 144), False, False)
+
+    def chunk(t, p, k, c, first=False):
+        a, b = CHUNKS[c]
+        fb = R(("pfa", "pfb")[k], 0, 144)
+        win = R("tab", t * TW + GH, (t + 1) * TW)
+        off = R("l2", 144 * p + 9 * a, 144 * p + 9 * b)
+        x, y = 2304 * k + 144 * a, 2304 * k + 144 * b
+        tt(R("eq", x, y), I(win, off), R("nt", 2304 * p + 144 * a, 2304 * p + 144 * b), A.is_equal)
+        act(R("sg", x, y), I(win, off), F.Sign)
+        for n, w in (("sg", "bsg"), ("eq", "beq")):
+            for m in range(a, b):
+                z = 2304 * k + 144 * m
+                mm(fb, R(w, 15 - m, 143 - m), R(n, z, z + 144), first and m == 0 and n == "sg", m == 15 and n == "eq")
+
+    def largest(k):
+        scan(H("sc", k, 144), R("r6"), R(("pfa", "pfb")[k], 0, 144), 0.0, A.mult, A.max)
+
+    def source(p, steps=(0, 1, 2)):
+        for s in steps:
+            if s == 0:
+                tt(R("si"), R("sc", 5, 144, 6), H("orgv", p, 24), A.max)
+            elif s == 1:
+                ts(R("sj"), R("si"), 2047, None, A.bitwise_and)
+            else:
+                cp(R("src"), R("sj"))
+
+    def nexthop(t, p, k, steps=(0, 1, 2)):
+        for s in steps:
+            if s == 0:
+                tt(H("hi", p, 24), R("sc", 144 * k + 5, 144 * k + 144, 6), H("v16", p, 24), A.max)
+            elif s == 1:
+                ts(H("hj", p, 24), H("hi", p, 24), 2047, None, A.bitwise_and)
+            else:
+                cp(H("nh", 2 * t + p, 24), H("hj", p, 24))
+
+    def winner(t):
+        act(R("best"), I(R("tab", t * TW + GH, (t + 1) * TW), R("src")))
+        mm(R("pnb", 0, 384), R("shm"), R("best"), True, True)
+
+    def hop(t, p, a=0, b=24, fn=act):
+        x = (t % 3) * WIN + 16 + p
+        fn(R("xx", x + 32 * a, x + 32 * b - 1, 2), I(R("hh"), R("nh", 48 * t + 24 * p + a, 48 * t + 24 * p + b)))
+
+    def sums(t, a=0, b=NV):
+        if t == 0:
+            return R("xx", 16 + a, 16 + b)
+        return R("smi", a, b) if t == RO - 1 else R("sm", (t % 2) * NV + a, (t % 2) * NV + b)
+
+    def follow(t, a, b):
+        tt(sums(t, a, b), I(H("xx", t % 3, WIN), R("pl", a // 16, b // 16)), sums(t - 1, a, b), A.add)
+
+    def to_list(t):
+        s = sums(t)
+        for m in range(16):
+            mm(R("pee", 0, 48), R("bx", 15 - m, 143 - m), R(s[0], s[1] + m, s[2], 16), m == 0, m == 15)
+
+    def places(t, steps=(0, 1, 2)):
+        for s in steps:
+            if s == 0:
+                if t == 0:
+                    cp(R("ei"), R("pee", 0, 48))
+                else:
+                    tt(R("ei"), R("pee", 0, 48), H("ee", (t - 1) % 2, 48), A.subtract)
+                if t < RO - 2:
+                    cp(H("ee", t % 2, 48), R("pee", 0, 48))
+            elif s == 1:
+                ts(R("ej"), R("ei"), 8, None, A.arith_shift_right)
+            else:
+                cp(R("pl"), R("ej"))
+
+    def decode(p, in_, steps=(0, 1)):
+        if 0 in steps:
+            act(H("d1", p, 384), in_, F.Ln, C0)
+        if 1 in steps:
+            act(H("d2", p, 384), H("d1", p, 384), F.Identity, MAGIC + 2316, 1.0 / CS)
+            act(R("yp", p, NV, 2), H("d2", p, 384), F.Identity, -MAGIC)
+
+    sent = [0]
+
+    def send(t, mk):
+        ds = sorted(mk)
+        win = R("tab", (t + 1) * TW, (t + 1) * TW + GH + 16 + NV)
+        parts = [(12 * (d - 1) + 6 * h, 12 * (d - 1) + 6 * h + 6) for d in ds for h in range(2)]
+        for fn, mine in ((cp, parts[:len(ds)]), (act, parts[len(ds):])):
+            runs = []
+            for a, b in mine:
+                if runs and runs[-1][1] == a:
+                    runs[-1][1] = b
+                else:
+                    runs.append([a, b])
+            for a, b in runs:
+                fn(old(t + 2, 16 * a, 16 * b), I(win, R("sl", a, b)))
+        trs = []
+        for d in ds:
+            rid, pid = topo.addr(T.cores[(r + d) % NR], core)
+            trs.append(RemoteDMATransfer(
+                dst_ids=[DstId(rid=rid, pnc=pid)], dma_engine_mask=sum(1 << e for e in mk[d]),
+                remote_sem=T.sem["arr%d" % t], src=ap(old(t + 2, NG * (d - 1), NG * d)),
+                dst=ap(ghost(t + 1, NG * (d - 1), NG * d))))
+            sent[0] += len(mk[d])
+        add("G", lambda: g.remote_dma_fused(trs, local_sem=T.sem.sent),
+            [old(t + 2, NG * (d - 1), NG * d) for d in ds], [], "remote", 0)
+
+    arrive = sum(len(mk[d]) for d in range(1, NR) for mk in calls_of(T, topo, T.cores[(r - d) % NR]) if d in mk)
+
+    dma("S", R("nbi"), T.nb[:])
+    dma("Y", R("pin", 0, 384), T.path0[:, 0:384])
+    dma("Y", R("pin", 384, NV), T.path0[:, 384:NV])
+    dma("Y", R("lki", 0, 288), T.lk[:])
+    dma("Y", R("lki", 288, 320), T.org[:, 0:512])
+    dma("Y", R("lki", 320, 352), T.org[:, 256:NV])
+    dma("Y", R("shi"), T.shown[:])
+    dma("Y", R("ati"), T.at0[:])
+    dma("Y", R("tg"), T.toll[:, NV:NV + GH])
+    iota(R("nti", 0, 48), [[2, 2], [32, 24]], r * NV + 1)
+    iota(R("ki", 0, 1), [[1, 1]], 0, 1)
+    iota(R("fp"), [[16, 9], [1000, 2], [2, 8]], -16)
+    iota(R("iox"), [[1, 144]], -15)
+    iota(R("fq"), [[32, 5], [1000, 2], [1, 16]], -32)
+    iota(R("fr"), [[32, 5], [1000, 2], [2, 16]], -32)
+    act(R("nte", 0, 48), R("nti", 0, 48), F.Exp, CB, CS)
+    ms(ghost(0), 0.0)
+    ts(R("nti", 48, 96), R("nti", 0, 48), 4.0, None, A.add)
+    ts(R("ki", 1, 2), R("ki", 0, 1), 112, None, A.bitwise_and)
+    ts(R("ki", 2, 3), R("ki", 0, 1), 15, None, A.bitwise_and)
+    ts(R("nti", 96, 192), R("nti", 0, 96), 8.0, None, A.add)
+    cp(R("kf", 0, 3), R("ki", 0, 3))
+    ts(R("nti", 192, 384), R("nti", 0, 192), 16.0, None, A.add)
+    act(R("nte", 48, 384), R("nti", 48, 384), F.Exp, CB, CS)
+    act(R("ntc", 0, 384), R("nte", 0, 384), F.Relu, -C0)
+    pads(0, 2, False)
+    for x in (R("l1h", 144, 160), R("l1h", 304, 320), R("shm")):
+        ms(x, 0.0)
+    ms(R("r6"), 1.0)
+    ts(R("cols", 0, 1), KL, 15.0, None, A.is_equal)
+    ts(R("cols", 1, 2), KL, 0.0, 1e29, A.not_equal, A.mult)
+    ms(R("r6", 0, 144, 6), 0.0)
+    for p in range(2):
+        ts(H("pm", p, 144), R("fp"), float(p), K, A.add, A.is_equal)
+    ts(R("bsg"), R("iox"), KG, -16384.0, A.is_equal, A.mult)
+    ts(R("beq"), R("iox"), KG, -B23, A.is_equal, A.mult)
+    pads(0, 2, True)
+    ts(R("ib"), R("iox", 15, 143), K, -1.0, A.is_equal, A.mult)
+    for b in range(2):
+        ts(H("qm", b, 160), R("fq"), 16.0 * b, K, A.add, A.is_equal)
+    for p in range(2):
+        ts(H("rm", p, 160), R("fr"), float(p), K, A.add, A.is_equal)
+    for i in range(3, 6):
+        act(R("nt", i, 2304, 6), R("ntc", 0, 384))
+    ts(R("nbh"), R("nbi"), 16.0, None, A.add)
+    list1(0, "ps1")
+    cp(R("pf", 0, 384), R("pin", 0, 384))
+    act(R("pe", 0, 384), R("pf", 0, 384), F.Exp, CB, CS)
+    cp(R("nt", 0, 2304, 6), R("ntc", 0, 384))
+    cp(R("l1h", 0, 144), R("ps1", 0, 144))
+    cp(R("pf", 384, NV), R("pin", 384, NV))
+    vt(R("l1t", 0, 160), R("l1h", 0, 160))
+    list2(0)
+    list1(1, "pfb")
+    act(R("tab", O0, O0 + 384), R("pe", 0, 384), F.Relu, -C0)
+    act(R("pe", 384, NV), R("pf", 384, NV), F.Exp, CB, CS)
+    act(R("tab", O0 + 384, O0 + NV), R("pe", 384, NV), F.Relu, -C0)
+    cp(R("lkb"), R("lki"))
+    vt(R("lkt"), R("lkb"))
+    for i in range(1, 3):
+        cp(R("nt", i, 2304, 6), R("ntc", 0, 384))
+    cp(R("l2", 0, 144), R("ps2", 0, 144))
+    list3(0)
+    list3(1)
+    sel(R("bsg", 15, 143, 16), [[-16, 8]], A.not_equal, B23, 0)
+    sel(R("bsg", 15, 143, 16), [[-16, 8]], A.not_equal, -B23, -15)
+    iota(R("bc"), [[0, 24], [2048, 6]], -127 * 2048)
+    iota(R("nni", 0, 384), [[2, 384]], r * NV + 1)
+    iota(R("fo"), [[16, 8], [0, 16]], 0)
+    sel(R("shm"), [[-1, 128]], A.not_equal, 1.0, 1)
+    sel(R("shm", 0, 128, 16), [[-16, 8]], A.not_equal, 0.0, 1)
+    sel(R("shm", 0, 128, 16), [[-16, 8]], A.not_equal, 2.0 ** 80, 0)
+    sel(R("shm", 0, 128, 16), [[-16, 8]], A.not_equal, 2.0 ** 80, -15)
+    iota(R("nti", 384, NV), [[2, 16], [32, 24]], r * NV + 2)
+    iota(R("v16"), [[1, 2], [32, 24]], 16, 2)
+    iota(R("oldp"), [[16, 60]], 0, 1)
+    iota(R("nni", 384, NV), [[2, 384]], r * NV + 2)
+
+    for t in range(RO - 1):
+        p = t & 1
+        for c in range(4):
+            chunk(t, p, 0, c, first=(t == 0))
+            if t == 0 and c == 0:
+                prefs(0)
+                act(R("lb", 0, 144), R("ps1", 0, 144))
+                act(R("orgn"), R("ps1", 288, 336), F.Copy, 0.0, 2 * B23)
+                down(0, 0, 144)
+                statics(0, 0, "pfa", False)
+        if t == 0:
+            act(R("orgv"), R("ps1", 288, 336), F.Copy, 0.0, B23 + 2.0)
+            act(R("nne", 0, 384), R("nni", 0, 384), F.Exp, CB, CS)
+            act(R("nte", 384, NV), R("nti", 384, NV), F.Exp, CB, CS)
+            cp(R("l1h", 160, 304), R("pfb", 0, 144))
+            ts(R("upm"), R("fo"), KG, 4096.0, A.is_equal, A.mult)
+            vt(R("l1t", 160, 320), R("l1h", 160, 320))
+            ts(R("sh16"), R("shi"), 16.0, None, A.add)
+            sel(R("upm"), [[-1, 128]], A.is_gt, 0.0, 0)
+            sel(R("upm"), [[-1, 128]], A.not_equal, 80.5 * 4096, 0)
+        if t >= 2:
+            places(t - 2)
+        largest(0)
+        source(p)
+        if t == 0:
+            list2(1)
+        winner(t)
+        act(own(t + 1, 1 - p), own(t, 1 - p))
+        if t < 2:
+            ts(H("mt", t, 384), H("nne", t, 384), C0, R("cols", 1, 2), A.subtract, A.max)
+        if t == 0:
+            ms(old(1), 0.0)
+        if t == 1:
+            ts(R("tgi", 0, 480), R("tg", 0, 480), 6.0, None, A.mult)
+        if t >= 2:
+            follow(t - 1, 0, 480)
+        tt(own(t + 1, p), R("pnb", 0, 384), H("mt", p, 384), A.min)
+        tt(R("neq"), I(R("tab", (t + 1) * TW + GH, (t + 1) * TW + GH + 16 + NV), R("sh16")), old(t + 1), A.not_equal)
+        if t > 0:
+            statics(t, 1 - p, "pfb", True)
+        for m in range(16):
+            mm(R("pcn", 0, 60), R("beq", 15 - m, 143 - m), R("neq", m, GH, 16), m == 0, m == 15)
+        if t == 0:
+            act(R("ntc", 384, NV), R("nte", 384, NV), F.Relu, -C0)
+            act(R("lb", 144, 288), R("ps1", 144, 288))
+            down(0, 144, 288)
+            down(1)
+            for i in range(4):
+                act(R("nt", 2304 + i, 4608, 6), R("ntc", 384, NV))
+            ms(R("r12"), 1000.0)
+            ts(R("obn"), R("fo"), KG, -4096.0, A.is_equal, A.mult)
+            cp(R("l2", 144, 288), R("ps2", 144, 288))
+            ms(R("r12", 0, 60, 12), 1.0)
+            ts(R("shf"), R("shi"), float(GH + 16), None, A.add)
+            ts(R("oldp"), R("oldp"), KG, None, A.subtract)
+            ts(R("v16"), R("v16"), KG, KG, A.subtract, A.subtract)
+        else:
+            down(t + 1)
+        if t == 1:
+            ts(R("tgi", 480, GH), R("tg", 480, GH), 6.0, None, A.mult)
+            hop(0, 0)
+            hop(0, 1)
+        if t >= 2:
+            follow(t - 1, 480, NV)
+        if t == RO - 2:
+            decode(0, own(t + 1, 0), (0,))
+        ts(R("ch"), R("pcn", 0, 60), -1.0, None, A.is_lt)
+        nexthop(t, p, 0, (0,))
+        scan(R("ci"), R("r12"), R("ch"), 1.0, A.min, A.add)
+        mm(R("ppf", 0, 60), R("upm"), R("ch"), True, False)
+        mm(R("ppf", 0, 60), R("obn"), R("ci"), False, True)
+        nexthop(t, p, 0, (1, 2))
+        tt(R("m1"), R("ppf", 0, 60), R("shf"), A.min)
+        tt(R("m2"), R("m1"), R("oldp"), A.max)
+        cp(R("sl"), R("m2"))
+        if t > 0:
+            statics(t + 1, 1 - p, "pfa", True)
+        if t == RO - 2:
+            to_list(t - 1)
+        for mk in calls_of(T, topo, core):
+            send(t, mk)
+        if t == 0:
+            prefs(1)
+            statics(1, 1, "pfa", True)
+            statics(0, 1, "pfb", True)
+            iota(R("hh"), [[256, WIN]], 0)
+            dma("G", R("hh", 16, WIN), T.toll[:], accum=True)
+            for k in range(3):
+                dma("Y", R("xx", k * WIN, k * WIN + 16), R("hh", 0, 16))
+                dma("Y", R("xx", k * WIN + 16 + NV, (k + 1) * WIN), R("hh", 16 + NV, WIN))
+            for i in range(4, 6):
+                cp(R("nt", 2304 + i, 4608, 6), R("ntc", 384, NV))
+        for c in range(4):
+            chunk(t, 1 - p, 1, c)
+            if t == RO - 2 and c > 0:
+                places(t - 1, (c - 1,))
+        if t == 0:
+            act(R("nne", 384, NV), R("nni", 384, NV), F.Exp, CB, CS)
+            ts(R("at16"), R("ati"), 16.0, None, A.add)
+            ms(R("bx"), 0.0)
+            ms(R("gt", 0, 16), 0.0)
+            sel(R("bx", 15, 143, 16), [[-16, 8]], A.not_equal, 1.0, 0)
+        else:
+            hop(t, p)
+        if t == 2:
+            ts(R("tgj", 0, 480), R("tgi", 0, 480), 255, None, A.bitwise_and)
+        if t == 3:
+            cp(R("gt", 16 + NV, 16 + NV + 480), R("tgj", 0, 480))
+        largest(1)
+        nexthop(t, 1 - p, 1)
+        if t > 0:
+            hop(t, 1 - p)
+        if t == 0:
+            pads(2, RO, False)
+            pads(2, RO, True)
+        if t == 2:
+            ts(R("tgj", 480, GH), R("tgi", 480, GH), 255, None, A.bitwise_and)
+        if t == 3:
+            cp(R("gt", 16 + NV + 480, WIN), R("tgj", 480, GH))
+        if t == RO - 2:
+            follow(t, 0, NV)
+            decode(0, None, (1,))
+            to_list(t)
+        elif t >= 1:
+            to_list(t - 1)
+        add("X", None, [], [ghost(t + 1)], "arr%d" % t, arrive)
+
+    t = RO - 1
+    for c in range(4):
+        chunk(t, 1, 0, c)
+        if c > 0:
+            places(t - 1, (c - 1,))
+    statics(t, 0, "pfb", True)
+    chunk(t, 0, 1, 0)
+    largest(0)
+    for c in range(3):
+        source(1, (c,))
+        nexthop(t, 1, 0, (c,))
+    chunk(t, 0, 1, 1)
+    winner(t)
+    chunk(t, 0, 1, 2)
+    chunk(t, 0, 1, 3)
+    hop(t, 1)
+    tt(R("lo"), R("pnb", 0, 384), R("mt", 384, NV), A.min)
+    largest(1)
+    nexthop(t, 0, 1)
+    hop(t, 0, 0, 12)
+    hop(t, 0, 12, 24, cp)
+    follow(t, 0, NV)
+    decode(1, R("lo"))
+    dma("Y", T.ypath[:], R("yp"))
+    ts(R("smj"), R("smi"), 255, None, A.bitwise_and)
+    cp(R("gt", 16, 16 + NV), R("smj"))
+    for a, b in ((0, 30), (30, 48)):
+        for fn, e, x in ((cp, "Y", 0), (act, "S", 48)):
+            fn(R("ys", 16 * (x + a), 16 * (x + b)), I(R("gt"), R("at16", x + a, x + b)))
+            dma(e, T.ysum[:, 16 * (x + a):16 * (x + b)], R("ys", 16 * (x + a), 16 * (x + b)))
+
+    seq = {}
+    for o in ops:
+        if o["key"] is None:
+            seq[o["e"]] = seq.get(o["e"], 0) + 1
+            o["at"] = ("e" + o["e"], seq[o["e"]])
+        else:
+            o["at"] = (o["key"], 1)
+    know = {e: {} for e in Q}
+    for o in ops:
+        o["waits"] = []
+        if o["e"] == "X":
+            o["clock"] = {o["key"]: 1}
+            continue
+        kn = know[o["e"]]
+        for k in sorted(o["deps"], reverse=True):
+            d = ops[k]
+            if d["key"] == "remote" or kn.get(d["at"][0], 0) >= d["at"][1]:
+                continue
+            o["waits"].append(k)
+            d["sig"] = True
+            for s, v in d["clock"].items():
+                kn[s] = max(kn.get(s, 0), v)
+        o["clock"] = dict(kn)
+        o["clock"][o["at"][0]] = o["at"][1]
+    cnt = {}
+    seen = {}
+    for o in ops:
+        if o["key"] is None:
+            cnt[o["e"]] = cnt.get(o["e"], 0) + int(o["sig"])
+            o["val"] = cnt[o["e"]]
+        else:
+            o["val"] = o["inc"]
+    for o in ops:
+        if o["e"] == "X":
+            continue
+        for k in o["waits"]:
+            s = ops[k]["at"][0]
+            Q[o["e"]].wait_ge(T.sem[s], ops[k]["val"])
+            seen[s] = max(seen.get(s, 0), ops[k]["val"])
+        ins = o["fn"]()
+        if o["key"] is None:
+            if o["sig"]:
+                ins.then_inc(T.sem[o["at"][0]], 1)
+        elif o["key"] != "remote":
+            ins.then_inc(T.sem[o["key"]], 16)
+    g.wait_ge(T.sem.sent, sent[0])
+    for o in ops:
+        if o["key"] is not None and o["key"] != "remote" and seen.get(o["key"], 0) < o["val"]:
+            g.wait_ge(T.sem[o["key"]], o["val"])

@@ -7,36 +7,40 @@ NV, NG, RO, NR = 768, 192, 6, 6
 GH = 960
 TW = GH + 16 + NV + GH
 WIN = 16 + NV + GH
-CS = 0.0095
-CB = -CS * 2316
-C0 = math.exp(CB) * 1.001
+CS = 39.0 / 4096
+N0 = 2324
+CB = -CS * N0
+C0 = 135.0 * 2.0 ** -39
+TINY = 2.0 ** -70
 MAGIC = 12582912.0
 B23 = 8388608.0
-CHUNKS = ((0, 6), (6, 10), (10, 14), (14, 16))
+NA = 4
+STAGES = ((0, 24), (24, 60))
+PP = 400
 
 f32, bf, i32, u16, f16 = "float32", "bfloat16", "int32", "uint16", "float16"
 SB = {
-    "tab": (7 * TW, bf), "pin": (NV, i32), "pf": (NV, f32), "pe": (NV, f32),
+    "tab": (7 * TW, bf), "pin": (NV, i32), "pe": (NV, bf), "nz": (NV, bf),
     "nbi": (288, i32), "nbh": (288, f16), "l1h": (320, f16), "l1t": (320, f16), "l2": (288, u16),
     "lki": (352, i32), "lkb": (352, bf), "lkt": (352, bf), "lb": (288, bf), "li": (288, i32), "lj": (288, i32),
     "a0": (288, bf), "dn": (6 * 288, bf), "orgv": (48, f32), "orgn": (48, bf), "bc": (144, bf),
-    "shi": (60, i32), "sh16": (60, u16), "shf": (60, f32), "ati": (96, i32), "at16": (96, u16),
-    "ki": (4, i32), "kf": (4, f32), "cols": (4, f32),
+    "shi": (60, i32), "sh16": (60, u16), "z0": (120, f32), "zz": (120, f32), "ati": (96, i32), "at16": (96, u16),
+    "ki": (4, i32), "kf": (4, f32), "cols": (8, f32),
     "fp": (144, f32), "fq": (160, f32), "fr": (160, f32), "iox": (144, f32), "fo": (128, f32),
-    "pm": (288, f16), "qm": (320, f16), "rm": (320, bf), "ib": (128, bf),
+    "pm": (288, f16), "qm": (320, f16), "rm": (320, bf), "ib": (128, bf), "ib15": (128, bf), "w0": (128, bf),
+    "wc": (128, bf), "wt": (128, bf), "ih": (128, f16), "lkl": (288, bf),
     "beq": (144, bf), "bsg": (144, bf), "bx": (144, f32), "shm": (128, bf), "obn": (128, bf), "upm": (128, bf),
-    "nti": (NV, f32), "nte": (NV, f32), "ntc": (NV, bf), "nt": (4608, bf),
-    "nni": (NV, f32), "nne": (NV, f32), "mt": (NV, bf),
+    "nti": (384, i32), "ntc": (NV, bf), "nt": (2 * NA * 144, bf), "nni": (384, i32), "nnc": (NV, bf),
     "v16": (48, f32), "oldp": (60, f32), "r6": (144, f32), "r12": (60, f32),
     "eq": (4608, bf), "sg": (4608, bf), "sc": (288, f32), "si": (24, i32), "sj": (24, i32), "src": (24, u16),
     "hi": (48, i32), "hj": (48, i32), "nh": (288, u16), "best": (384, bf), "neq": (GH, bf),
-    "ch": (60, bf), "ci": (60, bf), "m1": (60, f32), "m2": (60, f32), "sl": (60, u16),
-    "hh": (WIN, f32), "xx": (3 * WIN, f32), "sm": (2 * NV, f32), "smi": (NV, i32), "smj": (NV, i32),
+    "ch": (60, bf), "ci": (60, bf), "sl": (60, u16),
+    "hh": (WIN, f32), "xx": (3 * WIN, f32), "sm": (2 * NV, f32), "smi": (NV, i32),
     "ee": (96, f32), "ei": (48, i32), "ej": (48, i32), "pl": (48, u16),
-    "tg": (GH, bf), "tgi": (GH, i32), "tgj": (GH, i32), "gt": (WIN, bf), "ys": (1536, bf),
+    "tg": (GH, bf), "tgi": (GH, i32), "gt": (WIN, i32), "ys": (1536, bf),
     "lo": (384, f32), "d1": (NV, f32), "d2": (NV, f32), "yp": (NV, f32),
 }
-PS = ["pfa", "pfb", "pnb", "pcn", "ppf", "pee", "ps1", "ps2"]
+PS = ["pfa", "pfb", "pn0", "pn1", "pc0", "pc1", "nm0", "nm1"]
 SCRATCH = {k: ("sbuf", [128, v[0]], v[1]) for k, v in SB.items()}
 for _n in PS:
     SCRATCH[_n] = ("psum", [128, 512], "float32")
@@ -61,11 +65,12 @@ def calls_of(T, topo, src):
     dst = {d: T.cores[(r + d) % NR] for d in range(1, NR)}
     near = [d for d in dst if dst[d] in topo.cores_of(src)]
     far = [d for d in dst if d not in near]
+    order = [(far[0] - 1 + k) % (NR - 1) + 1 for k in range(NR - 1)]
     off = topo.engines(src, dst[far[0]])
     on = [e for e in topo.engines(src, dst[near[0]]) if e not in off]
     second = share(on, near[:2])
     second.update(share(off, far[2:] + near[2:]))
-    return [share(off, far[:2]), second]
+    return order, [share(off, far[:2]), second]
 
 
 def rank_program(g, core, T, topo):
@@ -142,7 +147,7 @@ def rank_program(g, core, T, topo):
         add("V", lambda: g.vector.transpose(ap(out), ap(in_)), [in_], [out])
 
     def act(out, in_, fn=F.Copy, bias=0.0, scale=1.0):
-        add("S", lambda: g.scalar.activation(ap(out), ap(in_), fn, bias=bias, scale=scale), [in_], [out])
+        add("S", lambda: g.scalar.activation(ap(out), ap(in_), fn, bias=ap(bias), scale=scale), [in_, bias], [out])
 
     def mm(out, lhs, rhs, start, stop):
         add("P", lambda: g.tensor.matmul(ap(out), ap(lhs), ap(rhs), start, stop), [lhs, rhs], [out])
@@ -156,10 +161,10 @@ def rank_program(g, core, T, topo):
     def sel(x, pat, op, fill, base):
         add("G", lambda: g.affine_select(ap(x), ap(x), pat, op, fill, base, 1), [x], [x])
 
-    def dma(e, out, in_, accum=False):
+    def dma(e, out, in_, accum=False, after=None):
         key = "dm%d" % ndma[0]
         ndma[0] += 1
-        reads = [in_] if isinstance(in_, tuple) else []
+        reads = [x for x in (in_, after) if isinstance(x, tuple)]
         writes = [out] if isinstance(out, tuple) else []
         if accum:
             add(e, lambda: g.dma_start(ap(out), ap(in_), accum_op=A.add), reads + writes, writes, key, 16)
@@ -169,76 +174,125 @@ def rank_program(g, core, T, topo):
     def old(t, a=0, b=GH):
         return R("tab", t * TW + a, t * TW + b)
 
-    def own(t, p):
-        return R("tab", t * TW + GH + 16 + p, t * TW + GH + 16 + NV, 2)
+    def own(t, p, a=0, b=384):
+        x = t * TW + GH + 16 + p
+        return R("tab", x + 2 * a, x + 2 * b - 1, 2)
 
     def ghost(t, a=0, b=GH):
         return R("tab", t * TW + GH + 16 + NV + a, t * TW + GH + 16 + NV + b)
 
+    def window(t):
+        return R("tab", t * TW + GH, (t + 1) * TW)
+
     def H(n, p, w, u=None):
         return R(n, w * p, w * p + (w if u is None else u))
 
+    def col(k):
+        return R("cols", k, k + 1)
+
     K, KG, KL = R("kf", 0, 1), R("kf", 1, 2), R("kf", 2, 3)
     O0 = GH + 16
+    order, calls = calls_of(T, topo, core)
 
     def pads(a, b, mark):
         if mark:
-            ts(R("tab", a * TW + GH + 2, (b - 1) * TW + GH + 3, TW), R("iox", 0, b - a), 0.0, R("cols", 0, 1), A.mult, A.add)
+            ts(R("tab", a * TW + GH, (b - 1) * TW + GH + 1, TW), R("iox", 0, b - a), 0.0, col(0), A.mult, A.add)
         else:
             for t in range(a, b):
                 ms(R("tab", t * TW + GH, t * TW + GH + 16), 0.0)
 
-    def list1(p, b):
+    def list1(p):
         for i in range(6):
             for h in range(2):
                 x = 144 * p + 16 - 8 * h
-                mm(R(b, i, 144, 6), R("pm", x, x + 128), R("nbh", 48 * i + h, 48 * i + 48, 2), h == 0, h == 1)
+                mm(R("pc0", 144 * p + i, 144 * p + 144, 6), R("pm", x, x + 128), R("nbh", 48 * i + h, 48 * i + 48, 2), h == 0, h == 1)
 
     def list2(p):
         for b in range(9):
             for c in range(2):
                 q = 160 * (b % 2) + 32 - 16 * c
                 x = 160 * p + 32 * (b // 2) + 16 * c
-                mm(R("ps2", 144 * p + b, 144 * p + 144, 9), R("qm", q, q + 128), R("l1t", x, x + 16), c == 0, c == 1)
+                mm(R("pc1", 144 * p + b, 144 * p + 144, 9), R("qm", q, q + 128), R("l1t", x, x + 16), c == 0, c == 1)
 
     def list3(p):
-        outs = [(R("ps1", 144 * p + e, 144 * p + 144, 9), 32 * e, 16) for e in range(9)]
-        outs += [(R("ps1", 288 + 24 * p, 304 + 24 * p), 288, 16), (R("ps1", 304 + 24 * p, 312 + 24 * p), 328, 8)]
+        outs = [(R("pfb", 144 * p + e, 144 * p + 144, 9), 32 * e, 16) for e in range(9)]
+        outs += [(R("pfb", 288 + 24 * p, 304 + 24 * p), 288, 16), (R("pfb", 304 + 24 * p, 312 + 24 * p), 328, 8)]
         for o, x, n in outs:
             for c in range(2):
                 q = 160 * p + 32 - 16 * c
                 mm(o, R("rm", q, q + 128), R("lkt", x + 16 * c, x + 16 * c + n), c == 0, c == 1)
 
-    def prefs(p):
-        cp(H("li", p, 144), H("ps1", p, 144))
-        ts(H("lj", p, 144), H("li", p, 144), 15, None, A.bitwise_and)
-        ts(H("a0", p, 144), H("lj", p, 144), -16.0, -524288.0, A.add, A.mult)
+    def encode(h):
+        b = R("pn%d" % h, 0, 384)
+        act(H("pe", h, 384), H("pin", h, 384), F.Exp, CB, CS)
+        ts(H("nz", h, 384), H("pin", h, 384), 0.0, None, A.is_equal)
+        mm(b, R("ib"), H("pe", h, 384), True, False)
+        mm(b, R("wc"), H("nz", h, 384), False, False)
+        mm(b, R("wt"), H("nz", h, 384), False, True)
 
     def down(t, a=0, b=288):
         act(R("dn", 288 * t + a, 288 * t + b), R("lb", a, b), F.Relu, B23 * 16 * (t + 1), -B23)
 
-    def statics(t, p, fb, first):
-        mm(R(fb, 0, 144), R("ib"), R("bc"), first, False)
-        for i in range(6):
-            x = 144 * p + 24 * i
-            mm(R(fb, i, 144, 6), R("ib"), R("a0", x, x + 24), False, False)
-            mm(R(fb, i, 144, 6), R("ib"), R("dn", 288 * t + x, 288 * t + x + 24), False, False)
-            mm(R(fb, i, 144, 6), R("ib"), H("orgn", p, 24), False, False)
-        mm(R(fb, 0, 144), R("qm", 32, 160), H("l1h", p, 160, 144), False, False)
-        mm(R(fb, 0, 144), R("qm", 176, 304), H("l1h", p, 160, 144), False, False)
+    left = {}
 
-    def chunk(t, p, k, c, first=False):
-        a, b = CHUNKS[c]
+    def score(k, out, lhs, rhs):
+        n = left.get(k, 0)
+        mm(out, lhs, rhs, n == 0, n == 35)
+        left[k] = (n + 1) % 36
+
+    def statics(t, p, k):
         fb = R(("pfa", "pfb")[k], 0, 144)
-        win = R("tab", t * TW + GH, (t + 1) * TW)
-        off = R("l2", 144 * p + 9 * a, 144 * p + 9 * b)
+        score(k, fb, R("ib"), R("bc"))
+        score(k, fb, R("ib"), H("a0", p, 144))
+        score(k, fb, R("ib"), R("dn", 288 * t + 144 * p, 288 * t + 144 * p + 144))
+        score(k, fb, R("ih"), H("l1h", p, 160, 144))
+
+    def prefs(p, step):
+        x = R("nm1", 144 * p, 144 * p + 144)
+        if step == 0:
+            cp(H("lkl", p, 144), R("pfb", 144 * p, 144 * p + 144))
+            ts(H("orgn", p, 24), R("pfb", 288 + 24 * p, 312 + 24 * p), -256.0, None, A.mult)
+            ts(H("orgv", p, 24), R("pfb", 288 + 24 * p, 312 + 24 * p), B23 + 2.0, None, A.mult)
+            for i in range(6):
+                mm(R("nm1", 144 * p + i, 144 * p + 144, 6), R("ib"), R("lkl", 144 * p + 24 * i, 144 * p + 24 * i + 24), True, False)
+                mm(R("nm1", 144 * p + i, 144 * p + 144, 6), R("ib"), H("orgn", p, 24), False, True)
+        elif step == 1:
+            ts(H("li", p, 144), x, -1.0, None, A.mult)
+            ts(H("dn", p, 144), x, -16.0, B23, A.is_gt, A.mult)
+            ts(H("lj", p, 144), H("li", p, 144), 15, None, A.bitwise_and)
+            ts(H("lb", p, 144), x, -1.0, None, A.mult)
+            ts(H("a0", p, 144), H("lj", p, 144), -524288.0, None, A.mult)
+
+    def sums_of(k, n, a, b):
+        w = {"sg": "bsg", "eq": "beq"}[n]
+        for m in range(a, b):
+            z = 2304 * k + 144 * m
+            score(k, R(("pfa", "pfb")[k], 0, 144), R(w, 15 - m, 143 - m), R(n, z, z + 144))
+
+    def fetch(t, p, k, a, b):
+        act(R("sg", 2304 * k + 144 * a, 2304 * k + 144 * b), I(window(t), R("l2", 144 * p + 9 * a, 144 * p + 9 * b)))
+
+    def match(p, k, a, b, steps=range(6)):
+        for i in steps:
+            x, y = 2304 * k + 144 * a + i, 2304 * k + 144 * b
+            tt(R("eq", x, y, 6), R("sg", x, y, 6), R("nm%d" % p, 24 * a, 24 * b), A.is_equal)
+
+    def alone(t, p, k, a, b):
         x, y = 2304 * k + 144 * a, 2304 * k + 144 * b
-        tt(R("eq", x, y), I(win, off), R("nt", 2304 * p + 144 * a, 2304 * p + 144 * b), A.is_equal)
-        act(R("sg", x, y), I(win, off), F.Sign)
-        for n, w in (("sg", "bsg"), ("eq", "beq")):
-            for m in range(a, b):
-                z = 2304 * k + 144 * m
-                mm(fb, R(w, 15 - m, 143 - m), R(n, z, z + 144), first and m == 0 and n == "sg", m == 15 and n == "eq")
+        z = NA * 144 * p
+        tt(R("sg", x, y), I(window(t), R("l2", 144 * p + 9 * a, 144 * p + 9 * b)), R("nt", z + 144 * a, z + 144 * b), A.subtract)
+        ts(R("eq", x, y), R("sg", x, y), 0.0, None, A.is_equal)
+
+    def links(t, p, k, plan):
+        for e, a, b in plan:
+            if e == "A":
+                alone(t, p, k, a, b)
+                sums_of(k, "sg", a, b)
+            else:
+                fetch(t, p, k, a, b)
+                sums_of(k, "sg", a, b)
+                match(p, k, a, b)
+            sums_of(k, "eq", a, b)
 
     def largest(k):
         scan(H("sc", k, 144), R("r6"), R(("pfa", "pfb")[k], 0, 144), 0.0, A.mult, A.max)
@@ -261,9 +315,38 @@ def rank_program(g, core, T, topo):
             else:
                 cp(H("nh", 2 * t + p, 24), H("hj", p, 24))
 
-    def winner(t):
-        act(R("best"), I(R("tab", t * TW + GH, (t + 1) * TW), R("src")))
-        mm(R("pnb", 0, 384), R("shm"), R("best"), True, True)
+    def names(p):
+        for h in range(2):
+            mm(R("pn%d" % h, 0, 192), R("w0"), R("nnc", 384 * p + 192 * h, 384 * p + 192 * h + 192), True, False)
+
+    def winner(t, out):
+        cp(H("best", 0, 192), I(window(t), R("src", 0, 12)))
+        act(H("best", 1, 192), I(window(t), R("src", 12, 24)))
+        for h in range(2):
+            mm(R("pn%d" % h, 0, 192), R("shm"), H("best", h, 192), False, True)
+        ts(out(0, 192), R("pn0", 0, 192), col(2), 0.0, A.add, A.max)
+        act(out(192, 384), R("pn1", 0, 192), F.Relu, col(2))
+
+    def differ(t, a, b):
+        tt(R("neq", 16 * a, 16 * b), I(R("tab", (t + 1) * TW + GH, (t + 1) * TW + GH + 16 + NV), R("sh16", a, b)),
+           old(t + 1, 16 * a, 16 * b), A.not_equal)
+
+    def count(s, step):
+        a, b = STAGES[s]
+        pc = "pc%d" % s
+        if step == 0:
+            for m in range(16):
+                mm(R(pc, 0, b - a), R("beq", 15 - m, 143 - m), R("neq", 16 * a + m, 16 * b, 16), m == 0, m == 15)
+        elif step == 1:
+            ts(R("ch", a, b), R(pc, 0, b - a), -1.0, None, A.is_lt)
+        elif step == 2:
+            scan(R("ci", a, b), R("r12", a, b), R("ch", a, b), 1.0, A.min, A.add)
+            mm(R(pc, PP, PP + 2 * (b - a), 2), R("upm"), R("ch", a, b), True, False)
+            mm(R(pc, PP, PP + 2 * (b - a), 2), R("obn"), R("ci", a, b), False, True)
+        elif step == 3:
+            scan(R("zz", 2 * a, 2 * b), R("z0", 2 * a, 2 * b), R(pc, PP, PP + 2 * (b - a)), 0.0, A.min, A.max)
+        else:
+            cp(R("sl", a, b), R("zz", 2 * a + 1, 2 * b, 2))
 
     def hop(t, p, a=0, b=24, fn=act):
         x = (t % 3) * WIN + 16 + p
@@ -274,70 +357,66 @@ def rank_program(g, core, T, topo):
             return R("xx", 16 + a, 16 + b)
         return R("smi", a, b) if t == RO - 1 else R("sm", (t % 2) * NV + a, (t % 2) * NV + b)
 
-    def follow(t, a, b):
+    def follow(t, a=0, b=NV):
         tt(sums(t, a, b), I(H("xx", t % 3, WIN), R("pl", a // 16, b // 16)), sums(t - 1, a, b), A.add)
 
-    def to_list(t):
+    def to_list(t, a=0, b=16):
         s = sums(t)
-        for m in range(16):
-            mm(R("pee", 0, 48), R("bx", 15 - m, 143 - m), R(s[0], s[1] + m, s[2], 16), m == 0, m == 15)
+        for m in range(a, b):
+            mm(R("pc1", 64, 112), R("bx", 15 - m, 143 - m), R(s[0], s[1] + m, s[2], 16), m == 0, m == 15)
 
     def places(t, steps=(0, 1, 2)):
         for s in steps:
             if s == 0:
                 if t == 0:
-                    cp(R("ei"), R("pee", 0, 48))
+                    cp(R("ei"), R("pc1", 64, 112))
                 else:
-                    tt(R("ei"), R("pee", 0, 48), H("ee", (t - 1) % 2, 48), A.subtract)
+                    tt(R("ei"), R("pc1", 64, 112), H("ee", (t - 1) % 2, 48), A.subtract)
                 if t < RO - 2:
-                    cp(H("ee", t % 2, 48), R("pee", 0, 48))
+                    cp(H("ee", t % 2, 48), R("pc1", 64, 112))
             elif s == 1:
                 ts(R("ej"), R("ei"), 8, None, A.arith_shift_right)
             else:
                 cp(R("pl"), R("ej"))
 
-    def decode(p, in_, steps=(0, 1)):
+    def decode(p, in_, steps=(0, 1, 2)):
         if 0 in steps:
-            act(H("d1", p, 384), in_, F.Ln, C0)
+            act(H("d1", p, 384), in_, F.Ln, 2.0 ** -60)
         if 1 in steps:
-            act(H("d2", p, 384), H("d1", p, 384), F.Identity, MAGIC + 2316, 1.0 / CS)
-            act(R("yp", p, NV, 2), H("d2", p, 384), F.Identity, -MAGIC)
+            act(H("d2", p, 384), H("d1", p, 384), F.Identity, MAGIC + N0, 1.0 / CS)
+        if 2 in steps:
+            act(R("yp", p, NV, 2), H("d2", p, 384), F.Relu, -MAGIC)
 
     sent = [0]
 
-    def send(t, mk):
-        ds = sorted(mk)
+    def send(t, s, cut):
+        a, b = STAGES[s]
         win = R("tab", (t + 1) * TW, (t + 1) * TW + GH + 16 + NV)
-        parts = [(12 * (d - 1) + 6 * h, 12 * (d - 1) + 6 * h + 6) for d in ds for h in range(2)]
-        for fn, mine in ((cp, parts[:len(ds)]), (act, parts[len(ds):])):
-            runs = []
-            for a, b in mine:
-                if runs and runs[-1][1] == a:
-                    runs[-1][1] = b
-                else:
-                    runs.append([a, b])
-            for a, b in runs:
-                fn(old(t + 2, 16 * a, 16 * b), I(win, R("sl", a, b)))
+        cp(old(t + 2, 16 * a, 16 * cut), I(win, R("sl", a, cut)))
+        act(old(t + 2, 16 * cut, 16 * b), I(win, R("sl", cut, b)))
         trs = []
-        for d in ds:
+        for j in range(a // 12, b // 12):
+            d = order[j]
             rid, pid = topo.addr(T.cores[(r + d) % NR], core)
             trs.append(RemoteDMATransfer(
-                dst_ids=[DstId(rid=rid, pnc=pid)], dma_engine_mask=sum(1 << e for e in mk[d]),
-                remote_sem=T.sem["arr%d" % t], src=ap(old(t + 2, NG * (d - 1), NG * d)),
+                dst_ids=[DstId(rid=rid, pnc=pid)], dma_engine_mask=sum(1 << e for e in calls[s][d]),
+                remote_sem=T.sem["arr%d" % t], src=ap(old(t + 2, NG * j, NG * j + NG)),
                 dst=ap(ghost(t + 1, NG * (d - 1), NG * d))))
-            sent[0] += len(mk[d])
-        add("G", lambda: g.remote_dma_fused(trs, local_sem=T.sem.sent),
-            [old(t + 2, NG * (d - 1), NG * d) for d in ds], [], "remote", 0)
+            sent[0] += len(calls[s][d])
+        add("G", lambda: g.remote_dma_fused(trs, local_sem=T.sem.sent), [old(t + 2, 16 * a, 16 * b)], [], "remote", 0)
 
-    arrive = sum(len(mk[d]) for d in range(1, NR) for mk in calls_of(T, topo, T.cores[(r - d) % NR]) if d in mk)
+    arrive = sum(len(mk[d]) for d in range(1, NR) for mk in calls_of(T, topo, T.cores[(r - d) % NR])[1] if d in mk)
 
+    turn = 12 * (order[0] - 1)
     dma("S", R("nbi"), T.nb[:])
     dma("Y", R("pin", 0, 384), T.path0[:, 0:384])
     dma("Y", R("pin", 384, NV), T.path0[:, 384:NV])
     dma("Y", R("lki", 0, 288), T.lk[:])
     dma("Y", R("lki", 288, 320), T.org[:, 0:512])
     dma("Y", R("lki", 320, 352), T.org[:, 256:NV])
-    dma("Y", R("shi"), T.shown[:])
+    dma("Y", R("shi", 0, 60 - turn), T.shown[:, turn:60])
+    if turn:
+        dma("Y", R("shi", 60 - turn, 60), T.shown[:, 0:turn])
     dma("Y", R("ati"), T.at0[:])
     dma("Y", R("tg"), T.toll[:, NV:NV + GH])
     iota(R("nti", 0, 48), [[2, 2], [32, 24]], r * NV + 1)
@@ -346,222 +425,222 @@ def rank_program(g, core, T, topo):
     iota(R("iox"), [[1, 144]], -15)
     iota(R("fq"), [[32, 5], [1000, 2], [1, 16]], -32)
     iota(R("fr"), [[32, 5], [1000, 2], [2, 16]], -32)
-    act(R("nte", 0, 48), R("nti", 0, 48), F.Exp, CB, CS)
+    iota(R("nti", 48, 384), [[2, 14], [32, 24]], r * NV + 5)
+    iota(R("bc"), [[0, 24], [2048, 6]], -135 * 2048)
+    iota(R("nni"), [[2, 384]], r * NV + 1)
+    act(R("ntc", 0, 48), R("nti", 0, 48), F.Exp, CB, CS)
     ms(ghost(0), 0.0)
-    ts(R("nti", 48, 96), R("nti", 0, 48), 4.0, None, A.add)
     ts(R("ki", 1, 2), R("ki", 0, 1), 112, None, A.bitwise_and)
     ts(R("ki", 2, 3), R("ki", 0, 1), 15, None, A.bitwise_and)
-    ts(R("nti", 96, 192), R("nti", 0, 96), 8.0, None, A.add)
-    cp(R("kf", 0, 3), R("ki", 0, 3))
-    ts(R("nti", 192, 384), R("nti", 0, 192), 16.0, None, A.add)
-    act(R("nte", 48, 384), R("nti", 48, 384), F.Exp, CB, CS)
-    act(R("ntc", 0, 384), R("nte", 0, 384), F.Relu, -C0)
     pads(0, 2, False)
+    cp(R("kf", 0, 3), R("ki", 0, 3))
+    dma("Y", old(1), ghost(0))
     for x in (R("l1h", 144, 160), R("l1h", 304, 320), R("shm")):
         ms(x, 0.0)
-    ms(R("r6"), 1.0)
-    ts(R("cols", 0, 1), KL, 15.0, None, A.is_equal)
-    ts(R("cols", 1, 2), KL, 0.0, 1e29, A.not_equal, A.mult)
-    ms(R("r6", 0, 144, 6), 0.0)
     for p in range(2):
         ts(H("pm", p, 144), R("fp"), float(p), K, A.add, A.is_equal)
-    ts(R("bsg"), R("iox"), KG, -16384.0, A.is_equal, A.mult)
-    ts(R("beq"), R("iox"), KG, -B23, A.is_equal, A.mult)
-    pads(0, 2, True)
+    ts(col(0), KL, 15.0, -2.0 ** 40, A.is_equal, A.mult)
+    ts(col(1), KL, 15.0, None, A.not_equal)
+    ts(col(2), KL, 15.0, TINY, A.is_equal, A.mult)
+    ts(col(3), KL, 15.0, 16 * TINY, A.is_equal, A.mult)
+    ts(col(4), KL, 0.0, None, A.is_equal)
+    ts(col(5), KL, 15.0, -16384.0 / TINY, A.is_equal, A.mult)
     ts(R("ib"), R("iox", 15, 143), K, -1.0, A.is_equal, A.mult)
+    ts(R("wc"), R("iox", 15, 143), K, C0, A.is_equal, A.mult)
+    ts(R("wt"), R("iox", 0, 128), KG, TINY, A.is_equal, A.mult)
+    ts(R("nbh"), R("nbi"), 16.0, None, A.add)
+    list1(0)
     for b in range(2):
         ts(H("qm", b, 160), R("fq"), 16.0 * b, K, A.add, A.is_equal)
-    for p in range(2):
-        ts(H("rm", p, 160), R("fr"), float(p), K, A.add, A.is_equal)
-    for i in range(3, 6):
-        act(R("nt", i, 2304, 6), R("ntc", 0, 384))
-    ts(R("nbh"), R("nbi"), 16.0, None, A.add)
-    list1(0, "ps1")
-    cp(R("pf", 0, 384), R("pin", 0, 384))
-    act(R("pe", 0, 384), R("pf", 0, 384), F.Exp, CB, CS)
-    cp(R("nt", 0, 2304, 6), R("ntc", 0, 384))
-    cp(R("l1h", 0, 144), R("ps1", 0, 144))
-    cp(R("pf", 384, NV), R("pin", 384, NV))
+    cp(R("l1h", 0, 144), R("pc0", 0, 144))
     vt(R("l1t", 0, 160), R("l1h", 0, 160))
     list2(0)
-    list1(1, "pfb")
-    act(R("tab", O0, O0 + 384), R("pe", 0, 384), F.Relu, -C0)
-    act(R("pe", 384, NV), R("pf", 384, NV), F.Exp, CB, CS)
-    act(R("tab", O0 + 384, O0 + NV), R("pe", 384, NV), F.Relu, -C0)
+    encode(0)
+    act(R("ntc", 48, 384), R("nti", 48, 384), F.Exp, CB, CS)
+    ts(R("ib15"), R("iox", 15, 143), K, col(1), A.is_equal, A.mult)
+    pads(0, 2, True)
+    encode(1)
+    cp(R("l2", 0, 144), R("pc1", 0, 144))
+    act(R("tab", O0, O0 + 384), R("pn0", 0, 384), F.Identity, col(3), -1.0)
+    mm(R("nm0", 0, 384), R("ib15"), R("ntc", 0, 384), True, True)
+    ts(R("bsg"), R("iox"), KG, col(5), A.is_equal, A.mult)
+    ts(R("beq"), R("iox"), KG, -B23, A.is_equal, A.mult)
+    ts(H("rm", 0, 160), R("fr"), 0.0, K, A.add, A.is_equal)
     cp(R("lkb"), R("lki"))
+    ts(R("tab", O0 + 384, O0 + NV), R("pn1", 0, 384), -1.0, col(3), A.mult, A.add)
     vt(R("lkt"), R("lkb"))
-    for i in range(1, 3):
-        cp(R("nt", i, 2304, 6), R("ntc", 0, 384))
-    cp(R("l2", 0, 144), R("ps2", 0, 144))
+    act(R("nnc", 0, 384), R("nni"), F.Exp, CB, CS)
     list3(0)
-    list3(1)
-    sel(R("bsg", 15, 143, 16), [[-16, 8]], A.not_equal, B23, 0)
-    sel(R("bsg", 15, 143, 16), [[-16, 8]], A.not_equal, -B23, -15)
-    iota(R("bc"), [[0, 24], [2048, 6]], -127 * 2048)
-    iota(R("nni", 0, 384), [[2, 384]], r * NV + 1)
+    list1(1)
     iota(R("fo"), [[16, 8], [0, 16]], 0)
-    sel(R("shm"), [[-1, 128]], A.not_equal, 1.0, 1)
-    sel(R("shm", 0, 128, 16), [[-16, 8]], A.not_equal, 0.0, 1)
-    sel(R("shm", 0, 128, 16), [[-16, 8]], A.not_equal, 2.0 ** 80, 0)
-    sel(R("shm", 0, 128, 16), [[-16, 8]], A.not_equal, 2.0 ** 80, -15)
-    iota(R("nti", 384, NV), [[2, 16], [32, 24]], r * NV + 2)
     iota(R("v16"), [[1, 2], [32, 24]], 16, 2)
     iota(R("oldp"), [[16, 60]], 0, 1)
-    iota(R("nni", 384, NV), [[2, 384]], r * NV + 2)
+    ts(R("upm"), R("fo"), KG, 4096.0, A.is_equal, A.mult)
+    ts(R("ih"), R("iox", 15, 143), K, None, A.is_equal)
+    ts(H("rm", 1, 160), R("fr"), 1.0, K, A.add, A.is_equal)
+    ms(R("r6"), 1.0)
+    ts(R("w0"), R("iox", 15, 143), K, col(4), A.is_equal, A.mult)
+    ms(R("r6", 0, 144, 6), 0.0)
+    sel(R("shm"), [[-1, 128]], A.not_equal, 1.0, 1)
+    sel(R("shm", 0, 128, 16), [[-16, 8]], A.not_equal, 0.0, 1)
+    sel(R("shm", 0, 128, 16), [[-16, 8]], A.not_equal, 1.0, -15)
+    sel(R("shm", 15, 128, 16), [[-16, 8]], A.not_equal, 1.0, -15)
+    iota(R("hh"), [[256, WIN]], 0)
+    dma("G", R("hh", 16, WIN), T.toll[:], accum=True)
+    sel(R("upm"), [[-1, 128]], A.is_gt, 0.0, 0)
+    sel(R("upm"), [[-1, 128]], A.not_equal, 80.5 * 4096, 0)
 
+    FIRST = (("A", 0, 4), ("S", 4, 8), ("S", 8, 12), ("S", 12, 14), ("S", 14, 16))
     for t in range(RO - 1):
-        p = t & 1
-        for c in range(4):
-            chunk(t, p, 0, c, first=(t == 0))
-            if t == 0 and c == 0:
-                prefs(0)
-                act(R("lb", 0, 144), R("ps1", 0, 144))
-                act(R("orgn"), R("ps1", 288, 336), F.Copy, 0.0, 2 * B23)
-                down(0, 0, 144)
-                statics(0, 0, "pfa", False)
+        p, q = t & 1, 1 - (t & 1)
         if t == 0:
-            act(R("orgv"), R("ps1", 288, 336), F.Copy, 0.0, B23 + 2.0)
-            act(R("nne", 0, 384), R("nni", 0, 384), F.Exp, CB, CS)
-            act(R("nte", 384, NV), R("nti", 384, NV), F.Exp, CB, CS)
-            cp(R("l1h", 160, 304), R("pfb", 0, 144))
-            ts(R("upm"), R("fo"), KG, 4096.0, A.is_equal, A.mult)
-            vt(R("l1t", 160, 320), R("l1h", 160, 320))
-            ts(R("sh16"), R("shi"), 16.0, None, A.add)
-            sel(R("upm"), [[-1, 128]], A.is_gt, 0.0, 0)
-            sel(R("upm"), [[-1, 128]], A.not_equal, 80.5 * 4096, 0)
-        if t >= 2:
-            places(t - 2)
-        largest(0)
-        source(p)
-        if t == 0:
-            list2(1)
-        winner(t)
-        act(own(t + 1, 1 - p), own(t, 1 - p))
-        if t < 2:
-            ts(H("mt", t, 384), H("nne", t, 384), C0, R("cols", 1, 2), A.subtract, A.max)
-        if t == 0:
-            ms(old(1), 0.0)
-        if t == 1:
-            ts(R("tgi", 0, 480), R("tg", 0, 480), 6.0, None, A.mult)
-        if t >= 2:
-            follow(t - 1, 0, 480)
-        tt(own(t + 1, p), R("pnb", 0, 384), H("mt", p, 384), A.min)
-        tt(R("neq"), I(R("tab", (t + 1) * TW + GH, (t + 1) * TW + GH + 16 + NV), R("sh16")), old(t + 1), A.not_equal)
-        if t > 0:
-            statics(t, 1 - p, "pfb", True)
-        for m in range(16):
-            mm(R("pcn", 0, 60), R("beq", 15 - m, 143 - m), R("neq", m, GH, 16), m == 0, m == 15)
-        if t == 0:
-            act(R("ntc", 384, NV), R("nte", 384, NV), F.Relu, -C0)
-            act(R("lb", 144, 288), R("ps1", 144, 288))
-            down(0, 144, 288)
-            down(1)
-            for i in range(4):
-                act(R("nt", 2304 + i, 4608, 6), R("ntc", 384, NV))
-            ms(R("r12"), 1000.0)
-            ts(R("obn"), R("fo"), KG, -4096.0, A.is_equal, A.mult)
-            cp(R("l2", 144, 288), R("ps2", 144, 288))
-            ms(R("r12", 0, 60, 12), 1.0)
-            ts(R("shf"), R("shi"), float(GH + 16), None, A.add)
-            ts(R("oldp"), R("oldp"), KG, None, A.subtract)
+            prefs(0, 0)
+            cp(R("l1h", 160, 304), R("pc0", 144, 288))
             ts(R("v16"), R("v16"), KG, KG, A.subtract, A.subtract)
+            vt(R("l1t", 160, 320), R("l1h", 160, 320))
+            links(0, 0, 0, (("S", 0, 4),))
+            list2(1)
+            prefs(0, 1)
+            statics(0, 0, 0)
+            links(0, 0, 0, (("S", 4, 8),))
+            names(0)
+            ts(R("obn"), R("fo"), KG, -4096.0, A.is_equal, A.mult)
+            ts(R("sh16"), R("shi"), 16.0, None, A.add)
+            cp(R("l2", 144, 288), R("pc1", 144, 288))
+            links(0, 0, 0, (("S", 8, 12),))
+            ms(R("r12"), 1000.0)
+            ms(R("z0", 0, 120, 2), -1e9)
+            ms(R("r12", 0, 60, 12), 1.0)
+            ts(R("z0", 1, 120, 2), R("shi"), float(GH + 16), None, A.add)
+            links(0, 0, 0, FIRST[3:])
+            list3(1)
+            for s, (a, b) in enumerate(STAGES):
+                ts(R("pc%d" % s, PP + 1, PP + 2 * (b - a), 2), R("oldp", a, b), KG, None, A.subtract)
+            act(own(1, 1), own(0, 1))
+            act(R("ntc", 384, NV), R("nti"), F.Exp, CB + CS, CS)
         else:
-            down(t + 1)
-        if t == 1:
-            ts(R("tgi", 480, GH), R("tg", 480, GH), 6.0, None, A.mult)
-            hop(0, 0)
-            hop(0, 1)
-        if t >= 2:
-            follow(t - 1, 480, NV)
-        if t == RO - 2:
-            decode(0, own(t + 1, 0), (0,))
-        ts(R("ch"), R("pcn", 0, 60), -1.0, None, A.is_lt)
-        nexthop(t, p, 0, (0,))
-        scan(R("ci"), R("r12"), R("ch"), 1.0, A.min, A.add)
-        mm(R("ppf", 0, 60), R("upm"), R("ch"), True, False)
-        mm(R("ppf", 0, 60), R("obn"), R("ci"), False, True)
-        nexthop(t, p, 0, (1, 2))
-        tt(R("m1"), R("ppf", 0, 60), R("shf"), A.min)
-        tt(R("m2"), R("m1"), R("oldp"), A.max)
-        cp(R("sl"), R("m2"))
-        if t > 0:
-            statics(t + 1, 1 - p, "pfa", True)
-        if t == RO - 2:
-            to_list(t - 1)
-        for mk in calls_of(T, topo, core):
-            send(t, mk)
-        if t == 0:
-            prefs(1)
-            statics(1, 1, "pfa", True)
-            statics(0, 1, "pfb", True)
-            iota(R("hh"), [[256, WIN]], 0)
-            dma("G", R("hh", 16, WIN), T.toll[:], accum=True)
-            for k in range(3):
-                dma("Y", R("xx", k * WIN, k * WIN + 16), R("hh", 0, 16))
+            if t < 4:
+                k = t % 3
+                dma("Y", R("xx", k * WIN, k * WIN + 16), R("hh", 0, 16), after=ghost(t))
                 dma("Y", R("xx", k * WIN + 16 + NV, (k + 1) * WIN), R("hh", 16 + NV, WIN))
-            for i in range(4, 6):
-                cp(R("nt", 2304 + i, 4608, 6), R("ntc", 384, NV))
-        for c in range(4):
-            chunk(t, 1 - p, 1, c)
-            if t == RO - 2 and c > 0:
-                places(t - 1, (c - 1,))
+            links(t, p, 0, FIRST)
+            hop(t - 1, p)
+            down(t + 1)
+        largest(0)
+        if t >= 2:
+            to_list(t - 2, 0, 7)
+        source(p, (0, 1))
+        nexthop(t, p, 0, (0,))
+        source(p, (2,))
+        winner(t, lambda a, b: own(t + 1, p, a, b))
+        if t >= 2:
+            to_list(t - 2, 7, 14)
         if t == 0:
-            act(R("nne", 384, NV), R("nni", 384, NV), F.Exp, CB, CS)
-            ts(R("at16"), R("ati"), 16.0, None, A.add)
-            ms(R("bx"), 0.0)
-            ms(R("gt", 0, 16), 0.0)
-            sel(R("bx", 15, 143, 16), [[-16, 8]], A.not_equal, 1.0, 0)
-        else:
-            hop(t, p)
-        if t == 2:
-            ts(R("tgj", 0, 480), R("tgi", 0, 480), 255, None, A.bitwise_and)
-        if t == 3:
-            cp(R("gt", 16 + NV, 16 + NV + 480), R("tgj", 0, 480))
-        largest(1)
-        nexthop(t, 1 - p, 1)
-        if t > 0:
-            hop(t, 1 - p)
+            prefs(1, 0)
+        differ(t, 0, 24)
+        count(0, 0)
+        if t >= 2:
+            to_list(t - 2, 14, 16)
+        fetch(t, q, 1, 0, 4)
+        differ(t, 24, 48)
+        fetch(t, q, 1, 4, 8)
+        count(0, 1)
+        nexthop(t, p, 0, (1,))
+        count(0, 2)
+        differ(t, 48, 60)
+        if t >= 2:
+            places(t - 2, (0,))
+        count(1, 0)
+        count(0, 3)
+        nexthop(t, p, 0, (2,))
+        count(0, 4)
+        send(t, 0, 12)
+        fill = (lambda c: places(t - 2, (c,))) if t >= 2 else (lambda c: None)
+        count(1, 1)
+        fill(1)
+        count(1, 2)
+        fetch(t, q, 1, 8, 10)
+        fill(2)
+        count(1, 3)
+        count(1, 4)
+        send(t, 1, 42)
+        fetch(t, q, 1, 10, 16)
         if t == 0:
+            prefs(1, 1)
+            mm(R("nm1", 0, 384), R("ib15"), R("ntc", 384, NV), True, True)
+        statics(t, q, 1)
+        for a, b in ((0, 4), (4, 8), (8, 10), (10, 16)):
+            sums_of(1, "sg", a, b)
+            match(q, 1, a, b)
+            sums_of(1, "eq", a, b)
+        if t == 0:
+            down(1)
+            act(R("nnc", 384, NV), R("nni"), F.Exp, CB + CS, CS)
+            for p2 in (1, 0):
+                for i in range(6):
+                    ts(R("nt", NA * 144 * p2 + i, NA * 144 * (p2 + 1), 6), R("ntc", 384 * p2, 384 * p2 + 24 * NA), col(1), None, A.mult)
             pads(2, RO, False)
             pads(2, RO, True)
-        if t == 2:
-            ts(R("tgj", 480, GH), R("tgi", 480, GH), 255, None, A.bitwise_and)
-        if t == 3:
-            cp(R("gt", 16 + NV + 480, WIN), R("tgj", 480, GH))
+        if t == 1:
+            ts(R("at16"), R("ati"), 16.0, None, A.add)
+            ms(R("bx"), 0.0)
+            ms(R("gt", 0, 16), 0)
+            sel(R("bx", 15, 143, 16), [[-16, 8]], A.not_equal, 1.0, 0)
+            ts(R("tgi"), R("tg"), 6.0, None, A.mult)
+            hop(0, 0)
+        if t >= 1:
+            hop(t, p)
         if t == RO - 2:
-            follow(t, 0, NV)
-            decode(0, None, (1,))
-            to_list(t)
-        elif t >= 1:
+            decode(0, own(t + 1, 0), (0, 1))
+        if t >= 2:
+            follow(t - 1)
+        statics(t + 1, q, 0)
+        names(q)
+        if t == RO - 2:
             to_list(t - 1)
+        if t < RO - 2:
+            cp(own(t + 2, p), own(t + 1, p))
+        largest(1)
+        nexthop(t, q, 1)
+        if t == 1:
+            ts(R("gt", 16 + NV, WIN), R("tgi"), 255, None, A.bitwise_and)
+        if t == RO - 2:
+            hop(t, q)
+            decode(0, None, (2,))
+            places(t - 1)
+            follow(t)
         add("X", None, [], [ghost(t + 1)], "arr%d" % t, arrive)
 
     t = RO - 1
-    for c in range(4):
-        chunk(t, 1, 0, c)
-        if c > 0:
-            places(t - 1, (c - 1,))
-    statics(t, 0, "pfb", True)
-    chunk(t, 0, 1, 0)
+    links(t, 1, 0, FIRST)
+    statics(t, 0, 1)
+    to_list(t - 1, 0, 8)
+    fetch(t, 0, 1, 4, 8)
+    alone(t, 0, 1, 0, 2)
     largest(0)
     for c in range(3):
         source(1, (c,))
         nexthop(t, 1, 0, (c,))
-    chunk(t, 0, 1, 1)
-    winner(t)
-    chunk(t, 0, 1, 2)
-    chunk(t, 0, 1, 3)
+    winner(t, lambda a, b: R("lo", a, b))
+    to_list(t - 1, 8, 16)
+    for n in ("sg", "eq"):
+        sums_of(1, n, 0, 2)
+    sums_of(1, "sg", 4, 8)
+    match(0, 1, 4, 8)
+    sums_of(1, "eq", 4, 8)
+    links(t, 0, 1, (("A", 2, 4),) + FIRST[2:])
     hop(t, 1)
-    tt(R("lo"), R("pnb", 0, 384), R("mt", 384, NV), A.min)
+    decode(1, R("lo"), (0,))
     largest(1)
-    nexthop(t, 0, 1)
+    for c in range(3):
+        nexthop(t, 0, 1, (c,))
+        places(t - 1, (c,))
     hop(t, 0, 0, 12)
     hop(t, 0, 12, 24, cp)
-    follow(t, 0, NV)
-    decode(1, R("lo"))
+    follow(t)
+    decode(1, None, (1, 2))
     dma("Y", T.ypath[:], R("yp"))
-    ts(R("smj"), R("smi"), 255, None, A.bitwise_and)
-    cp(R("gt", 16, 16 + NV), R("smj"))
+    ts(R("gt", 16, 16 + NV), R("smi"), 255, None, A.bitwise_and)
     for a, b in ((0, 30), (30, 48)):
         for fn, e, x in ((cp, "Y", 0), (act, "S", 48)):
             fn(R("ys", 16 * (x + a), 16 * (x + b)), I(R("gt"), R("at16", x + a, x + b)))

@@ -16,6 +16,7 @@ MAGIC = 12582912.0
 B23 = 8388608.0
 NA = 4
 STAGES = ((0, 24), (24, 60))
+HEAD = 4
 PP = 400
 
 f32, bf, i32, u16, f16 = "float32", "bfloat16", "int32", "uint16", "float16"
@@ -35,16 +36,16 @@ SB = {
     "eq": (4608, bf), "sg": (4608, bf), "sc": (288, f32), "si": (24, i32), "sj": (24, i32), "src": (24, u16),
     "hi": (48, i32), "hj": (48, i32), "nh": (288, u16), "best": (384, bf), "neq": (GH, bf),
     "ch": (60, bf), "ci": (60, bf), "sl": (60, u16),
-    "hh": (WIN, f32), "xx": (3 * WIN, f32), "sm": (2 * NV, f32), "smi": (NV, i32),
-    "ee": (96, f32), "ei": (48, i32), "ej": (48, i32), "pl": (48, u16),
-    "tg": (GH, bf), "tgi": (GH, i32), "gt": (WIN, i32), "ys": (1536, bf),
+    "hh": (WIN, f32), "xx": (2 * WIN, f32), "sm": (2 * NV, f32), "smi": (NV, i32),
+    "ee": (48, f32), "ei": (48, i32), "ej": (48, i32), "pl": (48, u16),
+    "tg": (NV + GH, bf), "tgi": (GH, i32), "gt": (WIN, i32), "ys": (1536, bf),
     "lo": (384, f32), "d1": (NV, f32), "d2": (NV, f32), "yp": (NV, f32),
 }
 PS = ["pfa", "pfb", "pn0", "pn1", "pc0", "pc1", "nm0", "nm1"]
 SCRATCH = {k: ("sbuf", [128, v[0]], v[1]) for k, v in SB.items()}
 for _n in PS:
     SCRATCH[_n] = ("psum", [128, 512], "float32")
-NDMA = 24
+NDMA = 28
 SEMAPHORES = ["eV", "eS", "eP", "eG", "sent"] + ["arr%d" % t for t in range(RO - 1)] + ["dm%d" % k for k in range(NDMA)]
 
 
@@ -70,7 +71,7 @@ def calls_of(T, topo, src):
     on = [e for e in topo.engines(src, dst[near[0]]) if e not in off]
     second = share(on, near[:2])
     second.update(share(off, far[2:] + near[2:]))
-    return order, [share(off, far[:2]), second]
+    return order, [share(off, far[:2]), share(off, far[:2]), second]
 
 
 def rank_program(g, core, T, topo):
@@ -223,12 +224,9 @@ def rank_program(g, core, T, topo):
                 mm(o, R("rm", q, q + 128), R("lkt", x + 16 * c, x + 16 * c + n), c == 0, c == 1)
 
     def encode(h):
-        b = R("pn%d" % h, 0, 384)
         act(H("pe", h, 384), H("pin", h, 384), F.Exp, CB, CS)
-        ts(H("nz", h, 384), H("pin", h, 384), 0.0, None, A.is_equal)
-        mm(b, R("ib"), H("pe", h, 384), True, False)
-        mm(b, R("wc"), H("nz", h, 384), False, False)
-        mm(b, R("wt"), H("nz", h, 384), False, True)
+        ts(H("nz", h, 384), H("pin", h, 384), 0.0, None, A.is_gt)
+        mm(R("pn%d" % h, 0, 384), R("wt"), H("nz", h, 384), True, True)
 
     def down(t, a=0, b=288):
         act(R("dn", 288 * t + a, 288 * t + b), R("lb", a, b), F.Relu, B23 * 16 * (t + 1), -B23)
@@ -252,16 +250,18 @@ def rank_program(g, core, T, topo):
         if step == 0:
             cp(H("lkl", p, 144), R("pfb", 144 * p, 144 * p + 144))
             ts(H("orgn", p, 24), R("pfb", 288 + 24 * p, 312 + 24 * p), -256.0, None, A.mult)
+        elif step == 1:
             ts(H("orgv", p, 24), R("pfb", 288 + 24 * p, 312 + 24 * p), B23 + 2.0, None, A.mult)
             for i in range(6):
                 mm(R("nm1", 144 * p + i, 144 * p + 144, 6), R("ib"), R("lkl", 144 * p + 24 * i, 144 * p + 24 * i + 24), True, False)
                 mm(R("nm1", 144 * p + i, 144 * p + 144, 6), R("ib"), H("orgn", p, 24), False, True)
-        elif step == 1:
+        elif step == 2:
             ts(H("li", p, 144), x, -1.0, None, A.mult)
-            ts(H("dn", p, 144), x, -16.0, B23, A.is_gt, A.mult)
+            act(H("dn", p, 144), x, F.Relu, 16 * B23, B23)
             ts(H("lj", p, 144), H("li", p, 144), 15, None, A.bitwise_and)
-            ts(H("lb", p, 144), x, -1.0, None, A.mult)
             ts(H("a0", p, 144), H("lj", p, 144), -524288.0, None, A.mult)
+        else:
+            act(H("lb", p, 144), x, F.Copy, 0.0, -1.0)
 
     def sums_of(k, n, a, b):
         w = {"sg": "bsg", "eq": "beq"}[n]
@@ -319,13 +319,21 @@ def rank_program(g, core, T, topo):
         for h in range(2):
             mm(R("pn%d" % h, 0, 192), R("w0"), R("nnc", 384 * p + 192 * h, 384 * p + 192 * h + 192), True, False)
 
+    spare = []
+
+    def fill(n):
+        for _ in range(min(n, len(spare))):
+            spare.pop(0)()
+
     def winner(t, out):
         cp(H("best", 0, 192), I(window(t), R("src", 0, 12)))
         act(H("best", 1, 192), I(window(t), R("src", 12, 24)))
         for h in range(2):
             mm(R("pn%d" % h, 0, 192), R("shm"), H("best", h, 192), False, True)
+        fill(1)
         ts(out(0, 192), R("pn0", 0, 192), col(2), 0.0, A.add, A.max)
         act(out(192, 384), R("pn1", 0, 192), F.Relu, col(2))
+        fill(1)
 
     def differ(t, a, b):
         tt(R("neq", 16 * a, 16 * b), I(R("tab", (t + 1) * TW + GH, (t + 1) * TW + GH + 16 + NV), R("sh16", a, b)),
@@ -348,62 +356,79 @@ def rank_program(g, core, T, topo):
         else:
             cp(R("sl", a, b), R("zz", 2 * a + 1, 2 * b, 2))
 
-    def hop(t, p, a=0, b=24, fn=act):
-        x = (t % 3) * WIN + 16 + p
-        fn(R("xx", x + 32 * a, x + 32 * b - 1, 2), I(R("hh"), R("nh", 48 * t + 24 * p + a, 48 * t + 24 * p + b)))
+    def nh(t, p):
+        return H("nh", 2 * t + p, 24)
 
-    def sums(t, a=0, b=NV):
-        if t == 0:
-            return R("xx", 16 + a, 16 + b)
-        return R("smi", a, b) if t == RO - 1 else R("sm", (t % 2) * NV + a, (t % 2) * NV + b)
+    def hop(t, p, on_vector=False):
+        out = R("xx", 16 + p, 16 + NV, 2)
+        if on_vector:
+            tt(out, I(R("hh"), nh(t, p)), R("tg", p, NV, 2), A.add)
+        else:
+            act(out, I(R("hh"), nh(t, p)))
 
-    def follow(t, a=0, b=NV):
-        tt(sums(t, a, b), I(H("xx", t % 3, WIN), R("pl", a // 16, b // 16)), sums(t - 1, a, b), A.add)
+    def sums(j):
+        return (R("sm", 0, NV), R("sm", NV, 2 * NV), R("smi"))[j]
 
-    def to_list(t, a=0, b=16):
-        s = sums(t)
+    def both(t, p, fn=act):
+        out = R("sm", p, NV, 2) if t == 0 else R("xx", WIN + 16 + p, WIN + 16 + NV, 2)
+        fn(out, I(H("xx", 0, WIN), nh(t, p)))
+
+    def follow(j):
+        tt(sums(j), I(H("xx", 1, WIN), R("pl")), sums(j - 1), A.add)
+
+    def to_list(j, a=0, b=16):
+        s = sums(j)
         for m in range(a, b):
             mm(R("pc1", 64, 112), R("bx", 15 - m, 143 - m), R(s[0], s[1] + m, s[2], 16), m == 0, m == 15)
 
-    def places(t, steps=(0, 1, 2)):
+    def places(j, steps=(0, 1, 2)):
         for s in steps:
             if s == 0:
-                if t == 0:
+                if j == 0:
                     cp(R("ei"), R("pc1", 64, 112))
+                    cp(R("ee"), R("pc1", 64, 112))
                 else:
-                    tt(R("ei"), R("pc1", 64, 112), H("ee", (t - 1) % 2, 48), A.subtract)
-                if t < RO - 2:
-                    cp(H("ee", t % 2, 48), R("pc1", 64, 112))
+                    tt(R("ei"), R("pc1", 64, 112), R("ee"), A.subtract)
             elif s == 1:
-                ts(R("ej"), R("ei"), 8, None, A.arith_shift_right)
+                ts(R("ej"), R("ei"), 10, None, A.arith_shift_right)
             else:
                 cp(R("pl"), R("ej"))
 
-    def decode(p, in_, steps=(0, 1, 2)):
-        if 0 in steps:
-            act(H("d1", p, 384), in_, F.Ln, 2.0 ** -60)
-        if 1 in steps:
-            act(H("d2", p, 384), H("d1", p, 384), F.Identity, MAGIC + N0, 1.0 / CS)
-        if 2 in steps:
-            act(R("yp", p, NV, 2), H("d2", p, 384), F.Relu, -MAGIC)
+    def decode(p, in_):
+        act(R("d1", p, NV, 2), in_, F.Ln, 2.0 ** -60)
 
     sent = [0]
 
-    def send(t, s, cut):
-        a, b = STAGES[s]
-        win = R("tab", (t + 1) * TW, (t + 1) * TW + GH + 16 + NV)
-        cp(old(t + 2, 16 * a, 16 * cut), I(win, R("sl", a, cut)))
-        act(old(t + 2, 16 * cut, 16 * b), I(win, R("sl", cut, b)))
-        trs = []
-        for j in range(a // 12, b // 12):
-            d = order[j]
+    def send(t, c):
+        pieces = []
+        for j, d in enumerate(order):
+            if d in calls[c]:
+                pieces.append((j, d, 0, HEAD) if c == 0 else (j, d, HEAD if d in calls[0] else 0, 12))
+        runs = []
+        for j, d, a, b in pieces:
+            for x in range(12 * j + a, 12 * j + b, 2):
+                runs.append(x)
+        for fn, mine in ((act, runs),) if c == 0 else ((cp, runs[:len(runs) // 2]), (act, runs[len(runs) // 2:])):
+            at = 0
+            for k in range(1, len(mine) + 1):
+                if k == len(mine) or mine[k] != mine[k - 1] + 2:
+                    a, b = mine[at], mine[k - 1] + 2
+                    if c == 0:
+                        src = I(R("tab", (t + 1) * TW + GH, (t + 1) * TW + GH + 16 + NV), R("sh16", a, b))
+                    else:
+                        src = I(R("tab", (t + 1) * TW, (t + 1) * TW + GH + 16 + NV), R("sl", a, b))
+                    fn(old(t + 2, 16 * a, 16 * b), src)
+                    at = k
+        trs, reads = [], []
+        for j, d, a, b in pieces:
             rid, pid = topo.addr(T.cores[(r + d) % NR], core)
+            reads.append(old(t + 2, NG * j + 16 * a, NG * j + 16 * b))
             trs.append(RemoteDMATransfer(
-                dst_ids=[DstId(rid=rid, pnc=pid)], dma_engine_mask=sum(1 << e for e in calls[s][d]),
-                remote_sem=T.sem["arr%d" % t], src=ap(old(t + 2, NG * j, NG * j + NG)),
-                dst=ap(ghost(t + 1, NG * (d - 1), NG * d))))
-            sent[0] += len(calls[s][d])
-        add("G", lambda: g.remote_dma_fused(trs, local_sem=T.sem.sent), [old(t + 2, 16 * a, 16 * b)], [], "remote", 0)
+                dst_ids=[DstId(rid=rid, pnc=pid)], dma_engine_mask=sum(1 << e for e in calls[c][d]),
+                remote_sem=T.sem["arr%d" % t], src=ap(reads[-1]),
+                dst=ap(ghost(t + 1, NG * (d - 1) + 16 * a, NG * (d - 1) + 16 * b))))
+            sent[0] += len(calls[c][d])
+        add("G", lambda: g.remote_dma_fused(trs, local_sem=T.sem.sent), reads, [], "remote", 0)
 
     arrive = sum(len(mk[d]) for d in range(1, NR) for mk in calls_of(T, topo, T.cores[(r - d) % NR])[1] if d in mk)
 
@@ -417,17 +442,11 @@ def rank_program(g, core, T, topo):
     dma("Y", R("shi", 0, 60 - turn), T.shown[:, turn:60])
     if turn:
         dma("Y", R("shi", 60 - turn, 60), T.shown[:, 0:turn])
-    dma("Y", R("ati"), T.at0[:])
-    dma("Y", R("tg"), T.toll[:, NV:NV + GH])
     iota(R("nti", 0, 48), [[2, 2], [32, 24]], r * NV + 1)
     iota(R("ki", 0, 1), [[1, 1]], 0, 1)
     iota(R("fp"), [[16, 9], [1000, 2], [2, 8]], -16)
     iota(R("iox"), [[1, 144]], -15)
     iota(R("fq"), [[32, 5], [1000, 2], [1, 16]], -32)
-    iota(R("fr"), [[32, 5], [1000, 2], [2, 16]], -32)
-    iota(R("nti", 48, 384), [[2, 14], [32, 24]], r * NV + 5)
-    iota(R("bc"), [[0, 24], [2048, 6]], -135 * 2048)
-    iota(R("nni"), [[2, 384]], r * NV + 1)
     act(R("ntc", 0, 48), R("nti", 0, 48), F.Exp, CB, CS)
     ms(ghost(0), 0.0)
     ts(R("ki", 1, 2), R("ki", 0, 1), 112, None, A.bitwise_and)
@@ -435,144 +454,171 @@ def rank_program(g, core, T, topo):
     pads(0, 2, False)
     cp(R("kf", 0, 3), R("ki", 0, 3))
     dma("Y", old(1), ghost(0))
-    for x in (R("l1h", 144, 160), R("l1h", 304, 320), R("shm")):
-        ms(x, 0.0)
-    for p in range(2):
-        ts(H("pm", p, 144), R("fp"), float(p), K, A.add, A.is_equal)
+    dma("Y", R("tg"), T.toll[:])
+    dma("Y", R("ati"), T.at0[:])
+    ms(R("l1h", 144, 160), 0.0)
     ts(col(0), KL, 15.0, -2.0 ** 40, A.is_equal, A.mult)
     ts(col(1), KL, 15.0, None, A.not_equal)
-    ts(col(2), KL, 15.0, TINY, A.is_equal, A.mult)
-    ts(col(3), KL, 15.0, 16 * TINY, A.is_equal, A.mult)
-    ts(col(4), KL, 0.0, None, A.is_equal)
     ts(col(5), KL, 15.0, -16384.0 / TINY, A.is_equal, A.mult)
-    ts(R("ib"), R("iox", 15, 143), K, -1.0, A.is_equal, A.mult)
-    ts(R("wc"), R("iox", 15, 143), K, C0, A.is_equal, A.mult)
+    ts(H("pm", 0, 144), R("fp"), 0.0, K, A.add, A.is_equal)
+    ts(col(2), KL, 15.0, TINY, A.is_equal, A.mult)
+    ts(col(3), KG, -1.0, None, A.mult)
+    ts(col(4), KL, 0.0, None, A.is_equal)
     ts(R("wt"), R("iox", 0, 128), KG, TINY, A.is_equal, A.mult)
+    sel(R("wt"), [[-1, 128]], A.not_equal, 2.0 ** 40, 0)
+    ts(R("bsg"), R("iox"), KG, col(5), A.is_equal, A.mult)
+    ts(R("beq"), R("iox"), KG, -B23, A.is_equal, A.mult)
+    ts(R("ib"), R("iox", 15, 143), K, -1.0, A.is_equal, A.mult)
+    ts(H("qm", 0, 160), R("fq"), 0.0, K, A.add, A.is_equal)
     ts(R("nbh"), R("nbi"), 16.0, None, A.add)
     list1(0)
-    for b in range(2):
-        ts(H("qm", b, 160), R("fq"), 16.0 * b, K, A.add, A.is_equal)
+    ts(H("qm", 1, 160), R("fq"), 16.0, K, A.add, A.is_equal)
+    ts(R("ib15"), R("iox", 15, 143), K, col(1), A.is_equal, A.mult)
+    pads(0, 2, True)
     cp(R("l1h", 0, 144), R("pc0", 0, 144))
     vt(R("l1t", 0, 160), R("l1h", 0, 160))
     list2(0)
-    encode(0)
-    act(R("ntc", 48, 384), R("nti", 48, 384), F.Exp, CB, CS)
-    ts(R("ib15"), R("iox", 15, 143), K, col(1), A.is_equal, A.mult)
-    pads(0, 2, True)
-    encode(1)
-    cp(R("l2", 0, 144), R("pc1", 0, 144))
-    act(R("tab", O0, O0 + 384), R("pn0", 0, 384), F.Identity, col(3), -1.0)
-    mm(R("nm0", 0, 384), R("ib15"), R("ntc", 0, 384), True, True)
-    ts(R("bsg"), R("iox"), KG, col(5), A.is_equal, A.mult)
-    ts(R("beq"), R("iox"), KG, -B23, A.is_equal, A.mult)
-    ts(H("rm", 0, 160), R("fr"), 0.0, K, A.add, A.is_equal)
-    cp(R("lkb"), R("lki"))
-    ts(R("tab", O0 + 384, O0 + NV), R("pn1", 0, 384), -1.0, col(3), A.mult, A.add)
-    vt(R("lkt"), R("lkb"))
-    act(R("nnc", 0, 384), R("nni"), F.Exp, CB, CS)
-    list3(0)
-    list1(1)
+    iota(R("nti", 48, 384), [[2, 14], [32, 24]], r * NV + 5)
+    iota(R("fr"), [[32, 5], [1000, 2], [2, 16]], -32)
+    iota(R("bc"), [[0, 24], [2048, 6]], -135 * 2048)
     iota(R("fo"), [[16, 8], [0, 16]], 0)
+    iota(R("nni"), [[2, 384]], r * NV + 1)
+    encode(0)
+    encode(1)
+    act(R("ntc", 48, 384), R("nti", 48, 384), F.Exp, CB, CS)
+    cp(R("l2", 0, 144), R("pc1", 0, 144))
+    for h in range(2):
+        tt(R("tab", O0 + 384 * h, O0 + 384 * h + 384), R("pn%d" % h, 0, 384), H("pe", h, 384), A.min)
+    mm(R("nm0", 0, 384), R("ib15"), R("ntc", 0, 384), True, True)
+    cp(R("lkb"), R("lki"))
+    ts(H("rm", 0, 160), R("fr"), 0.0, K, A.add, A.is_equal)
+    vt(R("lkt"), R("lkb"))
+    list3(0)
+    ts(H("pm", 1, 144), R("fp"), 1.0, K, A.add, A.is_equal)
+    list1(1)
+    for x in (R("shm"), R("l1h", 304, 320)):
+        ms(x, 0.0)
+    ts(R("ih"), R("iox", 15, 143), K, None, A.is_equal)
+    ts(R("upm"), R("fo"), KG, 4096.0, A.is_equal, A.mult)
     iota(R("v16"), [[1, 2], [32, 24]], 16, 2)
     iota(R("oldp"), [[16, 60]], 0, 1)
-    ts(R("upm"), R("fo"), KG, 4096.0, A.is_equal, A.mult)
-    ts(R("ih"), R("iox", 15, 143), K, None, A.is_equal)
-    ts(H("rm", 1, 160), R("fr"), 1.0, K, A.add, A.is_equal)
-    ms(R("r6"), 1.0)
-    ts(R("w0"), R("iox", 15, 143), K, col(4), A.is_equal, A.mult)
-    ms(R("r6", 0, 144, 6), 0.0)
+    iota(R("r6"), [[0, 144]], 1)
+    iota(R("r6", 0, 144, 6), [[0, 24]], 0)
     sel(R("shm"), [[-1, 128]], A.not_equal, 1.0, 1)
     sel(R("shm", 0, 128, 16), [[-16, 8]], A.not_equal, 0.0, 1)
     sel(R("shm", 0, 128, 16), [[-16, 8]], A.not_equal, 1.0, -15)
     sel(R("shm", 15, 128, 16), [[-16, 8]], A.not_equal, 1.0, -15)
-    iota(R("hh"), [[256, WIN]], 0)
-    dma("G", R("hh", 16, WIN), T.toll[:], accum=True)
+    iota(R("r12"), [[0, 5], [1000, 12]], 1)
+    iota(R("z0", 0, 120, 2), [[0, 60]], -int(B23))
     sel(R("upm"), [[-1, 128]], A.is_gt, 0.0, 0)
     sel(R("upm"), [[-1, 128]], A.not_equal, 80.5 * 4096, 0)
+    iota(R("hh", 0, 16 + NV), [[1024, 16 + NV]], 0)
 
     FIRST = (("A", 0, 4), ("S", 4, 8), ("S", 8, 12), ("S", 12, 14), ("S", 14, 16))
     for t in range(RO - 1):
         p, q = t & 1, 1 - (t & 1)
         if t == 0:
+            fetch(0, 0, 0, 0, 4)
+            match(0, 0, 0, 4)
             prefs(0, 0)
-            cp(R("l1h", 160, 304), R("pc0", 144, 288))
-            ts(R("v16"), R("v16"), KG, KG, A.subtract, A.subtract)
-            vt(R("l1t", 160, 320), R("l1h", 160, 320))
-            links(0, 0, 0, (("S", 0, 4),))
-            list2(1)
             prefs(0, 1)
+            for n in ("sg", "eq"):
+                sums_of(0, n, 0, 4)
+            fetch(0, 0, 0, 4, 8)
+            cp(R("l1h", 160, 304), R("pc0", 144, 288))
+            ts(R("w0"), R("iox", 15, 143), K, col(4), A.is_equal, A.mult)
+            vt(R("l1t", 160, 320), R("l1h", 160, 320))
+            sums_of(0, "sg", 4, 8)
+            match(0, 0, 4, 8)
+            sums_of(0, "eq", 4, 8)
+            fetch(0, 0, 0, 8, 12)
+            prefs(0, 2)
             statics(0, 0, 0)
-            links(0, 0, 0, (("S", 4, 8),))
-            names(0)
-            ts(R("obn"), R("fo"), KG, -4096.0, A.is_equal, A.mult)
-            ts(R("sh16"), R("shi"), 16.0, None, A.add)
-            cp(R("l2", 144, 288), R("pc1", 144, 288))
-            links(0, 0, 0, (("S", 8, 12),))
-            ms(R("r12"), 1000.0)
-            ms(R("z0", 0, 120, 2), -1e9)
-            ms(R("r12", 0, 60, 12), 1.0)
-            ts(R("z0", 1, 120, 2), R("shi"), float(GH + 16), None, A.add)
+            sums_of(0, "sg", 8, 12)
+            match(0, 0, 8, 12)
+            sums_of(0, "eq", 8, 12)
             links(0, 0, 0, FIRST[3:])
-            list3(1)
             for s, (a, b) in enumerate(STAGES):
-                ts(R("pc%d" % s, PP + 1, PP + 2 * (b - a), 2), R("oldp", a, b), KG, None, A.subtract)
-            act(own(1, 1), own(0, 1))
+                act(R("pc%d" % s, PP + 1, PP + 2 * (b - a), 2), R("oldp", a, b), F.Identity, col(3))
+            list2(1)
+            spare.append(lambda: cp(R("l2", 144, 288), R("pc1", 144, 288)))
+            ts(H("rm", 1, 160), R("fr"), 1.0, K, A.add, A.is_equal)
+            ts(R("v16"), R("v16"), KG, KG, A.subtract, A.subtract)
+            ts(R("sh16"), R("shi"), 16.0, None, A.add)
+            ts(R("obn"), R("fo"), KG, -4096.0, A.is_equal, A.mult)
+            act(R("nnc", 0, 384), R("nni"), F.Exp, CB, CS)
+            names(0)
+            prefs(0, 3)
+            act(R("z0", 1, 120, 2), R("shi"), F.Identity, float(GH + 16))
             act(R("ntc", 384, NV), R("nti"), F.Exp, CB + CS, CS)
         else:
-            if t < 4:
-                k = t % 3
-                dma("Y", R("xx", k * WIN, k * WIN + 16), R("hh", 0, 16), after=ghost(t))
-                dma("Y", R("xx", k * WIN + 16 + NV, (k + 1) * WIN), R("hh", 16 + NV, WIN))
+            if t == 1:
+                dma("G", R("hh", 16, WIN), T.toll[:], accum=True, after=ghost(t))
+            if t < 3:
+                dma("G", R("xx", 16 + NV, WIN), T.toll[:, NV:NV + GH], accum=True, after=ghost(t))
+            if t == 3:
+                dma("Y", R("xx", WIN + 16 + NV, 2 * WIN), R("xx", 16 + NV, WIN), after=ghost(t))
             links(t, p, 0, FIRST)
-            hop(t - 1, p)
-            down(t + 1)
+            if p == 0:
+                hop(t - 1, 0)
+                dma("G", R("xx", 16, 16 + NV), T.toll[:, 0:NV], accum=True)
+            if p == 1:
+                down(t + 1)
+        act(own(t + 1, q), own(t, q))
+        u = 2 * p
+        if u:
+            fetch(t, q, 1, 2, 4)
+        fill(2 if t else 0)
         largest(0)
-        if t >= 2:
-            to_list(t - 2, 0, 7)
+        if t == 3:
+            to_list(0, 0, 7)
         source(p, (0, 1))
         nexthop(t, p, 0, (0,))
         source(p, (2,))
         winner(t, lambda a, b: own(t + 1, p, a, b))
-        if t >= 2:
-            to_list(t - 2, 7, 14)
+        if t == 3:
+            to_list(0, 7, 14)
         if t == 0:
-            prefs(1, 0)
+            list3(1)
+        send(t, 0)
         differ(t, 0, 24)
         count(0, 0)
-        if t >= 2:
-            to_list(t - 2, 14, 16)
-        fetch(t, q, 1, 0, 4)
+        if t == 3:
+            to_list(0, 14, 16)
+        fetch(t, q, 1, u + 2, 6)
         differ(t, 24, 48)
-        fetch(t, q, 1, 4, 8)
+        fetch(t, q, 1, 6, u + 8)
         count(0, 1)
         nexthop(t, p, 0, (1,))
         count(0, 2)
         differ(t, 48, 60)
-        if t >= 2:
-            places(t - 2, (0,))
         count(1, 0)
         count(0, 3)
         nexthop(t, p, 0, (2,))
         count(0, 4)
-        send(t, 0, 12)
-        fill = (lambda c: places(t - 2, (c,))) if t >= 2 else (lambda c: None)
-        count(1, 1)
-        fill(1)
-        count(1, 2)
-        fetch(t, q, 1, 8, 10)
-        fill(2)
-        count(1, 3)
-        count(1, 4)
-        send(t, 1, 42)
-        fetch(t, q, 1, 10, 16)
+        send(t, 1)
+        fills = [[], [0], [1, 2], [3]] if t else [[], [], [], []]
+        for c in range(1, 5):
+            match(q, 1, 2, 6, fills[c - 1])
+            count(1, c)
+            if c == 2:
+                fetch(t, q, 1, u + 8, u + 10)
+            if t == 0 and c < 3:
+                prefs(1, c - 1)
+        send(t, 2)
         if t == 0:
-            prefs(1, 1)
+            for n in ("hh", "xx"):
+                iota(R(n, 16 + NV, WIN), [[1024, GH]], 1024 * (16 + NV))
+            prefs(1, 2)
+            prefs(1, 3)
             mm(R("nm1", 0, 384), R("ib15"), R("ntc", 384, NV), True, True)
         statics(t, q, 1)
-        for a, b in ((0, 4), (4, 8), (8, 10), (10, 16)):
-            sums_of(1, "sg", a, b)
-            match(q, 1, a, b)
-            sums_of(1, "eq", a, b)
+        sums_of(1, "sg", 2, u + 10)
+        match(q, 1, 2, 6, [i for i in range(6) if i not in sum(fills, [])])
+        sums_of(1, "eq", 2, 6)
+        match(q, 1, 6, u + 10)
+        sums_of(1, "eq", 6, u + 10)
+        links(t, q, 1, (("A" if t else "S", 0, 2), ("S", u + 10, 16)))
         if t == 0:
             down(1)
             act(R("nnc", 384, NV), R("nni"), F.Exp, CB + CS, CS)
@@ -582,64 +628,78 @@ def rank_program(g, core, T, topo):
             pads(2, RO, False)
             pads(2, RO, True)
         if t == 1:
-            ts(R("at16"), R("ati"), 16.0, None, A.add)
-            ms(R("bx"), 0.0)
-            ms(R("gt", 0, 16), 0)
+            for x in (R("bx"), R("xx", 0, 16), R("xx", WIN, WIN + 16)):
+                ms(x, 0.0)
             sel(R("bx", 15, 143, 16), [[-16, 8]], A.not_equal, 1.0, 0)
-            ts(R("tgi"), R("tg"), 6.0, None, A.mult)
-            hop(0, 0)
-        if t >= 1:
-            hop(t, p)
+        if p == 1:
+            hop(t, 1)
+        elif t:
+            both(t - 2, 0)
+            both(t - 2, 1)
         if t == RO - 2:
-            decode(0, own(t + 1, 0), (0, 1))
-        if t >= 2:
-            follow(t - 1)
+            decode(0, own(t + 1, 0))
         statics(t + 1, q, 0)
         names(q)
-        if t == RO - 2:
-            to_list(t - 1)
+        if p == 1:
+            down(t + 2)
         if t < RO - 2:
-            cp(own(t + 2, p), own(t + 1, p))
-        largest(1)
-        nexthop(t, q, 1)
-        if t == 1:
-            ts(R("gt", 16 + NV, WIN), R("tgi"), 255, None, A.bitwise_and)
+            largest(1)
+            for c in range(3):
+                nexthop(t, q, 1, (c,))
+                if t == 3:
+                    places(0, (c,))
+        if t == 0:
+            for a in range(0, GH, 160):
+                spare.append(lambda a=a: ts(R("tgi", a, a + 160), R("tg", NV + a, NV + a + 160), 6.0, None, A.mult))
+            for a in range(0, GH, 160):
+                spare.append(lambda a=a: ts(R("gt", 16 + NV + a, 176 + NV + a), R("tgi", a, a + 160), 255, None, A.bitwise_and))
+            spare.append(lambda: ts(R("at16"), R("ati"), 16.0, None, A.add))
+            spare.append(lambda: ms(R("gt", 0, 16), 0))
         if t == RO - 2:
-            hop(t, q)
-            decode(0, None, (2,))
-            places(t - 1)
-            follow(t)
+            follow(1)
+            to_list(1, 0, 6)
         add("X", None, [], [ghost(t + 1)], "arr%d" % t, arrive)
 
     t = RO - 1
     links(t, 1, 0, FIRST)
+    largest(1)
+    nexthop(t - 1, 1, 1, (0,))
     statics(t, 0, 1)
-    to_list(t - 1, 0, 8)
-    fetch(t, 0, 1, 4, 8)
-    alone(t, 0, 1, 0, 2)
+    to_list(1, 6, 11)
+    fill(len(spare))
+    fetch(t, 0, 1, 0, 4)
     largest(0)
+    nexthop(t - 1, 1, 1, (1,))
+    sums_of(1, "sg", 0, 4)
+    source(1, (0,))
+    nexthop(t - 1, 1, 1, (2,))
     for c in range(3):
-        source(1, (c,))
         nexthop(t, 1, 0, (c,))
-    winner(t, lambda a, b: R("lo", a, b))
-    to_list(t - 1, 8, 16)
-    for n in ("sg", "eq"):
-        sums_of(1, n, 0, 2)
-    sums_of(1, "sg", 4, 8)
-    match(0, 1, 4, 8)
-    sums_of(1, "eq", 4, 8)
-    links(t, 0, 1, (("A", 2, 4),) + FIRST[2:])
-    hop(t, 1)
-    decode(1, R("lo"), (0,))
+        source(1, (c + 1,) if c < 2 else ())
+    match(0, 1, 0, 4)
+    sums_of(1, "eq", 0, 4)
+    to_list(1, 11, 16)
+    links(t, 0, 1, FIRST[1:2])
+    hop(t, 1, True)
+    links(t, 0, 1, FIRST[2:])
+    act(R("best"), I(window(t), R("src")))
+    for h in range(2):
+        mm(R("pn%d" % h, 0, 192), R("shm"), H("best", h, 192), False, True)
+    for h in range(2):
+        act(H("lo", h, 192), R("pn%d" % h, 0, 192), F.Relu, col(2))
+    decode(1, R("lo"))
     largest(1)
     for c in range(3):
         nexthop(t, 0, 1, (c,))
-        places(t - 1, (c,))
-    hop(t, 0, 0, 12)
-    hop(t, 0, 12, 24, cp)
-    follow(t)
-    decode(1, None, (1, 2))
-    dma("Y", T.ypath[:], R("yp"))
+        places(1, (c,))
+    hop(t, 0, True)
+    both(t - 1, 0, cp)
+    both(t - 1, 1)
+    follow(2)
+    for h in range(2):
+        act(H("d2", h, 384), H("d1", h, 384), F.Identity, MAGIC + N0, 1.0 / CS)
+        act(H("yp", h, 384), H("d2", h, 384), F.Relu, -MAGIC)
+        dma("Y", T.ypath[:, 384 * h:384 * h + 384], H("yp", h, 384))
     ts(R("gt", 16, 16 + NV), R("smi"), 255, None, A.bitwise_and)
     for a, b in ((0, 30), (30, 48)):
         for fn, e, x in ((cp, "Y", 0), (act, "S", 48)):

@@ -17,7 +17,8 @@ B23 = 8388608.0
 NA = 4
 STAGES = ((0, 24), (24, 60))
 HEAD = 4
-PP = 400
+PN = ("pa", "pb")
+PP = 416
 
 f32, bf, i32, u16, f16 = "float32", "bfloat16", "int32", "uint16", "float16"
 SB = {
@@ -29,23 +30,23 @@ SB = {
     "ki": (4, i32), "kf": (4, f32), "cols": (8, f32),
     "fp": (144, f32), "fq": (160, f32), "fr": (160, f32), "iox": (144, f32), "fo": (128, f32),
     "pm": (288, f16), "qm": (320, f16), "rm": (320, bf), "ib": (128, bf), "ib15": (128, bf), "w0": (128, bf),
-    "wc": (128, bf), "wt": (128, bf), "ih": (128, f16), "lkl": (288, bf),
+    "ip": (128, bf), "wt": (128, bf), "ih": (128, f16), "lkl": (288, bf),
     "beq": (144, bf), "bsg": (144, bf), "bx": (144, f32), "shm": (128, bf), "obn": (128, bf), "upm": (128, bf),
-    "nti": (384, i32), "ntc": (NV, bf), "nt": (2 * NA * 144, bf), "nni": (384, i32), "nnc": (NV, bf),
-    "v16": (48, f32), "oldp": (60, f32), "r6": (144, f32), "r12": (60, f32),
+    "nti": (336, i32), "ntc": (672, bf), "n6": (288, i32), "nt": (2 * NA * 144, bf), "bz": (12, f32),
+    "nni": (384, i32), "nnc": (NV, bf),
+    "v16": (48, f32), "oldp": (60, f32), "r6": (144, f32), "r12": (120, bf),
     "eq": (4608, bf), "sg": (4608, bf), "sc": (288, f32), "si": (24, i32), "sj": (24, i32), "src": (24, u16),
-    "hi": (48, i32), "hj": (48, i32), "nh": (288, u16), "best": (384, bf), "neq": (GH, bf),
-    "ch": (60, bf), "ci": (60, bf), "sl": (60, u16),
-    "hh": (WIN, f32), "xx": (2 * WIN, f32), "sm": (2 * NV, f32), "smi": (NV, i32),
+    "hi": (96, i32), "hj": (96, i32), "nh": (288, u16), "best": (384, bf), "neq": (GH, bf),
+    "ch": (120, bf), "ci": (120, bf), "be2": (144, bf), "thr": (72, f32), "sl": (60, u16),
+    "cz": (WIN, f32), "hh": (WIN, f32), "xx": (2 * WIN, f32), "sm": (2 * NV, f32), "smi": (NV, i32),
     "ee": (48, f32), "ei": (48, i32), "ej": (48, i32), "pl": (48, u16),
     "tg": (NV + GH, bf), "tgi": (GH, i32), "gt": (WIN, i32), "ys": (1536, bf),
     "lo": (384, f32), "d1": (NV, f32), "d2": (NV, f32), "yp": (NV, f32),
 }
-PS = ["pfa", "pfb", "pn0", "pn1", "pc0", "pc1", "nm0", "nm1"]
-SCRATCH = {k: ("sbuf", [128, v[0]], v[1]) for k, v in SB.items()}
-for _n in PS:
-    SCRATCH[_n] = ("psum", [128, 512], "float32")
-NDMA = 28
+PS = {"nm": 2048, "pfa": 512, "pfb": 512, "pa": 512, "pb": 512}
+SCRATCH = {k: ("psum", [128, v], "float32") for k, v in PS.items()}
+SCRATCH.update({k: ("sbuf", [128, v[0]], v[1]) for k, v in SB.items()})
+NDMA = 34
 SEMAPHORES = ["eV", "eS", "eP", "eG", "sent"] + ["arr%d" % t for t in range(RO - 1)] + ["dm%d" % k for k in range(NDMA)]
 
 
@@ -61,7 +62,12 @@ def share(eng, ds):
     return out
 
 
-def calls_of(T, topo, src):
+ALLH = (9, 9)
+OPT = {"solo": (0, 2, 4), "fine": ((90, 122), (122, 136), (136, 144)), "o": 3, "w": (2, 2, 4), "w3": 2, "gaps": (1, 4)}
+U = (0, 2, 2, 4, 2)
+
+
+def calls_of(T, topo, src, t):
     r = T.rank_of(src)
     dst = {d: T.cores[(r + d) % NR] for d in range(1, NR)}
     near = [d for d in dst if dst[d] in topo.cores_of(src)]
@@ -71,7 +77,21 @@ def calls_of(T, topo, src):
     on = [e for e in topo.engines(src, dst[near[0]]) if e not in off]
     second = share(on, near[:2])
     second.update(share(off, far[2:] + near[2:]))
-    return order, [share(off, far[:2]), share(off, far[:2]), second]
+    allh = t >= ALLH[len(far) > 2]
+    heads = share(off, (far if OPT.get("four") else far[-2:]) if allh else far[:2])
+    if allh:
+        heads.update(share(on, near))
+    if len(far) == 2 and t >= OPT.get("three", 9):
+        first = share(off, far)
+        first[order[2]] = on
+        return order, [heads if allh else first, first, {order[3]: on, order[4]: off}, {}, {}], ((0, 36), (36, 60))
+    extra, last = {}, {}
+    if t < OPT.get("split", 0):
+        if len(far) == 2:
+            extra = share(on, near)
+        else:
+            last = {near[0]: second.pop(near[0])}
+    return order, [heads, share(off, far[:2]), second, extra, last], ((0, 24), (24, 60))
 
 
 def rank_program(g, core, T, topo):
@@ -82,7 +102,7 @@ def rank_program(g, core, T, topo):
     ops = []
     wr = {k: np.full(v[0], -1) for k, v in SB.items()}
     rd = {k: [] for k in SB}
-    bank = {k: {} for k in PS}
+    bank = {k: [{} for _ in range(n // 512)] for k, n in PS.items()}
     ndma = [0]
 
     def R(n, a=0, b=None, s=1):
@@ -105,19 +125,19 @@ def rank_program(g, core, T, topo):
         for x in reads:
             if isinstance(x, tuple):
                 flat += [x[1], x[2]] if x[0] == "*" else [x]
+        touched = [bank[x[0]][b] for x in flat + list(writes) if x[0] in bank for b in range(x[1] // 512, (x[2] - 1) // 512 + 1)]
+        for last in touched:
+            deps.update(k for q, k in last.items() if q != e)
         for x in flat + list(writes):
-            if x[0] in bank:
-                deps.update(k for q, k in bank[x[0]].items() if q != e)
-            else:
+            if x[0] not in bank:
                 deps.update(int(k) for k in np.unique(wr[x[0]][x[1]:x[2]:x[3]]) if k >= 0)
         for x in writes:
             if x[0] not in bank:
                 m = np.zeros(SB[x[0]][0], bool)
                 m[x[1]:x[2]:x[3]] = True
                 deps.update(k for k, y in rd[x[0]] if m[y[1]:y[2]:y[3]].any())
-        for x in flat + list(writes):
-            if x[0] in bank:
-                bank[x[0]][e] = me
+        for last in touched:
+            last[e] = me
         for x in flat:
             if x[0] not in bank:
                 rd[x[0]].append((me, x))
@@ -172,6 +192,17 @@ def rank_program(g, core, T, topo):
         else:
             add(e, lambda: Q[e].dma_start(ap(out), ap(in_)), reads, writes, key, 16)
 
+    def mark(out):
+        key = "dm%d" % ndma[0]
+        ndma[0] += 1
+        in_ = R("cz", out[1], out[2])
+        add("G", lambda: g.dma_start(T[out[0]][0:128:16, out[1]:out[2]], T.cz[0:128:16, out[1]:out[2]], accum_op=A.add),
+            [in_, out], [out], key, 16)
+
+    def keep(t):
+        x = t * TW + GH
+        dma("Y", R("tab", x + TW, x + TW + 16 + NV), R("tab", x, x + 16 + NV), after=ghost(t))
+
     def old(t, a=0, b=GH):
         return R("tab", t * TW + a, t * TW + b)
 
@@ -193,7 +224,7 @@ def rank_program(g, core, T, topo):
 
     K, KG, KL = R("kf", 0, 1), R("kf", 1, 2), R("kf", 2, 3)
     O0 = GH + 16
-    order, calls = calls_of(T, topo, core)
+    order = calls_of(T, topo, core, 0)[0]
 
     def pads(a, b, mark):
         if mark:
@@ -206,14 +237,14 @@ def rank_program(g, core, T, topo):
         for i in range(6):
             for h in range(2):
                 x = 144 * p + 16 - 8 * h
-                mm(R("pc0", 144 * p + i, 144 * p + 144, 6), R("pm", x, x + 128), R("nbh", 48 * i + h, 48 * i + 48, 2), h == 0, h == 1)
+                mm(R(("pfb", "pfa")[p], i, 144, 6), R("pm", x, x + 128), R("nbh", 48 * i + h, 48 * i + 48, 2), h == 0, h == 1)
 
     def list2(p):
         for b in range(9):
             for c in range(2):
                 q = 160 * (b % 2) + 32 - 16 * c
                 x = 160 * p + 32 * (b // 2) + 16 * c
-                mm(R("pc1", 144 * p + b, 144 * p + 144, 9), R("qm", q, q + 128), R("l1t", x, x + 16), c == 0, c == 1)
+                mm(R(("pfa", "pfb")[p], 340 + b, 484, 9), R("qm", q, q + 128), R("l1t", x, x + 16), c == 0, c == 1)
 
     def list3(p):
         outs = [(R("pfb", 144 * p + e, 144 * p + 144, 9), 32 * e, 16) for e in range(9)]
@@ -223,10 +254,12 @@ def rank_program(g, core, T, topo):
                 q = 160 * p + 32 - 16 * c
                 mm(o, R("rm", q, q + 128), R("lkt", x + 16 * c, x + 16 * c + n), c == 0, c == 1)
 
-    def encode(h):
-        act(H("pe", h, 384), H("pin", h, 384), F.Exp, CB, CS)
-        ts(H("nz", h, 384), H("pin", h, 384), 0.0, None, A.is_gt)
-        mm(R("pn%d" % h, 0, 384), R("wt"), H("nz", h, 384), True, True)
+    def encode():
+        for h in range(2):
+            act(H("nz", h, 384), H("pin", h, 384), F.Sign)
+            mm(R(PN[h], 0, 384), R("wt"), H("nz", h, 384), True, True)
+        for h in range(2):
+            act(H("pe", h, 384), H("pin", h, 384), F.Exp, CB, CS)
 
     def down(t, a=0, b=288):
         act(R("dn", 288 * t + a, 288 * t + b), R("lb", a, b), F.Relu, B23 * 16 * (t + 1), -B23)
@@ -246,18 +279,20 @@ def rank_program(g, core, T, topo):
         score(k, fb, R("ih"), H("l1h", p, 160, 144))
 
     def prefs(p, step):
-        x = R("nm1", 144 * p, 144 * p + 144)
+        n = PN[1 - p]
+        x = R(n, 264, 408)
         if step == 0:
             cp(H("lkl", p, 144), R("pfb", 144 * p, 144 * p + 144))
             ts(H("orgn", p, 24), R("pfb", 288 + 24 * p, 312 + 24 * p), -256.0, None, A.mult)
         elif step == 1:
             ts(H("orgv", p, 24), R("pfb", 288 + 24 * p, 312 + 24 * p), B23 + 2.0, None, A.mult)
             for i in range(6):
-                mm(R("nm1", 144 * p + i, 144 * p + 144, 6), R("ib"), R("lkl", 144 * p + 24 * i, 144 * p + 24 * i + 24), True, False)
-                mm(R("nm1", 144 * p + i, 144 * p + 144, 6), R("ib"), H("orgn", p, 24), False, True)
+                mm(R(n, 264 + i, 408, 6), R("ib"), R("lkl", 144 * p + 24 * i, 144 * p + 24 * i + 24), True, False)
+                mm(R(n, 264 + i, 408, 6), R("ib"), H("orgn", p, 24), False, True)
         elif step == 2:
             ts(H("li", p, 144), x, -1.0, None, A.mult)
             act(H("dn", p, 144), x, F.Relu, 16 * B23, B23)
+            ts(R(("ih", "ip")[p]), R("iox", 15, 143), K, None, A.is_equal)
             ts(H("lj", p, 144), H("li", p, 144), 15, None, A.bitwise_and)
             ts(H("a0", p, 144), H("lj", p, 144), -524288.0, None, A.mult)
         else:
@@ -272,16 +307,31 @@ def rank_program(g, core, T, topo):
     def fetch(t, p, k, a, b):
         act(R("sg", 2304 * k + 144 * a, 2304 * k + 144 * b), I(window(t), R("l2", 144 * p + 9 * a, 144 * p + 9 * b)))
 
-    def match(p, k, a, b, steps=range(6)):
-        for i in steps:
-            x, y = 2304 * k + 144 * a + i, 2304 * k + 144 * b
-            tt(R("eq", x, y, 6), R("sg", x, y, 6), R("nm%d" % p, 24 * a, 24 * b), A.is_equal)
+    def match(k, a, b):
+        x, y = 2304 * k + 144 * a, 2304 * k + 144 * b
+        tt(R("eq", x, y), R("sg", x, y), R("nm", 144 * (a - 2), 144 * (b - 2)) if a > 1 else R(PN[a], 264, 408), A.is_equal)
 
-    def alone(t, p, k, a, b):
+    def spare_names(p, m):
+        z = 144 * (NA * p + m)
+        mm(R(PN[m], 264, 408), R("ib15"), R("nt", z, z + 144), True, True)
+
+    def spread(p, banks=range(4)):
+        for b in banks:
+            for i in range(6):
+                x, y = (512 * b - i + 5) // 6, min(336, (512 * b + 511 - i) // 6 + 1)
+                mm(R("nm", 6 * x + i, 6 * y + i - 5, 6), R("ib15"), R("ntc", 336 * p + x, 336 * p + y), True, True)
+
+    def sixfold(p, a):
+        z = 144 * (NA * p + a)
+        act(R("nt", z, z + 288), R("n6"), F.Exp, R("bz", 2 * a + p, 2 * a + p + 1), CS)
+
+    def alone(t, p, k, a, b, steps=(0, 1)):
         x, y = 2304 * k + 144 * a, 2304 * k + 144 * b
         z = NA * 144 * p
-        tt(R("sg", x, y), I(window(t), R("l2", 144 * p + 9 * a, 144 * p + 9 * b)), R("nt", z + 144 * a, z + 144 * b), A.subtract)
-        ts(R("eq", x, y), R("sg", x, y), 0.0, None, A.is_equal)
+        if 0 in steps:
+            tt(R("sg", x, y), I(window(t), R("l2", 144 * p + 9 * a, 144 * p + 9 * b)), R("nt", z + 144 * a, z + 144 * b), A.subtract)
+        if 1 in steps:
+            ts(R("eq", x, y), R("sg", x, y), 0.0, None, A.is_equal)
 
     def links(t, p, k, plan):
         for e, a, b in plan:
@@ -291,8 +341,32 @@ def rank_program(g, core, T, topo):
             else:
                 fetch(t, p, k, a, b)
                 sums_of(k, "sg", a, b)
-                match(p, k, a, b)
+                match(k, a, b)
             sums_of(k, "eq", a, b)
+
+    def first(t, p, swap=False):
+        for a, b, c, d in ((0, 2, 4, 6), (2, 4, 6, 10)):
+            fetch(t, p, 0, c, d)
+            alone(t, p, 0, a, b, (0,))
+            sums_of(0, "sg", a, b)
+            sums_of(0, "sg", c, d)
+            match(0, c, d)
+            alone(t, p, 0, a, b, (1,))
+            sums_of(0, "eq", c, d)
+            sums_of(0, "eq", a, b)
+            if swap:
+                spread(1 - p, (a // 2,))
+        if swap or not OPT.get("fine"):
+            links(t, p, 0, (("S", 10, 14), ("S", 14, 16)))
+            return
+        for a, b in OPT["fine"]:
+            act(R("sg", 16 * a, 16 * b), I(window(t), R("l2", 144 * p + a, 144 * p + b)))
+            sums_of(0, "sg", a // 9, b // 9)
+            if a > 90:
+                sums_of(0, "eq", z // 9, a // 9)
+            tt(R("eq", 16 * a, 16 * b), R("sg", 16 * a, 16 * b), R("nm", 16 * a - 288, 16 * b - 288), A.is_equal)
+            z = a
+        sums_of(0, "eq", z // 9, 16)
 
     def largest(k):
         scan(H("sc", k, 144), R("r6"), R(("pfa", "pfb")[k], 0, 144), 0.0, A.mult, A.max)
@@ -306,18 +380,19 @@ def rank_program(g, core, T, topo):
             else:
                 cp(R("src"), R("sj"))
 
-    def nexthop(t, p, k, steps=(0, 1, 2)):
+    def nexthop(t, p, k, steps=(0, 1, 2), n=1):
+        z = 2 * (t & 1) + p
         for s in steps:
             if s == 0:
-                tt(H("hi", p, 24), R("sc", 144 * k + 5, 144 * k + 144, 6), H("v16", p, 24), A.max)
+                tt(H("hi", z, 24, 24 * n), R("sc", 144 * k + 5, 144 * (k + n), 6), H("v16", p, 24, 24 * n), A.max)
             elif s == 1:
-                ts(H("hj", p, 24), H("hi", p, 24), 2047, None, A.bitwise_and)
+                ts(H("hj", z, 24, 24 * n), H("hi", z, 24, 24 * n), 2047, None, A.bitwise_and)
             else:
-                cp(H("nh", 2 * t + p, 24), H("hj", p, 24))
+                cp(H("nh", 2 * t + p, 24, 24 * n), H("hj", z, 24, 24 * n))
 
     def names(p):
         for h in range(2):
-            mm(R("pn%d" % h, 0, 192), R("w0"), R("nnc", 384 * p + 192 * h, 384 * p + 192 * h + 192), True, False)
+            mm(R(PN[h], 0, 192), R("w0"), R("nnc", 384 * p + 192 * h, 384 * p + 192 * h + 192), True, False)
 
     spare = []
 
@@ -329,28 +404,40 @@ def rank_program(g, core, T, topo):
         cp(H("best", 0, 192), I(window(t), R("src", 0, 12)))
         act(H("best", 1, 192), I(window(t), R("src", 12, 24)))
         for h in range(2):
-            mm(R("pn%d" % h, 0, 192), R("shm"), H("best", h, 192), False, True)
+            mm(R(PN[h], 0, 192), R("shm"), H("best", h, 192), False, True)
         fill(1)
-        ts(out(0, 192), R("pn0", 0, 192), col(2), 0.0, A.add, A.max)
-        act(out(192, 384), R("pn1", 0, 192), F.Relu, col(2))
+        ts(out(0, 192), R("pa", 0, 192), col(2), 0.0, A.add, A.max)
+        act(out(192, 384), R("pb", 0, 192), F.Relu, col(2))
         fill(1)
+
+    stages = list(calls_of(T, topo, core, 0)[2])
+
+    def candidates():
+        for s, (a, b) in enumerate(stages):
+            act(R(PN[s], PP + 1, PP + 2 * (b - a), 2), R("oldp", a, b), F.Identity, col(3))
+
+    def shown_in(t):
+        return R("tab", (t + 1) * TW + GH, (t + 1) * TW + GH + 16 + NV)
 
     def differ(t, a, b):
         tt(R("neq", 16 * a, 16 * b), I(R("tab", (t + 1) * TW + GH, (t + 1) * TW + GH + 16 + NV), R("sh16", a, b)),
            old(t + 1, 16 * a, 16 * b), A.not_equal)
 
-    def count(s, step):
-        a, b = STAGES[s]
-        pc = "pc%d" % s
+    def count(s, step, between=None):
+        a, b = stages[s]
+        pc = PN[s]
         if step == 0:
-            for m in range(16):
-                mm(R(pc, 0, b - a), R("beq", 15 - m, 143 - m), R("neq", 16 * a + m, 16 * b, 16), m == 0, m == 15)
+            for m in range(8):
+                mm(R(pc, 192, 192 + 2 * (b - a)), R("be2", 15 - m, 143 - m), R("neq", 16 * a + m, 16 * b, 8), m == 0, m == 7)
         elif step == 1:
-            ts(R("ch", a, b), R(pc, 0, b - a), -1.0, None, A.is_lt)
+            tt(R("ch", 2 * a, 2 * b), R(pc, 192, 192 + 2 * (b - a)), R("thr", 0, 2 * (b - a)), A.is_lt)
         elif step == 2:
-            scan(R("ci", a, b), R("r12", a, b), R("ch", a, b), 1.0, A.min, A.add)
-            mm(R(pc, PP, PP + 2 * (b - a), 2), R("upm"), R("ch", a, b), True, False)
-            mm(R(pc, PP, PP + 2 * (b - a), 2), R("obn"), R("ci", a, b), False, True)
+            scan(R("ci", 2 * a, 2 * b), R("r12", 2 * a, 2 * b), R("ch", 2 * a, 2 * b), 1.0, A.min, A.add)
+            for h in range(2):
+                mm(R(pc, PP, PP + 2 * (b - a), 2), R("upm"), R("ch", 2 * a + h, 2 * b, 2), h == 0, False)
+            if between:
+                between()
+            mm(R(pc, PP, PP + 2 * (b - a), 2), R("obn"), R("ci", 2 * a + 1, 2 * b, 2), False, True)
         elif step == 3:
             scan(R("zz", 2 * a, 2 * b), R("z0", 2 * a, 2 * b), R(pc, PP, PP + 2 * (b - a)), 0.0, A.min, A.max)
         else:
@@ -379,16 +466,16 @@ def rank_program(g, core, T, topo):
     def to_list(j, a=0, b=16):
         s = sums(j)
         for m in range(a, b):
-            mm(R("pc1", 64, 112), R("bx", 15 - m, 143 - m), R(s[0], s[1] + m, s[2], 16), m == 0, m == 15)
+            mm(R(("pfa", "pb")[j], 192, 240), R("bx", 15 - m, 143 - m), R(s[0], s[1] + m, s[2], 16), m == 0, m == 15)
 
     def places(j, steps=(0, 1, 2)):
         for s in steps:
             if s == 0:
                 if j == 0:
-                    cp(R("ei"), R("pc1", 64, 112))
-                    cp(R("ee"), R("pc1", 64, 112))
+                    cp(R("ei"), R("pfa", 192, 240))
+                    cp(R("ee"), R("pfa", 192, 240))
                 else:
-                    tt(R("ei"), R("pc1", 64, 112), R("ee"), A.subtract)
+                    tt(R("ei"), R("pb", 192, 240), R("ee"), A.subtract)
             elif s == 1:
                 ts(R("ej"), R("ei"), 10, None, A.arith_shift_right)
             else:
@@ -399,21 +486,25 @@ def rank_program(g, core, T, topo):
 
     sent = [0]
 
-    def send(t, c):
+    def send(t, c, share_v=4):
         pieces = []
+        calls = calls_of(T, topo, core, t)[1]
         for j, d in enumerate(order):
             if d in calls[c]:
-                pieces.append((j, d, 0, HEAD) if c == 0 else (j, d, HEAD if d in calls[0] else 0, 12))
+                pieces.append((j, d, 0, HEAD) if c in (0, 3) else (j, d, HEAD if d in calls[0] or d in calls[3] else 0, 12))
+        if not pieces:
+            return
         runs = []
         for j, d, a, b in pieces:
             for x in range(12 * j + a, 12 * j + b, 2):
                 runs.append(x)
-        for fn, mine in ((act, runs),) if c == 0 else ((cp, runs[:len(runs) // 2]), (act, runs[len(runs) // 2:])):
+        cut = 0 if c in (0, 3) else len(runs) * share_v // 8
+        for fn, mine in ((cp, runs[:cut]), (act, runs[cut:])):
             at = 0
             for k in range(1, len(mine) + 1):
                 if k == len(mine) or mine[k] != mine[k - 1] + 2:
                     a, b = mine[at], mine[k - 1] + 2
-                    if c == 0:
+                    if c in (0, 3):
                         src = I(R("tab", (t + 1) * TW + GH, (t + 1) * TW + GH + 16 + NV), R("sh16", a, b))
                     else:
                         src = I(R("tab", (t + 1) * TW, (t + 1) * TW + GH + 16 + NV), R("sl", a, b))
@@ -430,7 +521,8 @@ def rank_program(g, core, T, topo):
             sent[0] += len(calls[c][d])
         add("G", lambda: g.remote_dma_fused(trs, local_sem=T.sem.sent), reads, [], "remote", 0)
 
-    arrive = sum(len(mk[d]) for d in range(1, NR) for mk in calls_of(T, topo, T.cores[(r - d) % NR])[1] if d in mk)
+    def arrive(t):
+        return sum(len(mk[d]) for d in range(1, NR) for mk in calls_of(T, topo, T.cores[(r - d) % NR], t)[1] if d in mk)
 
     turn = 12 * (order[0] - 1)
     dma("S", R("nbi"), T.nb[:])
@@ -442,269 +534,388 @@ def rank_program(g, core, T, topo):
     dma("Y", R("shi", 0, 60 - turn), T.shown[:, turn:60])
     if turn:
         dma("Y", R("shi", 60 - turn, 60), T.shown[:, 0:turn])
-    iota(R("nti", 0, 48), [[2, 2], [32, 24]], r * NV + 1)
+    iota(R("nti", 0, 48), [[2, 2], [32, 24]], r * NV + 5)
     iota(R("ki", 0, 1), [[1, 1]], 0, 1)
-    iota(R("fp"), [[16, 9], [1000, 2], [2, 8]], -16)
     iota(R("iox"), [[1, 144]], -15)
+    iota(R("fp"), [[16, 9], [1000, 2], [2, 8]], -16)
+    iota(R("nti", 48, 336), [[2, 12], [32, 24]], r * NV + 9)
     iota(R("fq"), [[32, 5], [1000, 2], [1, 16]], -32)
     act(R("ntc", 0, 48), R("nti", 0, 48), F.Exp, CB, CS)
+    act(R("ntc", 48, 336), R("nti", 48, 336), F.Exp, CB, CS)
     ms(ghost(0), 0.0)
     ts(R("ki", 1, 2), R("ki", 0, 1), 112, None, A.bitwise_and)
     ts(R("ki", 2, 3), R("ki", 0, 1), 15, None, A.bitwise_and)
-    pads(0, 2, False)
+    ms(R("tab", GH, GH + 16), 0.0)
     cp(R("kf", 0, 3), R("ki", 0, 3))
     dma("Y", old(1), ghost(0))
     dma("Y", R("tg"), T.toll[:])
     dma("Y", R("ati"), T.at0[:])
     ms(R("l1h", 144, 160), 0.0)
-    ts(col(0), KL, 15.0, -2.0 ** 40, A.is_equal, A.mult)
     ts(col(1), KL, 15.0, None, A.not_equal)
+    ts(col(0), KL, 15.0, -2.0 ** 40, A.is_equal, A.mult)
+    ts(R("ib15"), R("iox", 15, 143), K, col(1), A.is_equal, A.mult)
     ts(col(5), KL, 15.0, -16384.0 / TINY, A.is_equal, A.mult)
-    ts(H("pm", 0, 144), R("fp"), 0.0, K, A.add, A.is_equal)
-    ts(col(2), KL, 15.0, TINY, A.is_equal, A.mult)
-    ts(col(3), KG, -1.0, None, A.mult)
-    ts(col(4), KL, 0.0, None, A.is_equal)
     ts(R("wt"), R("iox", 0, 128), KG, TINY, A.is_equal, A.mult)
+    ts(H("pm", 0, 144), R("fp"), 0.0, K, A.add, A.is_equal)
+    ts(col(6), KL, 15.0, -200.0, A.is_equal, A.mult)
     sel(R("wt"), [[-1, 128]], A.not_equal, 2.0 ** 40, 0)
+    iota(R("fr"), [[32, 5], [1000, 2], [2, 16]], -32)
+    iota(R("n6"), [[2, 2], [32, 24], [0, 6]], r * NV + 1 - N0)
+    iota(R("bc"), [[0, 24], [2048, 6]], -135 * 2048)
     ts(R("bsg"), R("iox"), KG, col(5), A.is_equal, A.mult)
+    ts(R("bz"), R("iox", 15, 27), CS, col(6), A.mult, A.add)
     ts(R("beq"), R("iox"), KG, -B23, A.is_equal, A.mult)
     ts(R("ib"), R("iox", 15, 143), K, -1.0, A.is_equal, A.mult)
-    ts(H("qm", 0, 160), R("fq"), 0.0, K, A.add, A.is_equal)
     ts(R("nbh"), R("nbi"), 16.0, None, A.add)
+    spread(0, (0, 1))
     list1(0)
-    ts(H("qm", 1, 160), R("fq"), 16.0, K, A.add, A.is_equal)
-    ts(R("ib15"), R("iox", 15, 143), K, col(1), A.is_equal, A.mult)
-    pads(0, 2, True)
-    cp(R("l1h", 0, 144), R("pc0", 0, 144))
+    for b in range(2):
+        ts(H("qm", b, 160), R("fq"), 16.0 * b, K, A.add, A.is_equal)
+    cp(R("tab", GH, GH + 1), col(0))
+    ms(R("shm"), 0.0)
+    encode()
+    cp(R("l1h", 0, 144), R("pfb", 0, 144))
+    ts(H("rm", 0, 160), R("fr"), 0.0, K, A.add, A.is_equal)
     vt(R("l1t", 0, 160), R("l1h", 0, 160))
     list2(0)
-    iota(R("nti", 48, 384), [[2, 14], [32, 24]], r * NV + 5)
-    iota(R("fr"), [[32, 5], [1000, 2], [2, 16]], -32)
-    iota(R("bc"), [[0, 24], [2048, 6]], -135 * 2048)
-    iota(R("fo"), [[16, 8], [0, 16]], 0)
-    iota(R("nni"), [[2, 384]], r * NV + 1)
-    encode(0)
-    encode(1)
-    act(R("ntc", 48, 384), R("nti", 48, 384), F.Exp, CB, CS)
-    cp(R("l2", 0, 144), R("pc1", 0, 144))
+    spread(0, (2, 3))
     for h in range(2):
-        tt(R("tab", O0 + 384 * h, O0 + 384 * h + 384), R("pn%d" % h, 0, 384), H("pe", h, 384), A.min)
-    mm(R("nm0", 0, 384), R("ib15"), R("ntc", 0, 384), True, True)
-    cp(R("lkb"), R("lki"))
-    ts(H("rm", 0, 160), R("fr"), 0.0, K, A.add, A.is_equal)
+        tt(R("tab", O0 + 384 * h, O0 + 384 * h + 384), R(PN[h], 0, 384), H("pe", h, 384), A.min)
+    act(R("lkb"), R("lki"))
+    sixfold(0, 0)
+    cp(R("l2", 0, 144), R("pfa", 340, 484))
+    keep(0)
     vt(R("lkt"), R("lkb"))
     list3(0)
-    ts(H("pm", 1, 144), R("fp"), 1.0, K, A.add, A.is_equal)
-    list1(1)
-    for x in (R("shm"), R("l1h", 304, 320)):
-        ms(x, 0.0)
-    ts(R("ih"), R("iox", 15, 143), K, None, A.is_equal)
-    ts(R("upm"), R("fo"), KG, 4096.0, A.is_equal, A.mult)
-    iota(R("v16"), [[1, 2], [32, 24]], 16, 2)
-    iota(R("oldp"), [[16, 60]], 0, 1)
     iota(R("r6"), [[0, 144]], 1)
+    iota(R("nni"), [[2, 384]], r * NV + 1)
     iota(R("r6", 0, 144, 6), [[0, 24]], 0)
     sel(R("shm"), [[-1, 128]], A.not_equal, 1.0, 1)
+    iota(R("fo"), [[16, 8], [0, 16]], 0)
     sel(R("shm", 0, 128, 16), [[-16, 8]], A.not_equal, 0.0, 1)
+    iota(R("oldp"), [[16, 60]], 0, 1)
     sel(R("shm", 0, 128, 16), [[-16, 8]], A.not_equal, 1.0, -15)
     sel(R("shm", 15, 128, 16), [[-16, 8]], A.not_equal, 1.0, -15)
-    iota(R("r12"), [[0, 5], [1000, 12]], 1)
+    iota(R("thr"), [[0, 36], [1, 2]], 0)
+    iota(R("r12"), [[0, 5], [10, 24]], 1)
     iota(R("z0", 0, 120, 2), [[0, 60]], -int(B23))
-    sel(R("upm"), [[-1, 128]], A.is_gt, 0.0, 0)
-    sel(R("upm"), [[-1, 128]], A.not_equal, 80.5 * 4096, 0)
-    iota(R("hh", 0, 16 + NV), [[1024, 16 + NV]], 0)
+    iota(R("v16"), [[1, 2], [32, 24]], 16, 2)
+    dma("G", R("hh", 16, WIN), T.toll[:])
 
     FIRST = (("A", 0, 4), ("S", 4, 8), ("S", 8, 12), ("S", 12, 14), ("S", 14, 16))
     for t in range(RO - 1):
         p, q = t & 1, 1 - (t & 1)
         if t == 0:
-            fetch(0, 0, 0, 0, 4)
-            match(0, 0, 0, 4)
+            fetch(0, 0, 0, 2, 6)
+            alone(0, 0, 0, 0, 2, (0,))
+            ts(col(4), KL, 0.0, None, A.is_equal)
+            alone(0, 0, 0, 0, 2, (1,))
             prefs(0, 0)
+            sums_of(0, "sg", 0, 6)
             prefs(0, 1)
-            for n in ("sg", "eq"):
-                sums_of(0, n, 0, 4)
-            fetch(0, 0, 0, 4, 8)
-            cp(R("l1h", 160, 304), R("pc0", 144, 288))
-            ts(R("w0"), R("iox", 15, 143), K, col(4), A.is_equal, A.mult)
-            vt(R("l1t", 160, 320), R("l1h", 160, 320))
-            sums_of(0, "sg", 4, 8)
-            match(0, 0, 4, 8)
-            sums_of(0, "eq", 4, 8)
-            fetch(0, 0, 0, 8, 12)
+            match(0, 2, 6)
+            fetch(0, 0, 0, 6, 10)
+            sums_of(0, "eq", 0, 6)
+            fetch(0, 0, 0, 10, 14)
+            fetch(0, 0, 0, 14, 16)
+            sums_of(0, "sg", 6, 10)
             prefs(0, 2)
+            match(0, 6, 10)
+            sums_of(0, "sg", 10, 14)
+            sums_of(0, "eq", 6, 10)
+            sums_of(0, "sg", 14, 16)
             statics(0, 0, 0)
-            sums_of(0, "sg", 8, 12)
-            match(0, 0, 8, 12)
-            sums_of(0, "eq", 8, 12)
-            links(0, 0, 0, FIRST[3:])
-            for s, (a, b) in enumerate(STAGES):
-                act(R("pc%d" % s, PP + 1, PP + 2 * (b - a), 2), R("oldp", a, b), F.Identity, col(3))
-            list2(1)
-            spare.append(lambda: cp(R("l2", 144, 288), R("pc1", 144, 288)))
-            ts(H("rm", 1, 160), R("fr"), 1.0, K, A.add, A.is_equal)
-            ts(R("v16"), R("v16"), KG, KG, A.subtract, A.subtract)
-            ts(R("sh16"), R("shi"), 16.0, None, A.add)
-            ts(R("obn"), R("fo"), KG, -4096.0, A.is_equal, A.mult)
-            act(R("nnc", 0, 384), R("nni"), F.Exp, CB, CS)
-            names(0)
+            match(0, 10, 14)
+            sums_of(0, "eq", 10, 14)
+            match(0, 14, 16)
+            sums_of(0, "eq", 14, 16)
             prefs(0, 3)
-            act(R("z0", 1, 120, 2), R("shi"), F.Identity, float(GH + 16))
-            act(R("ntc", 384, NV), R("nti"), F.Exp, CB + CS, CS)
+            act(R("nnc", 0, 384), R("nni"), F.Exp, CB, CS)
+            ts(R("w0"), R("iox", 15, 143), K, col(4), A.is_equal, A.mult)
+            ts(R("upm"), R("fo"), KG, 4096.0, A.is_equal, A.mult)
+            names(0)
+            sel(R("upm"), [[-1, 128]], A.is_gt, 0.0, 0)
+            sel(R("upm"), [[-1, 128]], A.not_equal, 80.5 * 4096, 0)
         else:
+            keep(t)
             if t == 1:
-                dma("G", R("hh", 16, WIN), T.toll[:], accum=True, after=ghost(t))
-            if t < 3:
-                dma("G", R("xx", 16 + NV, WIN), T.toll[:, NV:NV + GH], accum=True, after=ghost(t))
+                mark(R("hh", 16, WIN))
+            if t == 2:
+                mark(R("xx", 16 + NV, WIN))
             if t == 3:
                 dma("Y", R("xx", WIN + 16 + NV, 2 * WIN), R("xx", 16 + NV, WIN), after=ghost(t))
-            links(t, p, 0, FIRST)
+            first(t, p)
             if p == 0:
                 hop(t - 1, 0)
                 dma("G", R("xx", 16, 16 + NV), T.toll[:, 0:NV], accum=True)
             if p == 1:
                 down(t + 1)
-        act(own(t + 1, q), own(t, q))
-        u = 2 * p
+        u = OPT.get("u", U)[t]
         if u:
-            fetch(t, q, 1, 2, 4)
-        fill(2 if t else 0)
-        largest(0)
-        if t == 3:
-            to_list(0, 0, 7)
-        source(p, (0, 1))
-        nexthop(t, p, 0, (0,))
-        source(p, (2,))
-        winner(t, lambda a, b: own(t + 1, p, a, b))
-        if t == 3:
-            to_list(0, 7, 14)
+            fetch(t, q, 1, 2, u + 2)
         if t == 0:
+            largest(0)
+            ts(H("pm", 1, 144), R("fp"), 1.0, K, A.add, A.is_equal)
+            list1(1)
+            source(0, (0,))
+            ts(col(3), KG, -1.0, None, A.mult)
+            act(R("ntc", 336, 672), R("nti"), F.Exp, CB + CS, CS)
+            act(R("z0", 1, 120, 2), R("shi"), F.Identity, float(GH + 16))
+            sixfold(1, 0)
+            act(R("nnc", 384, NV), R("nni"), F.Exp, CB + CS, CS)
+            source(0, (1,))
+            ts(col(2), KL, 15.0, TINY, A.is_equal, A.mult)
+            source(0, (2,))
+            ts(R("sh16"), R("shi"), 16.0, None, A.add)
+            spare.append(lambda: (ms(R("l1h", 304, 320), 0.0), cp(R("l1h", 160, 304), R("pfa", 0, 144)),
+                                  ts(col(7), KL, 8.0, None, A.is_ge)))
+            spare.append(lambda: vt(R("l1t", 160, 320), R("l1h", 160, 320)))
+            winner(0, lambda a, b: own(1, 0, a, b))
+            list2(1)
+            send(0, 0)
+            send(0, 3)
+            act(R("neq", 576, GH), I(shown_in(0), R("sh16", 36, 60)), F.Abs)
+            candidates()
+            differ(0, 0, 24)
+            tt(R("be2", 8, 144), R("beq", 8, 144), R("beq", 0, 136), A.add)
+            ts(R("thr"), R("thr"), col(7), -1e29, A.not_equal, A.mult)
+            differ(0, 24, 36)
+            count(0, 0)
+            sixfold(1, 2)
+            cp(R("l2", 144, 288), R("pfb", 340, 484))
+            count(1, 0)
+            fetch(0, 1, 1, 2, 4)
+            count(0, 1)
+            ts(R("obn"), R("fo"), KG, -4096.0, A.is_equal, A.mult)
+            count(0, 2)
+            count(1, 1)
+            ts(H("rm", 1, 160), R("fr"), 1.0, K, A.add, A.is_equal)
+            count(0, 3)
+            count(1, 2)
+            count(0, 4)
             list3(1)
-        send(t, 0)
-        differ(t, 0, 24)
-        count(0, 0)
-        if t == 3:
-            to_list(0, 14, 16)
-        fetch(t, q, 1, u + 2, 6)
-        differ(t, 24, 48)
-        fetch(t, q, 1, 6, u + 8)
-        count(0, 1)
-        nexthop(t, p, 0, (1,))
-        count(0, 2)
-        differ(t, 48, 60)
-        count(1, 0)
-        count(0, 3)
-        nexthop(t, p, 0, (2,))
-        count(0, 4)
-        send(t, 1)
-        fills = [[], [0], [1, 2], [3]] if t else [[], [], [], []]
-        for c in range(1, 5):
-            match(q, 1, 2, 6, fills[c - 1])
-            count(1, c)
-            if c == 2:
-                fetch(t, q, 1, u + 8, u + 10)
-            if t == 0 and c < 3:
-                prefs(1, c - 1)
-        send(t, 2)
+            send(0, 1)
+            count(1, 3)
+            ts(R("v16"), R("v16"), KG, KG, A.subtract, A.subtract)
+            count(1, 4)
+            send(0, 2)
+            send(0, 4)
+            spread(1)
+            prefs(1, 0)
+            prefs(1, 1)
+            fetch(0, 1, 1, 4, 8)
+            fetch(0, 1, 1, 8, 14)
+            u = 4
+        else:
+            if t == 1:
+                sixfold(0, 2)
+            fill(2)
+            largest(0)
+            spread(q, (0, 1, 2))
+            source(p, (0, 1))
+            nexthop(t, p, 0, (0,) if p else ())
+            source(p, (2,))
+            winner(t, lambda a, b: own(t + 1, p, a, b))
+            spread(q, (3,))
+            got = u + 2
+            send(t, 0)
+            if stages != list(calls_of(T, topo, core, t)[2]):
+                stages[:] = calls_of(T, topo, core, t)[2]
+                candidates()
+            cut = OPT.get("cut", 48)
+            w1, w2, sv = OPT.get("w", (0, 2, 0))
+            act(old(t + 2, 16 * cut, GH), I(shown_in(t), R("sh16", cut, 60)))
+            differ(t, 0, stages[0][1])
+            mm(R("pfb", 0, GH - 16 * cut), R("ib"), old(t + 1, 16 * cut, GH), True, False)
+            if t == 3:
+                to_list(0, 0, 6)
+            count(0, 0)
+            mm(R("pfb", 0, GH - 16 * cut), R("ip"), old(t + 2, 16 * cut, GH), False, True)
+            if t == 3:
+                to_list(0, 6, 8)
+            if w1:
+                fetch(t, q, 1, got, got + w1)
+                got += w1
+            act(R("neq", 16 * cut, GH), R("pfb", 0, GH - 16 * cut), F.Abs)
+            if w2:
+                fetch(t, q, 1, got, got + w2)
+                got += w2
+            differ(t, stages[0][1], cut)
+            done = [2]
+
+            def gap(k):
+                if k in OPT.get("gaps", ()) and done[0] < got:
+                    match(1, done[0], done[0] + 1)
+                    done[0] += 1
+            count(0, 1)
+            nexthop(t, p, 0, (1,) if p else ())
+            if not p:
+                gap(0)
+            if OPT.get("o") == 4:
+                count(0, 2, lambda: count(1, 0))
+                gap(1)
+                count(1, 1)
+                count(0, 3)
+                count(1, 2)
+                count(0, 4)
+                statics(t, q, 1)
+                sums_of(1, "sg", 2, got)
+                send(t, 1, sv)
+            else:
+                count(0, 2)
+                count(1, 0)
+                if t == 3:
+                    to_list(0, 8, 10)
+                gap(1)
+                count(0, 3)
+                gap(2)
+                count(0, 4)
+                if OPT.get("o") == 2:
+                    send(t, 1, sv)
+                count(1, 1)
+                if OPT.get("o") == 3:
+                    send(t, 1, sv)
+                else:
+                    gap(3)
+                count(1, 2)
+                statics(t, q, 1)
+                sums_of(1, "sg", 2, got)
+                if OPT.get("o") not in (2, 3):
+                    send(t, 1, sv)
+                else:
+                    gap(4)
+            if OPT.get("w3"):
+                fetch(t, q, 1, got, got + OPT["w3"])
+            count(1, 3)
+            nexthop(t, p, 0, (2,) if p else ())
+            if not p:
+                gap(5)
+            count(1, 4)
+            send(t, 2)
+            if OPT.get("w3"):
+                sums_of(1, "sg", got, got + OPT["w3"])
+                got += OPT["w3"]
+            done = done[0]
+            sums_of(1, "eq", 2, done)
         if t == 0:
-            for n in ("hh", "xx"):
-                iota(R(n, 16 + NV, WIN), [[1024, GH]], 1024 * (16 + NV))
+            iota(R("cz", 16, WIN), [[1024, NV + GH]], 1024 * 16)
+            match(1, 2, 8)
             prefs(1, 2)
             prefs(1, 3)
-            mm(R("nm1", 0, 384), R("ib15"), R("ntc", 384, NV), True, True)
-        statics(t, q, 1)
-        sums_of(1, "sg", 2, u + 10)
-        match(q, 1, 2, 6, [i for i in range(6) if i not in sum(fills, [])])
-        sums_of(1, "eq", 2, 6)
-        match(q, 1, 6, u + 10)
-        sums_of(1, "eq", 6, u + 10)
-        links(t, q, 1, (("A" if t else "S", 0, 2), ("S", u + 10, 16)))
+            statics(t, q, 1)
+            sums_of(1, "sg", 2, 14)
+            sums_of(1, "eq", 2, 8)
+            done, got = 8, 14
+        solo = t in OPT.get("solo", ())
+        runs = [(done, got)] + [(a, min(a + 4, 16)) for a in range(got, 16, 4)]
+        for n, (a, b) in enumerate(runs):
+            if n:
+                fetch(t, q, 1, a, b)
+                sums_of(1, "sg", a, b)
+            if t == 3 and n == 0:
+                to_list(0, 10, 16)
+            if t == 4 and n == len(runs) - 1:
+                to_list(1, 0, 4)
+            if a < b:
+                match(1, a, b)
+                sums_of(1, "eq", a, b)
+            if n == 0:
+                if solo:
+                    links(t, q, 1, (("A", 0, 2),))
+                else:
+                    for m in range(2):
+                        spare_names(q, m)
+            if t == 1 and n < 2:
+                ts(R("xx", 16 + NV + 480 * n, 496 + NV + 480 * n), R("tg", NV + 480 * n, NV + 480 * n + 480), 2.0, None, A.mult)
+            if t == 4 and n == 0:
+                both(2, 0)
+                both(2, 1)
+                follow(1)
+        if not solo:
+            fetch(t, q, 1, 0, 2)
+            sums_of(1, "sg", 0, 2)
+            for m in range(2):
+                match(1, m, m + 1)
+            sums_of(1, "eq", 0, 2)
         if t == 0:
             down(1)
-            act(R("nnc", 384, NV), R("nni"), F.Exp, CB + CS, CS)
-            for p2 in (1, 0):
-                for i in range(6):
-                    ts(R("nt", NA * 144 * p2 + i, NA * 144 * (p2 + 1), 6), R("ntc", 384 * p2, 384 * p2 + 24 * NA), col(1), None, A.mult)
-            pads(2, RO, False)
-            pads(2, RO, True)
+        if t == 0:
+            iota(R("hh", 0, 16), [[0, 16]], 0)
         if t == 1:
-            for x in (R("bx"), R("xx", 0, 16), R("xx", WIN, WIN + 16)):
-                ms(x, 0.0)
+            for x in (R("xx", 0, 16), R("xx", WIN, WIN + 16), R("bx")):
+                iota(x, [[0, x[2] - x[1]]], 0)
             sel(R("bx", 15, 143, 16), [[-16, 8]], A.not_equal, 1.0, 0)
         if p == 1:
             hop(t, 1)
-        elif t:
-            both(t - 2, 0)
-            both(t - 2, 1)
-        if t == RO - 2:
-            decode(0, own(t + 1, 0))
+        elif t == 2:
+            both(0, 0)
+            both(0, 1)
         statics(t + 1, q, 0)
-        names(q)
+        if t < RO - 2:
+            names(q)
         if p == 1:
             down(t + 2)
-        if t < RO - 2:
+        if t in OPT.get("late", (0, 4)):
+            spare[0:0] = [lambda: largest(1)] + [lambda c=c, t=t, p=p: nexthop(t, 0, p, (c,), 2 - p) for c in range(3)]
+        else:
             largest(1)
-            for c in range(3):
-                nexthop(t, q, 1, (c,))
-                if t == 3:
-                    places(0, (c,))
+            nexthop(t, 0, p, (0, 1, 2), 2 - p)
+        if t == 3:
+            spare[2:2] = [lambda: places(0, (0,)), lambda: places(0, (1, 2))]
         if t == 0:
-            for a in range(0, GH, 160):
-                spare.append(lambda a=a: ts(R("tgi", a, a + 160), R("tg", NV + a, NV + a + 160), 6.0, None, A.mult))
-            for a in range(0, GH, 160):
-                spare.append(lambda a=a: ts(R("gt", 16 + NV + a, 176 + NV + a), R("tgi", a, a + 160), 255, None, A.bitwise_and))
+            for a in range(0, GH, 192):
+                spare.append(lambda a=a: ts(R("tgi", a, a + 192), R("tg", NV + a, NV + a + 192), 6.0, None, A.mult))
+            for a in range(0, GH, 192):
+                spare.append(lambda a=a: ts(R("gt", 16 + NV + a, 208 + NV + a), R("tgi", a, a + 192), 255, None, A.bitwise_and))
             spare.append(lambda: ts(R("at16"), R("ati"), 16.0, None, A.add))
-            spare.append(lambda: ms(R("gt", 0, 16), 0))
-        if t == RO - 2:
-            follow(1)
-            to_list(1, 0, 6)
-        add("X", None, [], [ghost(t + 1)], "arr%d" % t, arrive)
+            iota(R("gt", 0, 16), [[0, 16]], 0)
+        add("X", None, [], [ghost(t + 1)], "arr%d" % t, arrive(t))
 
     t = RO - 1
-    links(t, 1, 0, FIRST)
-    largest(1)
-    nexthop(t - 1, 1, 1, (0,))
+    first(t, 1, True)
+    fill(1)
+    fetch(t, 0, 1, 2, 6)
+    alone(t, 0, 1, 0, 2, (0,))
+    fill(1)
+    alone(t, 0, 1, 0, 2, (1,))
+    spread(0, (2,))
     statics(t, 0, 1)
-    to_list(1, 6, 11)
-    fill(len(spare))
-    fetch(t, 0, 1, 0, 4)
+    match(1, 2, 6)
     largest(0)
-    nexthop(t - 1, 1, 1, (1,))
-    sums_of(1, "sg", 0, 4)
-    source(1, (0,))
-    nexthop(t - 1, 1, 1, (2,))
+    sums_of(1, "sg", 0, 6)
+    spread(0, (3,))
+    sums_of(1, "eq", 0, 6)
+    fill(len(spare))
     for c in range(3):
+        source(1, (c,))
         nexthop(t, 1, 0, (c,))
-        source(1, (c + 1,) if c < 2 else ())
-    match(0, 1, 0, 4)
-    sums_of(1, "eq", 0, 4)
-    to_list(1, 11, 16)
-    links(t, 0, 1, FIRST[1:2])
-    hop(t, 1, True)
-    links(t, 0, 1, FIRST[2:])
+    to_list(1, 4, 8)
+    links(t, 0, 1, (("S", 6, 10), ("S", 10, 14), ("S", 14, 16)))
     act(R("best"), I(window(t), R("src")))
-    for h in range(2):
-        mm(R("pn%d" % h, 0, 192), R("shm"), H("best", h, 192), False, True)
-    for h in range(2):
-        act(H("lo", h, 192), R("pn%d" % h, 0, 192), F.Relu, col(2))
-    decode(1, R("lo"))
+    hop(t, 1, True)
+    decode(0, own(t, 0))
+    mm(R("pa", 0, 384), R("w0"), H("nnc", 1, 384), True, False)
+    mm(R("pa", 0, 384), R("shm"), R("best"), False, True)
+    to_list(1, 8, 16)
+    act(R("lo"), R("pa", 0, 384), F.Relu, col(2))
     largest(1)
-    for c in range(3):
-        nexthop(t, 0, 1, (c,))
-        places(1, (c,))
+    nexthop(t, 0, 1)
     hop(t, 0, True)
-    both(t - 1, 0, cp)
+    places(1, (0,))
     both(t - 1, 1)
+    both(t - 1, 0, cp)
+    places(1, (1, 2))
     follow(2)
+    decode(1, R("lo"))
     for h in range(2):
         act(H("d2", h, 384), H("d1", h, 384), F.Identity, MAGIC + N0, 1.0 / CS)
+    for h in range(2):
         act(H("yp", h, 384), H("d2", h, 384), F.Relu, -MAGIC)
         dma("Y", T.ypath[:, 384 * h:384 * h + 384], H("yp", h, 384))
     ts(R("gt", 16, 16 + NV), R("smi"), 255, None, A.bitwise_and)
-    for a, b in ((0, 30), (30, 48)):
-        for fn, e, x in ((cp, "Y", 0), (act, "S", 48)):
-            fn(R("ys", 16 * (x + a), 16 * (x + b)), I(R("gt"), R("at16", x + a, x + b)))
-            dma(e, T.ysum[:, 16 * (x + a):16 * (x + b)], R("ys", 16 * (x + a), 16 * (x + b)))
+    for fn, a, b in ((cp, 0, 30), (act, 48, 78), (cp, 30, 48), (act, 78, 96)):
+        fn(R("ys", 16 * a, 16 * b), I(R("gt"), R("at16", a, b)))
+        dma("S" if b == 96 else "Y", T.ysum[:, 16 * a:16 * b], R("ys", 16 * a, 16 * b))
 
     seq = {}
     for o in ops:

import math
import numpy as np
from concourse.bass import DstId, RemoteDMATransfer
from concourse.mybir import AluOpType as A, ActivationFunctionType as F

NV, NG, RO, NR = 768, 192, 6, 6
GH = 960
TW = GH + 16 + NV + GH
WIN = 16 + NV + GH
CS = 39.0 / 4096
N0 = 2324
CB = -CS * N0
C0 = 135.0 * 2.0 ** -39
TINY = 2.0 ** -70
MAGIC = 12582912.0
B23 = 8388608.0
NA = 4
STAGES = ((0, 24), (24, 60))
HEAD = 4
PN = ("pa", "pb")
PP = 416

f32, bf, i32, u16, f16 = "float32", "bfloat16", "int32", "uint16", "float16"
SB = {
    "tab": (7 * TW, bf), "pin": (NV, i32), "pe": (NV, bf), "nz": (NV, bf),
    "nbi": (288, i32), "nbh": (288, f16), "l1h": (320, f16), "l1t": (320, f16), "l2": (288, u16),
    "lki": (352, i32), "lkb": (352, bf), "lkt": (352, bf), "lb": (288, bf), "li": (288, i32), "lj": (288, i32),
    "a0": (288, bf), "dn": (6 * 288, bf), "orgv": (48, f32), "orgn": (48, bf), "bc": (144, bf),
    "shi": (60, i32), "sh16": (60, u16), "z0": (120, f32), "zz": (120, f32), "ati": (96, i32), "at16": (96, u16),
    "ki": (4, i32), "kf": (4, f32), "cols": (8, f32),
    "fp": (144, f32), "fq": (160, f32), "fr": (160, f32), "iox": (144, f32), "fo": (128, f32),
    "pm": (288, f16), "qm": (320, f16), "rm": (320, bf), "ib": (128, bf), "ib15": (128, bf), "w0": (128, bf),
    "ip": (128, bf), "wt": (128, bf), "ih": (128, f16), "lkl": (288, bf),
    "beq": (144, bf), "bsg": (144, bf), "bx": (144, f32), "shm": (128, bf), "obn": (128, bf), "upm": (128, bf),
    "nti": (336, i32), "ntc": (672, bf), "n6": (288, i32), "nt": (2 * NA * 144, bf), "bz": (12, f32),
    "nni": (384, i32), "nnc": (NV, bf),
    "v16": (48, f32), "oldp": (60, f32), "r6": (144, f32), "r12": (120, bf),
    "eq": (4608, bf), "sg": (4608, bf), "sc": (288, f32), "si": (24, i32), "sj": (24, i32), "src": (24, u16),
    "hi": (96, i32), "hj": (96, i32), "nh": (288, u16), "best": (384, bf), "neq": (GH, bf),
    "ch": (120, bf), "ci": (120, bf), "be2": (144, bf), "thr": (72, f32), "sl": (60, u16),
    "cz": (WIN, f32), "hh": (WIN, f32), "xx": (2 * WIN, f32), "sm": (2 * NV, f32), "smi": (NV, i32),
    "ee": (48, f32), "ei": (48, i32), "ej": (48, i32), "pl": (48, u16),
    "tg": (NV + GH, bf), "tgi": (GH, i32), "gt": (WIN, i32), "ys": (1536, bf),
    "lo": (384, f32), "d1": (NV, f32), "d2": (NV, f32), "yp": (NV, f32),
}
PS = {"nm": 2048, "pfa": 512, "pfb": 512, "pa": 512, "pb": 512}
SCRATCH = {k: ("psum", [128, v], "float32") for k, v in PS.items()}
SCRATCH.update({k: ("sbuf", [128, v[0]], v[1]) for k, v in SB.items()})
NDMA = 34
SEMAPHORES = ["eV", "eS", "eP", "eG", "sent"] + ["arr%d" % t for t in range(RO - 1)] + ["dm%d" % k for k in range(NDMA)]


def share(eng, ds):
    out, at = {}, 0
    for k, d in enumerate(ds):
        left = len(ds) - k
        n = 1 << int(math.log2((len(eng) - at + left - 1) // left))
        while at + n + (left - 1) > len(eng):
            n //= 2
        out[d] = eng[at:at + n]
        at += n
    return out


ALLH = (9, 9)
OPT = {"solo": (0, 2, 4), "fine": ((90, 122), (122, 136), (136, 144)), "o": 3, "w": (2, 2, 4), "w3": 2, "gaps": (1, 4)}
U = (0, 2, 2, 4, 2)


def calls_of(T, topo, src, t):
    r = T.rank_of(src)
    dst = {d: T.cores[(r + d) % NR] for d in range(1, NR)}
    near = [d for d in dst if dst[d] in topo.cores_of(src)]
    far = [d for d in dst if d not in near]
    order = [(far[0] - 1 + k) % (NR - 1) + 1 for k in range(NR - 1)]
    off = topo.engines(src, dst[far[0]])
    on = [e for e in topo.engines(src, dst[near[0]]) if e not in off]
    second = share(on, near[:2])
    second.update(share(off, far[2:] + near[2:]))
    allh = t >= ALLH[len(far) > 2]
    heads = share(off, (far if OPT.get("four") else far[-2:]) if allh else far[:2])
    if allh:
        heads.update(share(on, near))
    if len(far) == 2 and t >= OPT.get("three", 9):
        first = share(off, far)
        first[order[2]] = on
        return order, [heads if allh else first, first, {order[3]: on, order[4]: off}, {}, {}], ((0, 36), (36, 60))
    extra, last = {}, {}
    if t < OPT.get("split", 0):
        if len(far) == 2:
            extra = share(on, near)
        else:
            last = {near[0]: second.pop(near[0])}
    return order, [heads, share(off, far[:2]), second, extra, last], ((0, 24), (24, 60))


def rank_program(g, core, T, topo):
    r = T.rank_of(core)
    if r is None:
        return
    Q = {"V": g.vector, "S": g.scalar, "P": g.tensor, "G": g, "Y": g.sync}
    ops = []
    wr = {k: np.full(v[0], -1) for k, v in SB.items()}
    rd = {k: [] for k in SB}
    bank = {k: [{} for _ in range(n // 512)] for k, n in PS.items()}
    ndma = [0]

    def R(n, a=0, b=None, s=1):
        return (n, a, SB[n][0] if b is None else b, s)

    def I(win, off):
        return ("*", win, off)

    def ap(x):
        if not isinstance(x, tuple):
            return x
        if x[0] == "*":
            return ap(x[1]).indirect(ap(x[2]))
        return T[x[0]][:, x[1]:x[2]] if x[3] == 1 else T[x[0]][:, x[1]:x[2]:x[3]]

    def add(e, fn, reads, writes, key=None, inc=1):
        me = len(ops)
        deps = set()
        flat = []
        for x in reads:
            if isinstance(x, tuple):
                flat += [x[1], x[2]] if x[0] == "*" else [x]
        touched = [bank[x[0]][b] for x in flat + list(writes) if x[0] in bank for b in range(x[1] // 512, (x[2] - 1) // 512 + 1)]
        for last in touched:
            deps.update(k for q, k in last.items() if q != e)
        for x in flat + list(writes):
            if x[0] not in bank:
                deps.update(int(k) for k in np.unique(wr[x[0]][x[1]:x[2]:x[3]]) if k >= 0)
        for x in writes:
            if x[0] not in bank:
                m = np.zeros(SB[x[0]][0], bool)
                m[x[1]:x[2]:x[3]] = True
                deps.update(k for k, y in rd[x[0]] if m[y[1]:y[2]:y[3]].any())
        for last in touched:
            last[e] = me
        for x in flat:
            if x[0] not in bank:
                rd[x[0]].append((me, x))
        for x in writes:
            if x[0] not in bank:
                wr[x[0]][x[1]:x[2]:x[3]] = me
        ops.append({"e": e, "fn": fn, "deps": deps, "key": key, "inc": inc, "sig": False})

    def ts(out, in0, s1, s2, o0, o1=None):
        if o1 is None:
            add("V", lambda: g.vector.tensor_scalar(ap(out), ap(in0), ap(s1), None, o0), [in0, s1], [out])
        else:
            add("V", lambda: g.vector.tensor_scalar(ap(out), ap(in0), ap(s1), ap(s2), o0, o1), [in0, s1, s2], [out])

    def tt(out, in0, in1, op):
        add("V", lambda: g.vector.tensor_tensor(ap(out), ap(in0), ap(in1), op), [in0, in1], [out])

    def cp(out, in_):
        add("V", lambda: g.vector.tensor_copy(ap(out), ap(in_)), [in_], [out])

    def ms(out, c):
        add("V", lambda: g.vector.memset(ap(out), c), [], [out])

    def scan(out, d0, d1, init, o0, o1):
        add("V", lambda: g.vector.tensor_tensor_scan(ap(out), ap(d0), ap(d1), init, o0, o1), [d0, d1], [out])

    def vt(out, in_):
        add("V", lambda: g.vector.transpose(ap(out), ap(in_)), [in_], [out])

    def act(out, in_, fn=F.Copy, bias=0.0, scale=1.0):
        add("S", lambda: g.scalar.activation(ap(out), ap(in_), fn, bias=ap(bias), scale=scale), [in_, bias], [out])

    def mm(out, lhs, rhs, start, stop):
        add("P", lambda: g.tensor.matmul(ap(out), ap(lhs), ap(rhs), start, stop), [lhs, rhs], [out])

    def iota(out, pat, base, cm=0):
        if SB[out[0]][1] == i32:
            add("G", lambda: g.iota(ap(out), pat, base, cm), [], [out])
        else:
            add("G", lambda: g.iota(ap(out), pat, base, cm, allow_small_or_imprecise_dtypes=True), [], [out])

    def sel(x, pat, op, fill, base):
        add("G", lambda: g.affine_select(ap(x), ap(x), pat, op, fill, base, 1), [x], [x])

    def dma(e, out, in_, accum=False, after=None):
        key = "dm%d" % ndma[0]
        ndma[0] += 1
        reads = [x for x in (in_, after) if isinstance(x, tuple)]
        writes = [out] if isinstance(out, tuple) else []
        if accum:
            add(e, lambda: g.dma_start(ap(out), ap(in_), accum_op=A.add), reads + writes, writes, key, 16)
        else:
            add(e, lambda: Q[e].dma_start(ap(out), ap(in_)), reads, writes, key, 16)

    def mark(out):
        key = "dm%d" % ndma[0]
        ndma[0] += 1
        in_ = R("cz", out[1], out[2])
        add("G", lambda: g.dma_start(T[out[0]][0:128:16, out[1]:out[2]], T.cz[0:128:16, out[1]:out[2]], accum_op=A.add),
            [in_, out], [out], key, 16)

    def keep(t):
        x = t * TW + GH
        dma("Y", R("tab", x + TW, x + TW + 16 + NV), R("tab", x, x + 16 + NV), after=ghost(t))

    def old(t, a=0, b=GH):
        return R("tab", t * TW + a, t * TW + b)

    def own(t, p, a=0, b=384):
        x = t * TW + GH + 16 + p
        return R("tab", x + 2 * a, x + 2 * b - 1, 2)

    def ghost(t, a=0, b=GH):
        return R("tab", t * TW + GH + 16 + NV + a, t * TW + GH + 16 + NV + b)

    def window(t):
        return R("tab", t * TW + GH, (t + 1) * TW)

    def H(n, p, w, u=None):
        return R(n, w * p, w * p + (w if u is None else u))

    def col(k):
        return R("cols", k, k + 1)

    K, KG, KL = R("kf", 0, 1), R("kf", 1, 2), R("kf", 2, 3)
    O0 = GH + 16
    order = calls_of(T, topo, core, 0)[0]

    def pads(a, b, mark):
        if mark:
            ts(R("tab", a * TW + GH, (b - 1) * TW + GH + 1, TW), R("iox", 0, b - a), 0.0, col(0), A.mult, A.add)
        else:
            for t in range(a, b):
                ms(R("tab", t * TW + GH, t * TW + GH + 16), 0.0)

    def list1(p):
        for i in range(6):
            for h in range(2):
                x = 144 * p + 16 - 8 * h
                mm(R(("pfb", "pfa")[p], i, 144, 6), R("pm", x, x + 128), R("nbh", 48 * i + h, 48 * i + 48, 2), h == 0, h == 1)

    def list2(p):
        for b in range(9):
            for c in range(2):
                q = 160 * (b % 2) + 32 - 16 * c
                x = 160 * p + 32 * (b // 2) + 16 * c
                mm(R(("pfa", "pfb")[p], 340 + b, 484, 9), R("qm", q, q + 128), R("l1t", x, x + 16), c == 0, c == 1)

    def list3(p):
        outs = [(R("pfb", 144 * p + e, 144 * p + 144, 9), 32 * e, 16) for e in range(9)]
        outs += [(R("pfb", 288 + 24 * p, 304 + 24 * p), 288, 16), (R("pfb", 304 + 24 * p, 312 + 24 * p), 328, 8)]
        for o, x, n in outs:
            for c in range(2):
                q = 160 * p + 32 - 16 * c
                mm(o, R("rm", q, q + 128), R("lkt", x + 16 * c, x + 16 * c + n), c == 0, c == 1)

    def encode():
        for h in range(2):
            act(H("nz", h, 384), H("pin", h, 384), F.Sign)
            mm(R(PN[h], 0, 384), R("wt"), H("nz", h, 384), True, True)
        for h in range(2):
            act(H("pe", h, 384), H("pin", h, 384), F.Exp, CB, CS)

    def down(t, a=0, b=288):
        act(R("dn", 288 * t + a, 288 * t + b), R("lb", a, b), F.Relu, B23 * 16 * (t + 1), -B23)

    left = {}

    def score(k, out, lhs, rhs):
        n = left.get(k, 0)
        mm(out, lhs, rhs, n == 0, n == 35)
        left[k] = (n + 1) % 36

    def statics(t, p, k):
        fb = R(("pfa", "pfb")[k], 0, 144)
        score(k, fb, R("ib"), R("bc"))
        score(k, fb, R("ib"), H("a0", p, 144))
        score(k, fb, R("ib"), R("dn", 288 * t + 144 * p, 288 * t + 144 * p + 144))
        score(k, fb, R("ih"), H("l1h", p, 160, 144))

    def prefs(p, step):
        n = PN[1 - p]
        x = R(n, 264, 408)
        if step == 0:
            cp(H("lkl", p, 144), R("pfb", 144 * p, 144 * p + 144))
            ts(H("orgn", p, 24), R("pfb", 288 + 24 * p, 312 + 24 * p), -256.0, None, A.mult)
        elif step == 1:
            ts(H("orgv", p, 24), R("pfb", 288 + 24 * p, 312 + 24 * p), B23 + 2.0, None, A.mult)
            for i in range(6):
                mm(R(n, 264 + i, 408, 6), R("ib"), R("lkl", 144 * p + 24 * i, 144 * p + 24 * i + 24), True, False)
                mm(R(n, 264 + i, 408, 6), R("ib"), H("orgn", p, 24), False, True)
        elif step == 2:
            ts(H("li", p, 144), x, -1.0, None, A.mult)
            act(H("dn", p, 144), x, F.Relu, 16 * B23, B23)
            ts(R(("ih", "ip")[p]), R("iox", 15, 143), K, None, A.is_equal)
            ts(H("lj", p, 144), H("li", p, 144), 15, None, A.bitwise_and)
            ts(H("a0", p, 144), H("lj", p, 144), -524288.0, None, A.mult)
        else:
            act(H("lb", p, 144), x, F.Copy, 0.0, -1.0)

    def sums_of(k, n, a, b):
        w = {"sg": "bsg", "eq": "beq"}[n]
        for m in range(a, b):
            z = 2304 * k + 144 * m
            score(k, R(("pfa", "pfb")[k], 0, 144), R(w, 15 - m, 143 - m), R(n, z, z + 144))

    def fetch(t, p, k, a, b):
        act(R("sg", 2304 * k + 144 * a, 2304 * k + 144 * b), I(window(t), R("l2", 144 * p + 9 * a, 144 * p + 9 * b)))

    def match(k, a, b):
        x, y = 2304 * k + 144 * a, 2304 * k + 144 * b
        tt(R("eq", x, y), R("sg", x, y), R("nm", 144 * (a - 2), 144 * (b - 2)) if a > 1 else R(PN[a], 264, 408), A.is_equal)

    def spare_names(p, m):
        z = 144 * (NA * p + m)
        mm(R(PN[m], 264, 408), R("ib15"), R("nt", z, z + 144), True, True)

    def spread(p, banks=range(4)):
        for b in banks:
            for i in range(6):
                x, y = (512 * b - i + 5) // 6, min(336, (512 * b + 511 - i) // 6 + 1)
                mm(R("nm", 6 * x + i, 6 * y + i - 5, 6), R("ib15"), R("ntc", 336 * p + x, 336 * p + y), True, True)

    def sixfold(p, a):
        z = 144 * (NA * p + a)
        act(R("nt", z, z + 288), R("n6"), F.Exp, R("bz", 2 * a + p, 2 * a + p + 1), CS)

    def alone(t, p, k, a, b, steps=(0, 1)):
        x, y = 2304 * k + 144 * a, 2304 * k + 144 * b
        z = NA * 144 * p
        if 0 in steps:
            tt(R("sg", x, y), I(window(t), R("l2", 144 * p + 9 * a, 144 * p + 9 * b)), R("nt", z + 144 * a, z + 144 * b), A.subtract)
        if 1 in steps:
            ts(R("eq", x, y), R("sg", x, y), 0.0, None, A.is_equal)

    def links(t, p, k, plan):
        for e, a, b in plan:
            if e == "A":
                alone(t, p, k, a, b)
                sums_of(k, "sg", a, b)
            else:
                fetch(t, p, k, a, b)
                sums_of(k, "sg", a, b)
                match(k, a, b)
            sums_of(k, "eq", a, b)

    def first(t, p, swap=False):
        for a, b, c, d in ((0, 2, 4, 6), (2, 4, 6, 10)):
            fetch(t, p, 0, c, d)
            alone(t, p, 0, a, b, (0,))
            sums_of(0, "sg", a, b)
            sums_of(0, "sg", c, d)
            match(0, c, d)
            alone(t, p, 0, a, b, (1,))
            sums_of(0, "eq", c, d)
            sums_of(0, "eq", a, b)
            if swap:
                spread(1 - p, (a // 2,))
        if swap or not OPT.get("fine"):
            links(t, p, 0, (("S", 10, 14), ("S", 14, 16)))
            return
        for a, b in OPT["fine"]:
            act(R("sg", 16 * a, 16 * b), I(window(t), R("l2", 144 * p + a, 144 * p + b)))
            sums_of(0, "sg", a // 9, b // 9)
            if a > 90:
                sums_of(0, "eq", z // 9, a // 9)
            tt(R("eq", 16 * a, 16 * b), R("sg", 16 * a, 16 * b), R("nm", 16 * a - 288, 16 * b - 288), A.is_equal)
            z = a
        sums_of(0, "eq", z // 9, 16)

    def largest(k):
        scan(H("sc", k, 144), R("r6"), R(("pfa", "pfb")[k], 0, 144), 0.0, A.mult, A.max)

    def source(p, steps=(0, 1, 2)):
        for s in steps:
            if s == 0:
                tt(R("si"), R("sc", 5, 144, 6), H("orgv", p, 24), A.max)
            elif s == 1:
                ts(R("sj"), R("si"), 2047, None, A.bitwise_and)
            else:
                cp(R("src"), R("sj"))

    def nexthop(t, p, k, steps=(0, 1, 2), n=1):
        z = 2 * (t & 1) + p
        for s in steps:
            if s == 0:
                tt(H("hi", z, 24, 24 * n), R("sc", 144 * k + 5, 144 * (k + n), 6), H("v16", p, 24, 24 * n), A.max)
            elif s == 1:
                ts(H("hj", z, 24, 24 * n), H("hi", z, 24, 24 * n), 2047, None, A.bitwise_and)
            else:
                cp(H("nh", 2 * t + p, 24, 24 * n), H("hj", z, 24, 24 * n))

    def names(p):
        for h in range(2):
            mm(R(PN[h], 0, 192), R("w0"), R("nnc", 384 * p + 192 * h, 384 * p + 192 * h + 192), True, False)

    spare = []

    def fill(n):
        for _ in range(min(n, len(spare))):
            spare.pop(0)()

    def winner(t, out):
        cp(H("best", 0, 192), I(window(t), R("src", 0, 12)))
        act(H("best", 1, 192), I(window(t), R("src", 12, 24)))
        for h in range(2):
            mm(R(PN[h], 0, 192), R("shm"), H("best", h, 192), False, True)
        fill(1)
        ts(out(0, 192), R("pa", 0, 192), col(2), 0.0, A.add, A.max)
        act(out(192, 384), R("pb", 0, 192), F.Relu, col(2))
        fill(1)

    stages = list(calls_of(T, topo, core, 0)[2])

    def candidates():
        for s, (a, b) in enumerate(stages):
            act(R(PN[s], PP + 1, PP + 2 * (b - a), 2), R("oldp", a, b), F.Identity, col(3))

    def shown_in(t):
        return R("tab", (t + 1) * TW + GH, (t + 1) * TW + GH + 16 + NV)

    def differ(t, a, b):
        tt(R("neq", 16 * a, 16 * b), I(R("tab", (t + 1) * TW + GH, (t + 1) * TW + GH + 16 + NV), R("sh16", a, b)),
           old(t + 1, 16 * a, 16 * b), A.not_equal)

    def count(s, step, between=None):
        a, b = stages[s]
        pc = PN[s]
        if step == 0:
            for m in range(8):
                mm(R(pc, 192, 192 + 2 * (b - a)), R("be2", 15 - m, 143 - m), R("neq", 16 * a + m, 16 * b, 8), m == 0, m == 7)
        elif step == 1:
            tt(R("ch", 2 * a, 2 * b), R(pc, 192, 192 + 2 * (b - a)), R("thr", 0, 2 * (b - a)), A.is_lt)
        elif step == 2:
            scan(R("ci", 2 * a, 2 * b), R("r12", 2 * a, 2 * b), R("ch", 2 * a, 2 * b), 1.0, A.min, A.add)
            for h in range(2):
                mm(R(pc, PP, PP + 2 * (b - a), 2), R("upm"), R("ch", 2 * a + h, 2 * b, 2), h == 0, False)
            if between:
                between()
            mm(R(pc, PP, PP + 2 * (b - a), 2), R("obn"), R("ci", 2 * a + 1, 2 * b, 2), False, True)
        elif step == 3:
            scan(R("zz", 2 * a, 2 * b), R("z0", 2 * a, 2 * b), R(pc, PP, PP + 2 * (b - a)), 0.0, A.min, A.max)
        else:
            cp(R("sl", a, b), R("zz", 2 * a + 1, 2 * b, 2))

    def nh(t, p):
        return H("nh", 2 * t + p, 24)

    def hop(t, p, on_vector=False):
        out = R("xx", 16 + p, 16 + NV, 2)
        if on_vector:
            tt(out, I(R("hh"), nh(t, p)), R("tg", p, NV, 2), A.add)
        else:
            act(out, I(R("hh"), nh(t, p)))

    def sums(j):
        return (R("sm", 0, NV), R("sm", NV, 2 * NV), R("smi"))[j]

    def both(t, p, fn=act):
        out = R("sm", p, NV, 2) if t == 0 else R("xx", WIN + 16 + p, WIN + 16 + NV, 2)
        fn(out, I(H("xx", 0, WIN), nh(t, p)))

    def follow(j):
        tt(sums(j), I(H("xx", 1, WIN), R("pl")), sums(j - 1), A.add)

    def to_list(j, a=0, b=16):
        s = sums(j)
        for m in range(a, b):
            mm(R(("pfa", "pb")[j], 192, 240), R("bx", 15 - m, 143 - m), R(s[0], s[1] + m, s[2], 16), m == 0, m == 15)

    def places(j, steps=(0, 1, 2)):
        for s in steps:
            if s == 0:
                if j == 0:
                    cp(R("ei"), R("pfa", 192, 240))
                    cp(R("ee"), R("pfa", 192, 240))
                else:
                    tt(R("ei"), R("pb", 192, 240), R("ee"), A.subtract)
            elif s == 1:
                ts(R("ej"), R("ei"), 10, None, A.arith_shift_right)
            else:
                cp(R("pl"), R("ej"))

    def decode(p, in_):
        act(R("d1", p, NV, 2), in_, F.Ln, 2.0 ** -60)

    sent = [0]

    def send(t, c, share_v=4):
        pieces = []
        calls = calls_of(T, topo, core, t)[1]
        for j, d in enumerate(order):
            if d in calls[c]:
                pieces.append((j, d, 0, HEAD) if c in (0, 3) else (j, d, HEAD if d in calls[0] or d in calls[3] else 0, 12))
        if not pieces:
            return
        runs = []
        for j, d, a, b in pieces:
            for x in range(12 * j + a, 12 * j + b, 2):
                runs.append(x)
        cut = 0 if c in (0, 3) else len(runs) * share_v // 8
        for fn, mine in ((cp, runs[:cut]), (act, runs[cut:])):
            at = 0
            for k in range(1, len(mine) + 1):
                if k == len(mine) or mine[k] != mine[k - 1] + 2:
                    a, b = mine[at], mine[k - 1] + 2
                    if c in (0, 3):
                        src = I(R("tab", (t + 1) * TW + GH, (t + 1) * TW + GH + 16 + NV), R("sh16", a, b))
                    else:
                        src = I(R("tab", (t + 1) * TW, (t + 1) * TW + GH + 16 + NV), R("sl", a, b))
                    fn(old(t + 2, 16 * a, 16 * b), src)
                    at = k
        trs, reads = [], []
        for j, d, a, b in pieces:
            rid, pid = topo.addr(T.cores[(r + d) % NR], core)
            reads.append(old(t + 2, NG * j + 16 * a, NG * j + 16 * b))
            trs.append(RemoteDMATransfer(
                dst_ids=[DstId(rid=rid, pnc=pid)], dma_engine_mask=sum(1 << e for e in calls[c][d]),
                remote_sem=T.sem["arr%d" % t], src=ap(reads[-1]),
                dst=ap(ghost(t + 1, NG * (d - 1) + 16 * a, NG * (d - 1) + 16 * b))))
            sent[0] += len(calls[c][d])
        add("G", lambda: g.remote_dma_fused(trs, local_sem=T.sem.sent), reads, [], "remote", 0)

    def arrive(t):
        return sum(len(mk[d]) for d in range(1, NR) for mk in calls_of(T, topo, T.cores[(r - d) % NR], t)[1] if d in mk)

    turn = 12 * (order[0] - 1)
    dma("S", R("nbi"), T.nb[:])
    dma("Y", R("pin", 0, 384), T.path0[:, 0:384])
    dma("Y", R("pin", 384, NV), T.path0[:, 384:NV])
    dma("Y", R("lki", 0, 288), T.lk[:])
    dma("Y", R("lki", 288, 320), T.org[:, 0:512])
    dma("Y", R("lki", 320, 352), T.org[:, 256:NV])
    dma("Y", R("shi", 0, 60 - turn), T.shown[:, turn:60])
    if turn:
        dma("Y", R("shi", 60 - turn, 60), T.shown[:, 0:turn])
    iota(R("nti", 0, 48), [[2, 2], [32, 24]], r * NV + 5)
    iota(R("ki", 0, 1), [[1, 1]], 0, 1)
    iota(R("iox"), [[1, 144]], -15)
    iota(R("fp"), [[16, 9], [1000, 2], [2, 8]], -16)
    iota(R("nti", 48, 336), [[2, 12], [32, 24]], r * NV + 9)
    iota(R("fq"), [[32, 5], [1000, 2], [1, 16]], -32)
    act(R("ntc", 0, 48), R("nti", 0, 48), F.Exp, CB, CS)
    act(R("ntc", 48, 336), R("nti", 48, 336), F.Exp, CB, CS)
    ms(ghost(0), 0.0)
    ts(R("ki", 1, 2), R("ki", 0, 1), 112, None, A.bitwise_and)
    ts(R("ki", 2, 3), R("ki", 0, 1), 15, None, A.bitwise_and)
    ms(R("tab", GH, GH + 16), 0.0)
    cp(R("kf", 0, 3), R("ki", 0, 3))
    dma("Y", old(1), ghost(0))
    dma("Y", R("tg"), T.toll[:])
    dma("Y", R("ati"), T.at0[:])
    ms(R("l1h", 144, 160), 0.0)
    ts(col(1), KL, 15.0, None, A.not_equal)
    ts(col(0), KL, 15.0, -2.0 ** 40, A.is_equal, A.mult)
    ts(R("ib15"), R("iox", 15, 143), K, col(1), A.is_equal, A.mult)
    ts(col(5), KL, 15.0, -16384.0 / TINY, A.is_equal, A.mult)
    ts(R("wt"), R("iox", 0, 128), KG, TINY, A.is_equal, A.mult)
    ts(H("pm", 0, 144), R("fp"), 0.0, K, A.add, A.is_equal)
    ts(col(6), KL, 15.0, -200.0, A.is_equal, A.mult)
    sel(R("wt"), [[-1, 128]], A.not_equal, 2.0 ** 40, 0)
    iota(R("fr"), [[32, 5], [1000, 2], [2, 16]], -32)
    iota(R("n6"), [[2, 2], [32, 24], [0, 6]], r * NV + 1 - N0)
    iota(R("bc"), [[0, 24], [2048, 6]], -135 * 2048)
    ts(R("bsg"), R("iox"), KG, col(5), A.is_equal, A.mult)
    ts(R("bz"), R("iox", 15, 27), CS, col(6), A.mult, A.add)
    ts(R("beq"), R("iox"), KG, -B23, A.is_equal, A.mult)
    ts(R("ib"), R("iox", 15, 143), K, -1.0, A.is_equal, A.mult)
    ts(R("nbh"), R("nbi"), 16.0, None, A.add)
    spread(0, (0, 1))
    list1(0)
    for b in range(2):
        ts(H("qm", b, 160), R("fq"), 16.0 * b, K, A.add, A.is_equal)
    cp(R("tab", GH, GH + 1), col(0))
    ms(R("shm"), 0.0)
    encode()
    cp(R("l1h", 0, 144), R("pfb", 0, 144))
    ts(H("rm", 0, 160), R("fr"), 0.0, K, A.add, A.is_equal)
    vt(R("l1t", 0, 160), R("l1h", 0, 160))
    list2(0)
    spread(0, (2, 3))
    for h in range(2):
        tt(R("tab", O0 + 384 * h, O0 + 384 * h + 384), R(PN[h], 0, 384), H("pe", h, 384), A.min)
    act(R("lkb"), R("lki"))
    sixfold(0, 0)
    cp(R("l2", 0, 144), R("pfa", 340, 484))
    keep(0)
    vt(R("lkt"), R("lkb"))
    list3(0)
    iota(R("r6"), [[0, 144]], 1)
    iota(R("nni"), [[2, 384]], r * NV + 1)
    iota(R("r6", 0, 144, 6), [[0, 24]], 0)
    sel(R("shm"), [[-1, 128]], A.not_equal, 1.0, 1)
    iota(R("fo"), [[16, 8], [0, 16]], 0)
    sel(R("shm", 0, 128, 16), [[-16, 8]], A.not_equal, 0.0, 1)
    iota(R("oldp"), [[16, 60]], 0, 1)
    sel(R("shm", 0, 128, 16), [[-16, 8]], A.not_equal, 1.0, -15)
    sel(R("shm", 15, 128, 16), [[-16, 8]], A.not_equal, 1.0, -15)
    iota(R("thr"), [[0, 36], [1, 2]], 0)
    iota(R("r12"), [[0, 5], [10, 24]], 1)
    iota(R("z0", 0, 120, 2), [[0, 60]], -int(B23))
    iota(R("v16"), [[1, 2], [32, 24]], 16, 2)
    dma("G", R("hh", 16, WIN), T.toll[:])

    FIRST = (("A", 0, 4), ("S", 4, 8), ("S", 8, 12), ("S", 12, 14), ("S", 14, 16))
    for t in range(RO - 1):
        p, q = t & 1, 1 - (t & 1)
        if t == 0:
            fetch(0, 0, 0, 2, 6)
            alone(0, 0, 0, 0, 2, (0,))
            ts(col(4), KL, 0.0, None, A.is_equal)
            alone(0, 0, 0, 0, 2, (1,))
            prefs(0, 0)
            sums_of(0, "sg", 0, 6)
            prefs(0, 1)
            match(0, 2, 6)
            fetch(0, 0, 0, 6, 10)
            sums_of(0, "eq", 0, 6)
            fetch(0, 0, 0, 10, 14)
            fetch(0, 0, 0, 14, 16)
            sums_of(0, "sg", 6, 10)
            prefs(0, 2)
            match(0, 6, 10)
            sums_of(0, "sg", 10, 14)
            sums_of(0, "eq", 6, 10)
            sums_of(0, "sg", 14, 16)
            statics(0, 0, 0)
            match(0, 10, 14)
            sums_of(0, "eq", 10, 14)
            match(0, 14, 16)
            sums_of(0, "eq", 14, 16)
            prefs(0, 3)
            act(R("nnc", 0, 384), R("nni"), F.Exp, CB, CS)
            ts(R("w0"), R("iox", 15, 143), K, col(4), A.is_equal, A.mult)
            ts(R("upm"), R("fo"), KG, 4096.0, A.is_equal, A.mult)
            names(0)
            sel(R("upm"), [[-1, 128]], A.is_gt, 0.0, 0)
            sel(R("upm"), [[-1, 128]], A.not_equal, 80.5 * 4096, 0)
        else:
            keep(t)
            if t == 1:
                mark(R("hh", 16, WIN))
            if t == 2:
                mark(R("xx", 16 + NV, WIN))
            if t == 3:
                dma("Y", R("xx", WIN + 16 + NV, 2 * WIN), R("xx", 16 + NV, WIN), after=ghost(t))
            first(t, p)
            if p == 0:
                hop(t - 1, 0)
                dma("G", R("xx", 16, 16 + NV), T.toll[:, 0:NV], accum=True)
            if p == 1:
                down(t + 1)
        u = OPT.get("u", U)[t]
        if u:
            fetch(t, q, 1, 2, u + 2)
        if t == 0:
            largest(0)
            ts(H("pm", 1, 144), R("fp"), 1.0, K, A.add, A.is_equal)
            list1(1)
            source(0, (0,))
            ts(col(3), KG, -1.0, None, A.mult)
            act(R("ntc", 336, 672), R("nti"), F.Exp, CB + CS, CS)
            act(R("z0", 1, 120, 2), R("shi"), F.Identity, float(GH + 16))
            sixfold(1, 0)
            act(R("nnc", 384, NV), R("nni"), F.Exp, CB + CS, CS)
            source(0, (1,))
            ts(col(2), KL, 15.0, TINY, A.is_equal, A.mult)
            source(0, (2,))
            ts(R("sh16"), R("shi"), 16.0, None, A.add)
            spare.append(lambda: (ms(R("l1h", 304, 320), 0.0), cp(R("l1h", 160, 304), R("pfa", 0, 144)),
                                  ts(col(7), KL, 8.0, None, A.is_ge)))
            spare.append(lambda: vt(R("l1t", 160, 320), R("l1h", 160, 320)))
            winner(0, lambda a, b: own(1, 0, a, b))
            list2(1)
            send(0, 0)
            send(0, 3)
            act(R("neq", 576, GH), I(shown_in(0), R("sh16", 36, 60)), F.Abs)
            candidates()
            differ(0, 0, 24)
            tt(R("be2", 8, 144), R("beq", 8, 144), R("beq", 0, 136), A.add)
            ts(R("thr"), R("thr"), col(7), -1e29, A.not_equal, A.mult)
            differ(0, 24, 36)
            count(0, 0)
            sixfold(1, 2)
            cp(R("l2", 144, 288), R("pfb", 340, 484))
            count(1, 0)
            fetch(0, 1, 1, 2, 4)
            count(0, 1)
            ts(R("obn"), R("fo"), KG, -4096.0, A.is_equal, A.mult)
            count(0, 2)
            count(1, 1)
            ts(H("rm", 1, 160), R("fr"), 1.0, K, A.add, A.is_equal)
            count(0, 3)
            count(1, 2)
            count(0, 4)
            list3(1)
            send(0, 1)
            count(1, 3)
            ts(R("v16"), R("v16"), KG, KG, A.subtract, A.subtract)
            count(1, 4)
            send(0, 2)
            send(0, 4)
            spread(1)
            prefs(1, 0)
            prefs(1, 1)
            fetch(0, 1, 1, 4, 8)
            fetch(0, 1, 1, 8, 14)
            u = 4
        else:
            if t == 1:
                sixfold(0, 2)
            fill(2)
            largest(0)
            spread(q, (0, 1, 2))
            source(p, (0, 1))
            nexthop(t, p, 0, (0,) if p else ())
            source(p, (2,))
            winner(t, lambda a, b: own(t + 1, p, a, b))
            spread(q, (3,))
            got = u + 2
            send(t, 0)
            if stages != list(calls_of(T, topo, core, t)[2]):
                stages[:] = calls_of(T, topo, core, t)[2]
                candidates()
            cut = OPT.get("cut", 48)
            w1, w2, sv = OPT.get("w", (0, 2, 0))
            act(old(t + 2, 16 * cut, GH), I(shown_in(t), R("sh16", cut, 60)))
            differ(t, 0, stages[0][1])
            mm(R("pfb", 0, GH - 16 * cut), R("ib"), old(t + 1, 16 * cut, GH), True, False)
            if t == 3:
                to_list(0, 0, 6)
            count(0, 0)
            mm(R("pfb", 0, GH - 16 * cut), R("ip"), old(t + 2, 16 * cut, GH), False, True)
            if t == 3:
                to_list(0, 6, 8)
            if w1:
                fetch(t, q, 1, got, got + w1)
                got += w1
            act(R("neq", 16 * cut, GH), R("pfb", 0, GH - 16 * cut), F.Abs)
            if w2:
                fetch(t, q, 1, got, got + w2)
                got += w2
            differ(t, stages[0][1], cut)
            done = [2]

            def gap(k):
                if k in OPT.get("gaps", ()) and done[0] < got:
                    match(1, done[0], done[0] + 1)
                    done[0] += 1
            count(0, 1)
            nexthop(t, p, 0, (1,) if p else ())
            if not p:
                gap(0)
            if OPT.get("o") == 4:
                count(0, 2, lambda: count(1, 0))
                gap(1)
                count(1, 1)
                count(0, 3)
                count(1, 2)
                count(0, 4)
                statics(t, q, 1)
                sums_of(1, "sg", 2, got)
                send(t, 1, sv)
            else:
                count(0, 2)
                count(1, 0)
                if t == 3:
                    to_list(0, 8, 10)
                gap(1)
                count(0, 3)
                gap(2)
                count(0, 4)
                if OPT.get("o") == 2:
                    send(t, 1, sv)
                count(1, 1)
                if OPT.get("o") == 3:
                    send(t, 1, sv)
                else:
                    gap(3)
                count(1, 2)
                statics(t, q, 1)
                sums_of(1, "sg", 2, got)
                if OPT.get("o") not in (2, 3):
                    send(t, 1, sv)
                else:
                    gap(4)
            if OPT.get("w3"):
                fetch(t, q, 1, got, got + OPT["w3"])
            count(1, 3)
            nexthop(t, p, 0, (2,) if p else ())
            if not p:
                gap(5)
            count(1, 4)
            send(t, 2)
            if OPT.get("w3"):
                sums_of(1, "sg", got, got + OPT["w3"])
                got += OPT["w3"]
            done = done[0]
            sums_of(1, "eq", 2, done)
        if t == 0:
            iota(R("cz", 16, WIN), [[1024, NV + GH]], 1024 * 16)
            match(1, 2, 8)
            prefs(1, 2)
            prefs(1, 3)
            statics(t, q, 1)
            sums_of(1, "sg", 2, 14)
            sums_of(1, "eq", 2, 8)
            done, got = 8, 14
        solo = t in OPT.get("solo", ())
        runs = [(done, got)] + [(a, min(a + 4, 16)) for a in range(got, 16, 4)]
        for n, (a, b) in enumerate(runs):
            if n:
                fetch(t, q, 1, a, b)
                sums_of(1, "sg", a, b)
            if t == 3 and n == 0:
                to_list(0, 10, 16)
            if t == 4 and n == len(runs) - 1:
                to_list(1, 0, 4)
            if a < b:
                match(1, a, b)
                sums_of(1, "eq", a, b)
            if n == 0:
                if solo:
                    links(t, q, 1, (("A", 0, 2),))
                else:
                    for m in range(2):
                        spare_names(q, m)
            if t == 1 and n < 2:
                ts(R("xx", 16 + NV + 480 * n, 496 + NV + 480 * n), R("tg", NV + 480 * n, NV + 480 * n + 480), 2.0, None, A.mult)
            if t == 4 and n == 0:
                both(2, 0)
                both(2, 1)
                follow(1)
        if not solo:
            fetch(t, q, 1, 0, 2)
            sums_of(1, "sg", 0, 2)
            for m in range(2):
                match(1, m, m + 1)
            sums_of(1, "eq", 0, 2)
        if t == 0:
            down(1)
        if t == 0:
            iota(R("hh", 0, 16), [[0, 16]], 0)
        if t == 1:
            for x in (R("xx", 0, 16), R("xx", WIN, WIN + 16), R("bx")):
                iota(x, [[0, x[2] - x[1]]], 0)
            sel(R("bx", 15, 143, 16), [[-16, 8]], A.not_equal, 1.0, 0)
        if p == 1:
            hop(t, 1)
        elif t == 2:
            both(0, 0)
            both(0, 1)
        statics(t + 1, q, 0)
        if t < RO - 2:
            names(q)
        if p == 1:
            down(t + 2)
        if t in OPT.get("late", (0, 4)):
            spare[0:0] = [lambda: largest(1)] + [lambda c=c, t=t, p=p: nexthop(t, 0, p, (c,), 2 - p) for c in range(3)]
        else:
            largest(1)
            nexthop(t, 0, p, (0, 1, 2), 2 - p)
        if t == 3:
            spare[2:2] = [lambda: places(0, (0,)), lambda: places(0, (1, 2))]
        if t == 0:
            for a in range(0, GH, 192):
                spare.append(lambda a=a: ts(R("tgi", a, a + 192), R("tg", NV + a, NV + a + 192), 6.0, None, A.mult))
            for a in range(0, GH, 192):
                spare.append(lambda a=a: ts(R("gt", 16 + NV + a, 208 + NV + a), R("tgi", a, a + 192), 255, None, A.bitwise_and))
            spare.append(lambda: ts(R("at16"), R("ati"), 16.0, None, A.add))
            iota(R("gt", 0, 16), [[0, 16]], 0)
        add("X", None, [], [ghost(t + 1)], "arr%d" % t, arrive(t))

    t = RO - 1
    first(t, 1, True)
    fill(1)
    fetch(t, 0, 1, 2, 6)
    alone(t, 0, 1, 0, 2, (0,))
    fill(1)
    alone(t, 0, 1, 0, 2, (1,))
    spread(0, (2,))
    statics(t, 0, 1)
    match(1, 2, 6)
    largest(0)
    sums_of(1, "sg", 0, 6)
    spread(0, (3,))
    sums_of(1, "eq", 0, 6)
    fill(len(spare))
    for c in range(3):
        source(1, (c,))
        nexthop(t, 1, 0, (c,))
    to_list(1, 4, 8)
    links(t, 0, 1, (("S", 6, 10), ("S", 10, 14), ("S", 14, 16)))
    act(R("best"), I(window(t), R("src")))
    hop(t, 1, True)
    decode(0, own(t, 0))
    mm(R("pa", 0, 384), R("w0"), H("nnc", 1, 384), True, False)
    mm(R("pa", 0, 384), R("shm"), R("best"), False, True)
    to_list(1, 8, 16)
    act(R("lo"), R("pa", 0, 384), F.Relu, col(2))
    largest(1)
    nexthop(t, 0, 1)
    hop(t, 0, True)
    places(1, (0,))
    both(t - 1, 1)
    both(t - 1, 0, cp)
    places(1, (1, 2))
    follow(2)
    decode(1, R("lo"))
    for h in range(2):
        act(H("d2", h, 384), H("d1", h, 384), F.Identity, MAGIC + N0, 1.0 / CS)
    for h in range(2):
        act(H("yp", h, 384), H("d2", h, 384), F.Relu, -MAGIC)
        dma("Y", T.ypath[:, 384 * h:384 * h + 384], H("yp", h, 384))
    ts(R("gt", 16, 16 + NV), R("smi"), 255, None, A.bitwise_and)
    for fn, a, b in ((cp, 0, 30), (act, 48, 78), (cp, 30, 48), (act, 78, 96)):
        fn(R("ys", 16 * a, 16 * b), I(R("gt"), R("at16", a, b)))
        dma("S" if b == 96 else "Y", T.ysum[:, 16 * a:16 * b], R("ys", 16 * a, 16 * b))

    seq = {}
    for o in ops:
        if o["key"] is None:
            seq[o["e"]] = seq.get(o["e"], 0) + 1
            o["at"] = ("e" + o["e"], seq[o["e"]])
        else:
            o["at"] = (o["key"], 1)
    know = {e: {} for e in Q}
    for o in ops:
        o["waits"] = []
        if o["e"] == "X":
            o["clock"] = {o["key"]: 1}
            continue
        kn = know[o["e"]]
        for k in sorted(o["deps"], reverse=True):
            d = ops[k]
            if d["key"] == "remote" or kn.get(d["at"][0], 0) >= d["at"][1]:
                continue
            o["waits"].append(k)
            d["sig"] = True
            for s, v in d["clock"].items():
                kn[s] = max(kn.get(s, 0), v)
        o["clock"] = dict(kn)
        o["clock"][o["at"][0]] = o["at"][1]
    cnt = {}
    seen = {}
    for o in ops:
        if o["key"] is None:
            cnt[o["e"]] = cnt.get(o["e"], 0) + int(o["sig"])
            o["val"] = cnt[o["e"]]
        else:
            o["val"] = o["inc"]
    for o in ops:
        if o["e"] == "X":
            continue
        for k in o["waits"]:
            s = ops[k]["at"][0]
            Q[o["e"]].wait_ge(T.sem[s], ops[k]["val"])
            seen[s] = max(seen.get(s, 0), ops[k]["val"])
        ins = o["fn"]()
        if o["key"] is None:
            if o["sig"]:
                ins.then_inc(T.sem[o["at"][0]], 1)
        elif o["key"] != "remote":
            ins.then_inc(T.sem[o["key"]], 16)
    g.wait_ge(T.sem.sent, sent[0])
    for o in ops:
        if o["key"] is not None and o["key"] != "remote" and seen.get(o["key"], 0) < o["val"]:
            g.wait_ge(T.sem[o["key"]], o["val"])
